import numpy as np
import ml_dtypes


def mxq(x, axis, fmt="e4m3"):
    dtype, down = {"e4m3": (ml_dtypes.float8_e4m3fn, 7), "e5m2": (ml_dtypes.float8_e5m2, 14)}[fmt]
    v = np.moveaxis(np.asarray(x, np.float32).astype(ml_dtypes.bfloat16).astype(np.float64), axis, -1)
    blocks = v.reshape(v.shape[:-1] + (-1, 32))
    amax = np.abs(blocks).max(-1, keepdims=True)
    byte = np.maximum(np.where(amax > 0, np.frexp(amax)[1] - 1 + 127, 0) - down, 1)
    scale = np.exp2(byte - 127.0)
    codes = (blocks / scale).astype(np.float32).astype(dtype).astype(np.float64)
    return np.moveaxis((codes * scale).reshape(v.shape), -1, axis)


WIDE = False


def mx_kscale(k):
    if not WIDE:
        return np.ones(k)
    levels = np.array([10, -10, 5, -5, 0])
    if k % 512:
        return np.exp2(np.random.permutation(np.resize(levels, k // 32))).repeat(32)
    a = np.empty((k // 512, 16))
    for p in range(k // 512):
        a[p, :8] = np.random.permutation(np.resize(levels, 8))
        for g in range(8):
            far = levels[np.abs(levels - a[p, g]) >= 10]
            a[p, g + 8] = far[np.random.randint(len(far))]
    return np.exp2(a.ravel()).repeat(32)


def f64(x):
    return np.asarray(x).astype(np.float64)


def striped(idx):
    return np.tile(idx.reshape(-1, 16).T, (8, 1)).astype(np.uint16)


def unstriped(offs):
    return offs[:16].T.reshape(-1).astype(np.int64)


E2M1 = np.array([0.0, 0.5, 1.0, 1.5, 2.0, 3.0, 4.0, 6.0, -0.0, -0.5, -1.0, -1.5, -2.0, -3.0, -4.0, -6.0])


def pack_weight(w, fmt):
    k, n = w.shape
    w = f64(np.asarray(w, np.float32).astype(ml_dtypes.bfloat16)).reshape(k // 32, 32, n)
    amax = np.abs(w).max(1)
    if fmt == "e4m3":
        byte = np.frexp(amax)[1] - 1 + 127 - 7
    else:
        mant, ex = np.frexp(amax / 6.0)
        byte = np.where(mant > 0.5, ex, ex - 1) + 127
    byte = np.clip(np.where(amax > 0, byte, 1), 1, 254)
    scaled = (w * np.exp2(127.0 - byte)[:, None, :]).reshape(k, n).astype(np.float32)
    by_word = np.ascontiguousarray(scaled.reshape(k // 512, 128, 4, n).transpose(0, 1, 3, 2))
    if fmt == "e4m3":
        words = by_word.astype(ml_dtypes.float8_e4m3fn).view(np.uint8)
    else:
        c = by_word.astype(ml_dtypes.float4_e2m1fn).view(np.uint8) & 0xF
        words = (c[..., 0::2] | (c[..., 1::2] << 4)).reshape(k // 512, 128, 2 * n)
    return np.ascontiguousarray(words), np.ascontiguousarray(byte.astype(np.uint8).reshape(k // 512, 16, n))


def unpack_weight(words, scales, fmt):
    g, _, n = scales.shape
    words = np.ascontiguousarray(words).reshape(g, 128, n, -1)
    if fmt == "e4m3":
        vals = words.view(ml_dtypes.float8_e4m3fn).astype(np.float64)
    else:
        nib = np.empty((g, 128, n, 4), np.uint8)
        nib[..., 0::2] = words & 0xF
        nib[..., 1::2] = words >> 4
        vals = E2M1[nib]
    vals = vals * np.repeat(np.exp2(scales.astype(np.float64) - 127.0), 8, axis=1)[..., None]
    return vals.transpose(0, 1, 3, 2).reshape(g * 512, n)


def gelu(v):
    return 0.5 * v * (1.0 + np.tanh(np.sqrt(2.0 / np.pi) * (v + 0.044715 * v**3)))


def striped8(idx):
    return np.concatenate([v.reshape(-1, 16).T for v in idx]).astype(np.uint16)


def unstriped8(offs):
    return np.stack([offs[16 * g:16 * g + 16].T.reshape(-1) for g in range(8)]).astype(np.int64)


def heads(h, wgt, idx8):
    r = np.arange(h.shape[0])
    return wgt[r // 4 % 128] * h[r[:, None], idx8[r % 512 // 64]]


K, T, S, P, H, N = 512, 4096, 2048, 1024, 1024, 512

def setup_inputs():
    n = np.random.standard_normal
    s = mx_kscale(K)[:, None]
    u = mx_kscale(H)[:, None]
    tab_words, tab_scales = pack_weight(n((K, T)) * s, "e4m3")
    wa_words, wa_scales = pack_weight(n((H, N)) / np.sqrt(H) / u, "e2m1")
    return {
        "tab_words": tab_words, "tab_scales": tab_scales,
        "offs": striped(np.random.permutation(T)[:S]),
        "w1": (n((K, H)) / np.sqrt(K) / s * u.T).astype(np.float32),
        "offs2": striped8(np.stack([np.random.permutation(S)[:P] for _ in range(8)])),
        "wgt": np.repeat(np.random.uniform(0.5, 2.0, (8, P)), 16, axis=0).astype(np.float32),
        "own": (n((H, P)) * u).astype(np.float32),
        "wa_words": wa_words, "wa_scales": wa_scales,
        "ba": (0.5 * n(N)).astype(np.float32),
        "wb": (n((H, N)) / np.sqrt(H) / u).astype(np.float32),
        "bb": (0.5 * n(N)).astype(np.float32),
    }

def reference(tab_words, tab_scales, offs, w1, offs2, wgt, own, wa_words, wa_scales, ba, wb, bb):
    v = unpack_weight(tab_words, tab_scales, "e4m3")[:, unstriped(offs)]
    h = mxq(f64(w1), 0, "e4m3").T @ v
    x = heads(h, f64(wgt), unstriped8(offs2))
    z = np.abs(x - f64(own))
    zq = mxq(z, 0, "e4m3")
    a = unpack_weight(wa_words, wa_scales, "e2m1").T @ zq
    b = mxq(f64(wb), 0, "e4m3").T @ zq
    return (a + f64(ba)[:, None]) * (b + f64(bb)[:, None])

@@ -1,0 +1,317 @@
+from contextlib import ExitStack
+
+import concourse.mybir as mybir
+from concourse.masks import make_identity
+
+K, T, S, PB, H, N = 512, 4096, 2048, 1024, 1024, 512
+FLOPS = 2 * K * H * S + 2 * 2 * H * N * PB
+
+F32 = mybir.dt.float32
+BF16 = mybir.dt.bfloat16
+I32 = mybir.dt.int32
+U32 = mybir.dt.uint32
+U16 = mybir.dt.uint16
+U8 = mybir.dt.uint8
+FP8X4 = mybir.dt.float8_e4m3fn_x4
+FP4X4 = mybir.dt.float4_e2m1fn_x4
+ALU = mybir.AluOpType
+ACT = mybir.ActivationFunctionType
+
+P = 128
+PACK = 4
+BANK = 512
+PASSES = H // (P * PACK)
+N_TILES = N // P
+S_CHUNKS = S // BANK
+CLEAR_SPLIT = 2816
+MAIN = 6
+M_CHUNKS = [(0, 512), (512, 256), (768, 256)]
+
+
+def tile_list_clone_audit_kernel(
+    tc, tab_words, tab_scales, offs, w1, offs2, wgt, own, wa_words, wa_scales, ba, wb, bb, out
+):
+    nc = tc.nc
+    with ExitStack() as ctx:
+        keep = ctx.enter_context(tc.tile_pool(name="keep", bufs=1))
+        ring = ctx.enter_context(tc.tile_pool(name="ring", bufs=2))
+        psum = ctx.enter_context(tc.psum_pool(name="psum", bufs=4))
+
+        idx = keep.tile([P, S // 16], U16, name="idx")
+        nc.sync.dma_start(idx[:], offs)
+
+        def load_weight(src, name):
+            raw = ring.tile([P, PACK, BANK], F32, name=name, tag="raw", bufs=2)
+            nc.sync.dma_start(raw[:], src.rearrange("(p j) c -> p j c", j=PACK))
+            return raw
+
+        w1_raw = [load_weight(w1[:, 0:BANK], "w1_raw0")]
+
+        tab_plane = keep.tile([P, T], U8, name="tab_plane")
+        nc.vector.memset(tab_plane[:, 0:CLEAR_SPLIT].bitcast(I32), 0)
+        nc.gpsimd.memset(tab_plane[:, CLEAR_SPLIT:T].bitcast(I32), 0)
+        for q in range(4):
+            nc.sync.dma_start(
+                tab_plane[32 * q : 32 * q + 4, :].bitcast(I32),
+                tab_scales[0, 4 * q : 4 * q + 4, :].bitcast(I32),
+            )
+        ident = keep.tile([P, P], F32, name="ident")
+        make_identity(nc, ident[:])
+
+        tab_w = ring.tile([P, T], I32, name="tab_w", tag="big", bufs=1)
+        nc.sync.dma_start(tab_w[:], tab_words[0].rearrange("p t i -> p (t i)").bitcast(I32))
+        w1_raw.append(load_weight(w1[:, BANK : 2 * BANK], "w1_raw1"))
+        idx2 = keep.tile([P, PB // 16], U16, name="idx2")
+        nc.sync.dma_start(idx2[:], offs2)
+        wgt_sb = keep.tile([P, PB], F32, name="wgt_sb")
+        nc.sync.dma_start(wgt_sb[:], wgt)
+
+        own_v = own.rearrange("(b p t) m -> b p t m", p=P, t=PACK)
+        gap = [keep.tile([P, PACK, PB], F32, name="own0")]
+        for u in range(2):
+            nc.sync.dma_start(gap[0][:, 2 * u : 2 * u + 2, :], own_v[0, :, 2 * u : 2 * u + 2, :])
+        wb_raw = [load_weight(wb[b * BANK : (b + 1) * BANK, :], "wb_raw%d" % b) for b in range(PASSES)]
+
+        wa_w = keep.tile([P, PASSES, 2 * N], U8, name="wa_w", align_bytes=64)
+        nc.sync.dma_start(wa_w[:].bitcast(I32), wa_words.rearrange("a p c -> p a c").bitcast(I32))
+        wa_plane = keep.tile([P, PASSES, N], U8, name="wa_plane", align_bytes=64)
+        nc.gpsimd.memset(wa_plane[:].bitcast(I32), 0)
+        for q in range(4):
+            nc.sync.dma_start(
+                wa_plane[32 * q : 32 * q + 4, :, :].bitcast(I32),
+                wa_scales[:, 4 * q : 4 * q + 4, :].rearrange("a r c -> r a c").bitcast(I32),
+            )
+        ba_sb = keep.tile([P, N_TILES], F32, name="ba_sb")
+        bb_sb = keep.tile([P, N_TILES], F32, name="bb_sb")
+        with nc.allow_non_contiguous_dma(reason="one bias value a partition"):
+            nc.sync.dma_start(ba_sb[:], ba.rearrange("(j p) -> p j", p=P))
+            nc.sync.dma_start(bb_sb[:], bb.rearrange("(j p) -> p j", p=P))
+
+        v_plane = keep.tile([P, S], U8, name="v_plane", align_bytes=64)
+        nc.vector.tensor_copy(v_plane[:], tab_plane[:].indirect(idx[:]))
+
+        def quantise(grouped, width, name):
+            codes = keep.tile([P, width], U32, name=name + "_codes", align_bytes=64)
+            plane = keep.tile([P, width], U8, name=name + "_plane", align_bytes=64)
+            nc.vector.quantize_mx(out=codes[:].bitcast(FP8X4), scales=plane[:], in_=grouped)
+            return codes, plane
+
+        def round_w1(b):
+            grouped = ring.tile([P, PACK * BANK], BF16, name="w1_bf%d" % b, tag="w_bf", align_bytes=64)
+            copy = nc.scalar.copy if b == 0 else nc.vector.tensor_copy
+            copy(
+                grouped[:].rearrange("p (t m j) -> p m j t", t=PACK, j=PACK),
+                w1_raw[b][:].rearrange("p j (m t) -> p m j t", t=PACK),
+            )
+            return grouped
+
+        def round_wb(b):
+            grouped = ring.tile([P, PACK * BANK], BF16, name="wb_bf%d" % b, tag="w_bf", align_bytes=64)
+            nc.vector.tensor_copy(
+                grouped[:].rearrange("p (c i j) -> p c j i", i=4, j=PACK),
+                wb_raw[b][:].rearrange("p j (c i) -> p c j i", i=4),
+            )
+            return grouped
+
+        w1_q = [quantise(round_w1(0)[:], BANK, "w1q0")]
+
+        v_words = [keep.tile([P, BANK], U32, name="v_words%d" % c, align_bytes=64) for c in range(S_CHUNKS)]
+        h = [ring.tile([P, S], F32, name="h%d" % s, tag="h", bufs=8) for s in range(2)]
+
+        def h_chunk(s, c):
+            b, t = divmod(s, PACK)
+            acc = psum.tile([P, BANK], F32, name="h_acc", tag="main", bufs=MAIN)
+            nc.tensor.matmul_mx(
+                out=acc[:],
+                lhsT=w1_q[b][0][:, t * P : (t + 1) * P].bitcast(FP8X4),
+                lhsT_scale=w1_q[b][1][:, t * P : (t + 1) * P],
+                rhs=v_words[c][:].bitcast(FP8X4),
+                rhs_scale=v_plane[:, c * BANK : (c + 1) * BANK],
+                start=True,
+                stop=True,
+            )
+            nc.scalar.activation(h[s][:, c * BANK : (c + 1) * BANK], acc[:], ACT.Copy, scale=-1.0)
+
+        for c in range(S_CHUNKS):
+            nc.vector.tensor_copy(
+                v_words[c][:], tab_w[:].bitcast(U32).indirect(idx[:, c * BANK // 16 : (c + 1) * BANK // 16])
+            )
+            for s in range(2):
+                h_chunk(s, c)
+
+        gap.append(ring.tile([P, PACK, PB], F32, name="own1", tag="big", bufs=1))
+        for u in range(2):
+            nc.sync.dma_start(gap[1][:, 2 * u : 2 * u + 2, :], own_v[1, :, 2 * u : 2 * u + 2, :])
+
+        def h_slices(slices):
+            for s in slices:
+                h.append(ring.tile([P, S], F32, name="h%d" % s, tag="h", bufs=8))
+            for c in range(S_CHUNKS):
+                for s in slices:
+                    h_chunk(s, c)
+
+        def pick(s, m0, width, x):
+            nc.vector.tensor_tensor(
+                x, h[s][:].indirect(idx2[:, m0 // 16 : (m0 + width) // 16]), wgt_sb[:, m0 : m0 + width], ALU.mult
+            )
+            return x
+
+        def round_gap(b, m0, width):
+            z = ring.tile([P, PACK * width], BF16, name="z_bf", tag="z_bf", bufs=3, align_bytes=64)
+            nc.scalar.activation(
+                z[:].rearrange("p (c i t) -> p c t i", i=4, t=PACK),
+                gap[b][:, :, m0 : m0 + width].rearrange("p t (c i) -> p c t i", i=4),
+                ACT.Abs,
+            )
+            return z
+
+        def turn_pair(b, u, m0, width, xs, x0, zt):
+            for j0 in range(0, width // P, 2):
+                bank = psum.tile([P, 2, 2, P], F32, name="gap_t", tag="main", bufs=MAIN)
+                places = [(jj, e) for jj in range(2) for e in range(2)]
+                for n, (jj, e) in enumerate(places):
+                    c0 = m0 + (j0 + jj) * P
+                    nc.tensor.matmul(
+                        bank[:, jj, e, :], gap[b][:, 2 * u + e, c0 : c0 + P], ident[:],
+                        start=(n == 0), stop=False, is_transpose=True,
+                    )
+                for n, (jj, e) in enumerate(places):
+                    c0 = m0 - x0 + (j0 + jj) * P
+                    nc.tensor.matmul(
+                        bank[:, jj, e, :], xs[e][:, c0 : c0 + P], ident[:],
+                        start=False, stop=(n == 3), is_transpose=True,
+                    )
+                nc.scalar.activation(
+                    zt[:, j0 : j0 + 2, u, :].rearrange("m j (p e) -> m j p e", e=2),
+                    bank[:].rearrange("m j e p -> m j p e"),
+                    ACT.Abs,
+                )
+
+        def turn_back(width, zt, copy, tag):
+            z = ring.tile([P, PACK * width], BF16, name="z_bf", tag="z_bf", bufs=3, align_bytes=64)
+            for j0 in range(0, width // P, 2):
+                bank = psum.tile([P, 2, 2, P], F32, name="z_t", tag=tag, bufs=MAIN if tag == "main" else 8 - MAIN)
+                for jj in range(2):
+                    for u in range(2):
+                        nc.tensor.transpose(bank[:, jj, u, :], zt[:, j0 + jj, u, :].bitcast(F32), ident[:])
+                copy(
+                    z[:, PACK * j0 * P : PACK * (j0 + 2) * P].bitcast(F32).rearrange("p (j m u) -> p j m u", j=2, u=2),
+                    bank[:].rearrange("p j u m -> p j m u"),
+                )
+            return z
+
+        def new_zt(b, m0, width):
+            return keep.tile([P, width // P, 2, 2 * P], BF16, name="zt%d_%d" % (b, m0))
+
+        z_bf = {}
+        z_q = {}
+
+        out_v = out.rearrange("(j p) m -> p j m", p=P)
+
+        def second_stage(m0, width):
+            step = BANK if width == BANK else P
+            for j in range(N_TILES):
+                if width == BANK:
+                    acc_b = psum.tile([P, width], F32, name="acc_b", tag="main", bufs=MAIN)[:]
+                    acc_a = psum.tile([P, width], F32, name="acc_a", tag="main", bufs=MAIN)[:]
+                else:
+                    both = psum.tile([P, 2, width], F32, name="acc_ab", tag="main", bufs=MAIN)
+                    acc_a, acc_b = both[:, 0, :], both[:, 1, :]
+                for c0 in range(0, width, step):
+                    for b in range(PASSES):
+                        codes, plane = z_q[(b, m0)]
+                        nc.tensor.matmul_mx(
+                            out=acc_b[:, c0 : c0 + step],
+                            lhsT=wb_q[b][0][:, j * P : (j + 1) * P].bitcast(FP8X4),
+                            lhsT_scale=wb_q[b][1][:, j * P : (j + 1) * P],
+                            rhs=codes[:, c0 : c0 + step].bitcast(FP8X4),
+                            rhs_scale=plane[:, c0 : c0 + step],
+                            start=(b == 0),
+                            stop=(b == PASSES - 1),
+                        )
+                for c0 in range(0, width, step):
+                    for b in range(PASSES):
+                        codes, plane = z_q[(b, m0)]
+                        nc.tensor.matmul_mx(
+                            out=acc_a[:, c0 : c0 + step],
+                            lhsT=wa_w[:, b, 2 * j * P : 2 * (j + 1) * P].bitcast(FP4X4),
+                            lhsT_scale=wa_plane[:, b, j * P : (j + 1) * P],
+                            rhs=codes[:, c0 : c0 + step].bitcast(FP8X4),
+                            rhs_scale=plane[:, c0 : c0 + step],
+                            start=(b == 0),
+                            stop=(b == PASSES - 1),
+                        )
+                b_sb = ring.tile([P, width], F32, name="b_sb", tag="b_sb", bufs=3)
+                nc.scalar.activation(b_sb[:], acc_b, ACT.Identity, bias=bb_sb[:, j : j + 1])
+                if width == BANK or j % 2 == 0:
+                    staged = ring.tile([P, BANK // width, width], F32, name="staged", tag="staged", bufs=4)
+                jj = j % (BANK // width)
+                nc.vector.scalar_tensor_tensor(
+                    staged[:, jj, :], acc_a, ba_sb[:, j : j + 1], b_sb[:], ALU.add, ALU.mult
+                )
+                if jj == BANK // width - 1:
+                    nc.sync.dma_start(out_v[:, j - jj : j + 1, m0 : m0 + width], staged[:])
+
+        (m0, w0), (m1, w1_), (m2, w2) = M_CHUNKS
+
+        def gap_codes(b, m, width):
+            z_q[(b, m)] = quantise(z_bf[(b, m)][:], width, "zq%d_%d" % (b, m))
+
+        w1_q.append(quantise(round_w1(1)[:], BANK, "w1q1"))
+        h_slices([2])
+        h_slices([3])
+        last = range(PACK, 2 * PACK)
+        h_slices(last)
+        x_first = [pick(s, 0, PB, ring.tile([P, PB], F32, name="x%d" % s, tag="x", bufs=4)[:]) for s in range(PACK)]
+        wb_bf = [round_wb(b) for b in range(PASSES)]
+        wb_q = [quantise(wb_bf[b][:], BANK, "wbq%d" % b) for b in range(PASSES)]
+        x_last = [keep.tile([P, PACK, w0], F32, name="x_last0")]
+        for s in last:
+            pick(s, m0, w0, x_last[0][:, s - PACK, :])
+        zt = {(b, m): new_zt(b, m, w) for b in range(PASSES) for m, w in M_CHUNKS[: 3 - b]}
+
+        def turn(b, u, i):
+            m, w = M_CHUNKS[i]
+            if b == 0:
+                turn_pair(b, u, m, w, x_first[2 * u : 2 * u + 2], 0, zt[(b, m)])
+            else:
+                turn_pair(b, u, m, w, [x_last[i][:, 2 * u + e, :] for e in range(2)], m, zt[(b, m)])
+
+        def back(b, i, on_vector):
+            m, w = M_CHUNKS[i]
+            if on_vector:
+                z_bf[(b, m)] = turn_back(w, zt[(b, m)], nc.vector.tensor_copy, "z_t")
+            else:
+                z_bf[(b, m)] = turn_back(w, zt[(b, m)], nc.scalar.copy, "main")
+
+        for i in range(3):
+            turn(0, 0, i)
+        for i in (1, 2):
+            m, w = M_CHUNKS[i]
+            x_last.append(ring.tile([P, PACK, w], F32, name="x_last%d" % i, tag="x", bufs=4))
+            for s in last:
+                pick(s, m, w, x_last[i][:, s - PACK, :])
+        turn(0, 1, 0)
+        turn(1, 0, 0)
+        back(0, 0, False)
+        turn(1, 1, 0)
+        turn(0, 1, 1)
+        back(1, 0, False)
+        d = gap[1][:, :, m2 : m2 + w2]
+        nc.vector.tensor_tensor(d, x_last[2][:], d, ALU.add)
+        gap_codes(0, m0, w0)
+        gap_codes(1, m0, w0)
+        turn(1, 0, 1)
+        turn(1, 1, 1)
+        turn(0, 1, 2)
+        back(0, 1, True)
+        back(1, 1, True)
+        second_stage(m0, w0)
+        gap_codes(0, m1, w1_)
+        gap_codes(1, m1, w1_)
+        z_bf[(1, m2)] = round_gap(1, m2, w2)
+        back(0, 2, True)
+        second_stage(m1, w1_)
+        gap_codes(0, m2, w2)
+        gap_codes(1, m2, w2)
+        second_stage(m2, w2)

@@ -24,8 +24,9 @@ PASSES = H // (P * PACK)
 N_TILES = N // P
 S_CHUNKS = S // BANK
 CLEAR_SPLIT = 2816
-MAIN = 6
-M_CHUNKS = [(0, 512), (512, 256), (768, 256)]
+MAIN = 4
+BLOCK = 256
+M_CHUNKS = [(0, 256), (256, 256), (512, 256), (768, 256)]
 
 
 def tile_list_clone_audit_kernel(
@@ -45,7 +46,8 @@ def tile_list_clone_audit_kernel(
             nc.sync.dma_start(raw[:], src.rearrange("(p j) c -> p j c", j=PACK))
             return raw
 
-        w1_raw = [load_weight(w1[:, 0:BANK], "w1_raw0")]
+        idx2 = keep.tile([P, PB // 16], U16, name="idx2")
+        nc.sync.dma_start(idx2[:], offs2)
 
         tab_plane = keep.tile([P, T], U8, name="tab_plane")
         nc.vector.memset(tab_plane[:, 0:CLEAR_SPLIT].bitcast(I32), 0)
@@ -60,9 +62,8 @@ def tile_list_clone_audit_kernel(
 
         tab_w = ring.tile([P, T], I32, name="tab_w", tag="big", bufs=1)
         nc.sync.dma_start(tab_w[:], tab_words[0].rearrange("p t i -> p (t i)").bitcast(I32))
+        w1_raw = [load_weight(w1[:, 0:BANK], "w1_raw0")]
         w1_raw.append(load_weight(w1[:, BANK : 2 * BANK], "w1_raw1"))
-        idx2 = keep.tile([P, PB // 16], U16, name="idx2")
-        nc.sync.dma_start(idx2[:], offs2)
         wgt_sb = keep.tile([P, PB], F32, name="wgt_sb")
         nc.sync.dma_start(wgt_sb[:], wgt)
 
@@ -96,48 +97,57 @@ def tile_list_clone_audit_kernel(
             nc.vector.quantize_mx(out=codes[:].bitcast(FP8X4), scales=plane[:], in_=grouped)
             return codes, plane
 
-        def round_w1(b):
-            grouped = ring.tile([P, PACK * BANK], BF16, name="w1_bf%d" % b, tag="w_bf", align_bytes=64)
-            copy = nc.scalar.copy if b == 0 else nc.vector.tensor_copy
+        def round_w1(b, t0, nt, copy, tag, bufs):
+            grouped = ring.tile([P, nt * BANK], BF16, name="w1_bf%d_%d" % (b, t0), tag=tag, bufs=bufs, align_bytes=64)
             copy(
-                grouped[:].rearrange("p (t m j) -> p m j t", t=PACK, j=PACK),
-                w1_raw[b][:].rearrange("p j (m t) -> p m j t", t=PACK),
+                grouped[:].rearrange("p (t m j) -> p m j t", t=nt, j=PACK),
+                w1_raw[b][:].rearrange("p j (m t) -> p m j t", t=PACK)[:, :, :, t0 : t0 + nt],
             )
             return grouped
 
-        def round_wb(b):
-            grouped = ring.tile([P, PACK * BANK], BF16, name="wb_bf%d" % b, tag="w_bf", align_bytes=64)
-            nc.vector.tensor_copy(
+        def round_wb(b, copy):
+            grouped = ring.tile([P, PACK * BANK], BF16, name="wb_bf%d" % b, tag="w_bf", bufs=2, align_bytes=64)
+            copy(
                 grouped[:].rearrange("p (c i j) -> p c j i", i=4, j=PACK),
                 wb_raw[b][:].rearrange("p j (c i) -> p c j i", i=4),
             )
             return grouped
 
-        w1_q = [quantise(round_w1(0)[:], BANK, "w1q0")]
+        w1_q = {}
 
-        v_words = [keep.tile([P, BANK], U32, name="v_words%d" % c, align_bytes=64) for c in range(S_CHUNKS)]
-        h = [ring.tile([P, S], F32, name="h%d" % s, tag="h", bufs=8) for s in range(2)]
+        def w1_codes(b, t0, nt, grouped):
+            codes, plane = quantise(grouped[:], nt * P, "w1q%d_%d" % (b, t0))
+            for t in range(nt):
+                w1_q[PACK * b + t0 + t] = (codes[:, t * P : (t + 1) * P], plane[:, t * P : (t + 1) * P])
+
+        v_words = [keep.tile([P, BANK], U32, name="v_words%d" % c, align_bytes=64) for c in range(S_CHUNKS - 1)]
+
+        def gather_words(c):
+            nc.vector.tensor_copy(
+                v_words[c][:], tab_w[:].bitcast(U32).indirect(idx[:, c * BANK // 16 : (c + 1) * BANK // 16])
+            )
+
+        for c in range(S_CHUNKS - 1):
+            gather_words(c)
+        w1_codes(0, 0, 2, round_w1(0, 0, 2, nc.scalar.copy, "first", 1))
+        w1_bf = round_w1(0, 2, 2, nc.scalar.copy, "w_bf", 2)
+        v_words.append(ring.tile([P, BANK], U32, name="v_words3", tag="first", bufs=1, align_bytes=64))
+        gather_words(S_CHUNKS - 1)
+        w1_codes(0, 2, 2, w1_bf)
+        h = []
 
         def h_chunk(s, c):
-            b, t = divmod(s, PACK)
             acc = psum.tile([P, BANK], F32, name="h_acc", tag="main", bufs=MAIN)
             nc.tensor.matmul_mx(
                 out=acc[:],
-                lhsT=w1_q[b][0][:, t * P : (t + 1) * P].bitcast(FP8X4),
-                lhsT_scale=w1_q[b][1][:, t * P : (t + 1) * P],
+                lhsT=w1_q[s][0].bitcast(FP8X4),
+                lhsT_scale=w1_q[s][1],
                 rhs=v_words[c][:].bitcast(FP8X4),
                 rhs_scale=v_plane[:, c * BANK : (c + 1) * BANK],
                 start=True,
                 stop=True,
             )
             nc.scalar.activation(h[s][:, c * BANK : (c + 1) * BANK], acc[:], ACT.Copy, scale=-1.0)
-
-        for c in range(S_CHUNKS):
-            nc.vector.tensor_copy(
-                v_words[c][:], tab_w[:].bitcast(U32).indirect(idx[:, c * BANK // 16 : (c + 1) * BANK // 16])
-            )
-            for s in range(2):
-                h_chunk(s, c)
 
         gap.append(ring.tile([P, PACK, PB], F32, name="own1", tag="big", bufs=1))
         for u in range(2):
@@ -157,7 +167,7 @@ def tile_list_clone_audit_kernel(
             return x
 
         def round_gap(b, m0, width):
-            z = ring.tile([P, PACK * width], BF16, name="z_bf", tag="z_bf", bufs=3, align_bytes=64)
+            z = ring.tile([P, PACK * width], BF16, name="z_bf", tag="z_bf", bufs=6, align_bytes=64)
             nc.scalar.activation(
                 z[:].rearrange("p (c i t) -> p c t i", i=4, t=PACK),
                 gap[b][:, :, m0 : m0 + width].rearrange("p t (c i) -> p c t i", i=4),
@@ -165,8 +175,8 @@ def tile_list_clone_audit_kernel(
             )
             return z
 
-        def turn_pair(b, u, m0, width, xs, x0, zt):
-            for j0 in range(0, width // P, 2):
+        def turn_pair(b, u, m0, starts, xs, x0, zt):
+            for j0 in starts:
                 bank = psum.tile([P, 2, 2, P], F32, name="gap_t", tag="main", bufs=MAIN)
                 places = [(jj, e) for jj in range(2) for e in range(2)]
                 for n, (jj, e) in enumerate(places):
@@ -188,7 +198,7 @@ def tile_list_clone_audit_kernel(
                 )
 
         def turn_back(width, zt, copy, tag):
-            z = ring.tile([P, PACK * width], BF16, name="z_bf", tag="z_bf", bufs=3, align_bytes=64)
+            z = ring.tile([P, PACK * width], BF16, name="z_bf", tag="z_bf", bufs=6, align_bytes=64)
             for j0 in range(0, width // P, 2):
                 bank = psum.tile([P, 2, 2, P], F32, name="z_t", tag=tag, bufs=MAIN if tag == "main" else 8 - MAIN)
                 for jj in range(2):
@@ -208,74 +218,72 @@ def tile_list_clone_audit_kernel(
 
         out_v = out.rearrange("(j p) m -> p j m", p=P)
 
-        def second_stage(m0, width):
-            step = BANK if width == BANK else P
-            for j in range(N_TILES):
-                if width == BANK:
-                    acc_b = psum.tile([P, width], F32, name="acc_b", tag="main", bufs=MAIN)[:]
-                    acc_a = psum.tile([P, width], F32, name="acc_a", tag="main", bufs=MAIN)[:]
-                else:
-                    both = psum.tile([P, 2, width], F32, name="acc_ab", tag="main", bufs=MAIN)
-                    acc_a, acc_b = both[:, 0, :], both[:, 1, :]
-                for c0 in range(0, width, step):
-                    for b in range(PASSES):
-                        codes, plane = z_q[(b, m0)]
-                        nc.tensor.matmul_mx(
-                            out=acc_b[:, c0 : c0 + step],
-                            lhsT=wb_q[b][0][:, j * P : (j + 1) * P].bitcast(FP8X4),
-                            lhsT_scale=wb_q[b][1][:, j * P : (j + 1) * P],
-                            rhs=codes[:, c0 : c0 + step].bitcast(FP8X4),
-                            rhs_scale=plane[:, c0 : c0 + step],
-                            start=(b == 0),
-                            stop=(b == PASSES - 1),
-                        )
-                for c0 in range(0, width, step):
-                    for b in range(PASSES):
-                        codes, plane = z_q[(b, m0)]
-                        nc.tensor.matmul_mx(
-                            out=acc_a[:, c0 : c0 + step],
-                            lhsT=wa_w[:, b, 2 * j * P : 2 * (j + 1) * P].bitcast(FP4X4),
-                            lhsT_scale=wa_plane[:, b, j * P : (j + 1) * P],
-                            rhs=codes[:, c0 : c0 + step].bitcast(FP8X4),
-                            rhs_scale=plane[:, c0 : c0 + step],
-                            start=(b == 0),
-                            stop=(b == PASSES - 1),
-                        )
-                b_sb = ring.tile([P, width], F32, name="b_sb", tag="b_sb", bufs=3)
-                nc.scalar.activation(b_sb[:], acc_b, ACT.Identity, bias=bb_sb[:, j : j + 1])
-                if width == BANK or j % 2 == 0:
-                    staged = ring.tile([P, BANK // width, width], F32, name="staged", tag="staged", bufs=4)
-                jj = j % (BANK // width)
-                nc.vector.scalar_tensor_tensor(
-                    staged[:, jj, :], acc_a, ba_sb[:, j : j + 1], b_sb[:], ALU.add, ALU.mult
-                )
-                if jj == BANK // width - 1:
-                    nc.sync.dma_start(out_v[:, j - jj : j + 1, m0 : m0 + width], staged[:])
+        accs = {}
 
-        (m0, w0), (m1, w1_), (m2, w2) = M_CHUNKS
+        def products(b, i):
+            m0, width = TAIL[i]
+            first = m0 if b == 1 else m0 // BLOCK * BLOCK
+            codes, plane = z_q[(b, first)]
+            per_bank = BLOCK // width
+            for j in range(N_TILES):
+                if b == 0 and j % per_bank == 0:
+                    bank = psum.tile([P, per_bank, 2, width], F32, name="acc_ab", tag=ACC_TAG[i], bufs=MAIN)
+                    for jj in range(per_bank):
+                        accs[(i, j + jj)] = bank[:, jj, :, :]
+                both = accs[(i, j)]
+                z0 = m0 - first
+                nc.tensor.matmul_mx(
+                    out=both[:, 1, :],
+                    lhsT=wb_q[b][0][:, j * P : (j + 1) * P].bitcast(FP8X4),
+                    lhsT_scale=wb_q[b][1][:, j * P : (j + 1) * P],
+                    rhs=codes[:, z0 : z0 + width].bitcast(FP8X4),
+                    rhs_scale=plane[:, z0 : z0 + width],
+                    start=(b == 0 and j % per_bank == 0),
+                    stop=False,
+                )
+                for c0 in range(0, width, P):
+                    nc.tensor.matmul_mx(
+                        out=both[:, 0, c0 : c0 + P],
+                        lhsT=wa_w[:, b, 2 * j * P : 2 * (j + 1) * P].bitcast(FP4X4),
+                        lhsT_scale=wa_plane[:, b, j * P : (j + 1) * P],
+                        rhs=codes[:, z0 + c0 : z0 + c0 + P].bitcast(FP8X4),
+                        rhs_scale=plane[:, z0 + c0 : z0 + c0 + P],
+                        start=False,
+                        stop=(b == PASSES - 1 and c0 + P == width and j % per_bank == per_bank - 1),
+                    )
+
+        def finish(i):
+            m0, width = TAIL[i]
+            group = BANK // width
+            for j in range(N_TILES):
+                both = accs[(i, j)]
+                b_sb = ring.tile([P, width], F32, name="b_sb", tag="b_sb", bufs=4)
+                nc.scalar.activation(b_sb[:], both[:, 1, :], ACT.Identity, bias=bb_sb[:, j : j + 1])
+                if j % group == 0:
+                    staged = ring.tile([P, group, width], F32, name="staged", tag="staged", bufs=4)
+                nc.vector.scalar_tensor_tensor(
+                    staged[:, j % group, :], both[:, 0, :], ba_sb[:, j : j + 1], b_sb[:], ALU.add, ALU.mult
+                )
+                if j % group == group - 1:
+                    nc.sync.dma_start(out_v[:, j + 1 - group : j + 1, m0 : m0 + width], staged[:])
 
         def gap_codes(b, m, width):
             z_q[(b, m)] = quantise(z_bf[(b, m)][:], width, "zq%d_%d" % (b, m))
 
-        w1_q.append(quantise(round_w1(1)[:], BANK, "w1q1"))
-        h_slices([2])
-        h_slices([3])
+        V, A = nc.vector.tensor_copy, nc.scalar.copy
         last = range(PACK, 2 * PACK)
-        h_slices(last)
-        x_first = [pick(s, 0, PB, ring.tile([P, PB], F32, name="x%d" % s, tag="x", bufs=4)[:]) for s in range(PACK)]
-        wb_bf = [round_wb(b) for b in range(PASSES)]
-        wb_q = [quantise(wb_bf[b][:], BANK, "wbq%d" % b) for b in range(PASSES)]
-        x_last = [keep.tile([P, PACK, w0], F32, name="x_last0")]
-        for s in last:
-            pick(s, m0, w0, x_last[0][:, s - PACK, :])
-        zt = {(b, m): new_zt(b, m, w) for b in range(PASSES) for m, w in M_CHUNKS[: 3 - b]}
+        zt = {}
+        xs = {}
 
-        def turn(b, u, i):
+        def new_h(s):
+            h.append(ring.tile([P, S], F32, name="h%d" % s, tag="h", bufs=8))
+
+        def turn(b, u, i, starts=None):
             m, w = M_CHUNKS[i]
-            if b == 0:
-                turn_pair(b, u, m, w, x_first[2 * u : 2 * u + 2], 0, zt[(b, m)])
-            else:
-                turn_pair(b, u, m, w, [x_last[i][:, 2 * u + e, :] for e in range(2)], m, zt[(b, m)])
+            if (b, m) not in zt:
+                zt[(b, m)] = new_zt(b, m, w)
+            pair = [xs[(4 * b + 2 * u + e, i)] for e in range(2)]
+            turn_pair(b, u, m, starts or range(0, w // P, 2), pair, m, zt[(b, m)])
 
         def back(b, i, on_vector):
             m, w = M_CHUNKS[i]
@@ -284,34 +292,95 @@ def tile_list_clone_audit_kernel(
             else:
                 z_bf[(b, m)] = turn_back(w, zt[(b, m)], nc.scalar.copy, "main")
 
-        for i in range(3):
-            turn(0, 0, i)
-        for i in (1, 2):
-            m, w = M_CHUNKS[i]
-            x_last.append(ring.tile([P, PACK, w], F32, name="x_last%d" % i, tag="x", bufs=4))
-            for s in last:
-                pick(s, m, w, x_last[i][:, s - PACK, :])
-        turn(0, 1, 0)
-        turn(1, 0, 0)
+        def pick_full(s, bufs):
+            x = pick(s, 0, PB, ring.tile([P, PB], F32, name="x%d" % s, tag="x", bufs=bufs)[:])
+            for i, (m, w) in enumerate(M_CHUNKS):
+                xs[(s, i)] = x[:, m : m + w]
+            return x
+
+        def add_own(s, m, w, x):
+            d = gap[s // 4][:, s % 4, m : m + w]
+            nc.vector.tensor_tensor(d, x, d, ALU.add)
+
+        def codes(b, i):
+            gap_codes(b, *M_CHUNKS[i])
+
+        def rg(b, i):
+            z_bf[(b, M_CHUNKS[i][0])] = round_gap(b, *M_CHUNKS[i])
+
+        ACC_TAG = ["acc","main","acc","main","acc"]
+        TAIL = [(0, 256), (256, 256), (512, 256), (768, 256)]
+        h_slices([0])
+        w1_codes(1, 0, 4, round_w1(1, 0, 4, V, "w_bf", 2))
+        h_slices([1])
+        h_slices([2])
+        h_slices([3])
+        h_slices([4])
+
+        def pick_pair(s, m, w, tag, bufs):
+            x = ring.tile([P, 2, w], F32, name="x%d_%d" % (s, m), tag=tag, bufs=bufs)
+            for e in range(2):
+                pick(s + e, m, w, x[:, e, :])
+                for i, (mm, ww) in enumerate(M_CHUNKS):
+                    if m <= mm < m + w:
+                        xs[(s + e, i)] = x[:, e, mm - m : mm - m + ww]
+            return x
+
+        def add_pair(s, m, w, x):
+            d = gap[1][:, s - 4 : s - 2, m : m + w]
+            nc.vector.tensor_tensor(d, x, d, ALU.add)
+
+        pick_pair(0, 0, PB, "xa", 3)
+        pick_pair(2, 0, PB, "xa", 3)
+        banks = [(u, i) for u in range(2) for i in range(4)]
+        n = 0
+        k = 0
+        for s in (5, 6, 7):
+            new_h(s)
+            for c in range(4):
+                h_chunk(s, c)
+                if k in [1,2,3,5,6,7,9,10]:
+                    turn(0, *banks[n])
+                    n = n + 1
+                k = k + 1
+        wb_bf = [round_wb(b, V) for b in range(PASSES)]
+        x45 = pick_pair(4, 0, PB, "xa", 3)
+        wb_q = [quantise(wb_bf[b][:], BANK, "wbq%d" % b) for b in range(PASSES)]
+        by_pe = []
+        for m, w in [(0, 512), (512, 512)]:
+            add_pair(4, m, w, x45[:, :, m : m + w])
+        early = banks[n:]
+        for u, i in early:
+            if i == 0:
+                turn(0, u, i)
         back(0, 0, False)
-        turn(1, 1, 0)
-        turn(0, 1, 1)
-        back(1, 0, False)
-        d = gap[1][:, :, m2 : m2 + w2]
-        nc.vector.tensor_tensor(d, x_last[2][:], d, ALU.add)
-        gap_codes(0, m0, w0)
-        gap_codes(1, m0, w0)
-        turn(1, 0, 1)
-        turn(1, 1, 1)
-        turn(0, 1, 2)
-        back(0, 1, True)
-        back(1, 1, True)
-        second_stage(m0, w0)
-        gap_codes(0, m1, w1_)
-        gap_codes(1, m1, w1_)
-        z_bf[(1, m2)] = round_gap(1, m2, w2)
-        back(0, 2, True)
-        second_stage(m1, w1_)
-        gap_codes(0, m2, w2)
-        gap_codes(1, m2, w2)
-        second_stage(m2, w2)
+        codes(0, 0)
+        products(0, 0)
+        for u, i in early:
+            if i > 0:
+                turn(0, u, i)
+        for i in by_pe:
+            turn(1, 0, i)
+
+        def tail(i):
+            m, w = TAIL[i]
+            x = pick_pair(6, m, w, "xb", 1)
+            if i in by_pe:
+                turn(1, 1, i)
+                back(1, i, False)
+            else:
+                add_pair(6, m, w, x[:])
+                z_bf[(1, m)] = round_gap(1, m, w)
+
+        for i in range(len(TAIL)):
+            tail(i)
+            if i < 3:
+                back(0, i + 1, False)
+            if 1 <= i <= 3:
+                codes(0, i)
+            gap_codes(1, *TAIL[i])
+            if i >= 1:
+                finish(i - 1)
+                products(0, i)
+            products(1, i)
+        finish(len(TAIL) - 1)

@@ -42,7 +42,7 @@ def tile_list_clone_audit_kernel(
         nc.sync.dma_start(idx[:], offs)
 
         def load_weight(src, name):
-            raw = ring.tile([P, PACK, BANK], F32, name=name, tag="raw", bufs=2)
+            raw = ring.tile([P, PACK, BANK], F32, name=name, tag="raw", bufs=4)
             nc.sync.dma_start(raw[:], src.rearrange("(p j) c -> p j c", j=PACK))
             return raw
 
@@ -69,24 +69,10 @@ def tile_list_clone_audit_kernel(
 
         own_v = own.rearrange("(b p t) m -> b p t m", p=P, t=PACK)
         gap = [keep.tile([P, PACK, PB], F32, name="own0")]
+        wb_raw = []
         for u in range(2):
             nc.sync.dma_start(gap[0][:, 2 * u : 2 * u + 2, :], own_v[0, :, 2 * u : 2 * u + 2, :])
-        wb_raw = [load_weight(wb[b * BANK : (b + 1) * BANK, :], "wb_raw%d" % b) for b in range(PASSES)]
-
-        wa_w = keep.tile([P, PASSES, 2 * N], U8, name="wa_w", align_bytes=64)
-        nc.sync.dma_start(wa_w[:].bitcast(I32), wa_words.rearrange("a p c -> p a c").bitcast(I32))
-        wa_plane = keep.tile([P, PASSES, N], U8, name="wa_plane", align_bytes=64)
-        nc.gpsimd.memset(wa_plane[:].bitcast(I32), 0)
-        for q in range(4):
-            nc.sync.dma_start(
-                wa_plane[32 * q : 32 * q + 4, :, :].bitcast(I32),
-                wa_scales[:, 4 * q : 4 * q + 4, :].rearrange("a r c -> r a c").bitcast(I32),
-            )
-        ba_sb = keep.tile([P, N_TILES], F32, name="ba_sb")
-        bb_sb = keep.tile([P, N_TILES], F32, name="bb_sb")
-        with nc.allow_non_contiguous_dma(reason="one bias value a partition"):
-            nc.sync.dma_start(ba_sb[:], ba.rearrange("(j p) -> p j", p=P))
-            nc.sync.dma_start(bb_sb[:], bb.rearrange("(j p) -> p j", p=P))
+            wb_raw.append(load_weight(wb[u * BANK : (u + 1) * BANK, :], "wb_raw%d" % u))
 
         v_plane = keep.tile([P, S], U8, name="v_plane", align_bytes=64)
         nc.vector.tensor_copy(v_plane[:], tab_plane[:].indirect(idx[:]))
@@ -97,6 +83,12 @@ def tile_list_clone_audit_kernel(
             nc.vector.quantize_mx(out=codes[:].bitcast(FP8X4), scales=plane[:], in_=grouped)
             return codes, plane
 
+        def negate_on_scalar(dst, src):
+            nc.scalar.activation(dst, src, ACT.Copy, scale=-1.0)
+
+        def negate_on_vector(dst, src):
+            nc.vector.tensor_scalar(dst, src, -1.0, None, ALU.mult)
+
         def round_w1(b, t0, nt, copy, tag, bufs):
             grouped = ring.tile([P, nt * BANK], BF16, name="w1_bf%d_%d" % (b, t0), tag=tag, bufs=bufs, align_bytes=64)
             copy(
@@ -106,7 +98,7 @@ def tile_list_clone_audit_kernel(
             return grouped
 
         def round_wb(b, copy):
-            grouped = ring.tile([P, PACK * BANK], BF16, name="wb_bf%d" % b, tag="w_bf", bufs=2, align_bytes=64)
+            grouped = ring.tile([P, PACK * BANK], BF16, name="wb_bf%d" % b, tag="w_bf", bufs=1, align_bytes=64)
             copy(
                 grouped[:].rearrange("p (c i j) -> p c j i", i=4, j=PACK),
                 wb_raw[b][:].rearrange("p j (c i) -> p c j i", i=4),
@@ -129,8 +121,8 @@ def tile_list_clone_audit_kernel(
 
         for c in range(S_CHUNKS - 1):
             gather_words(c)
-        w1_codes(0, 0, 2, round_w1(0, 0, 2, nc.scalar.copy, "first", 1))
-        w1_bf = round_w1(0, 2, 2, nc.scalar.copy, "w_bf", 2)
+        w1_codes(0, 0, 2, round_w1(0, 0, 2, negate_on_scalar, "first", 1))
+        w1_bf = round_w1(0, 2, 2, negate_on_scalar, "w_bf", 1)
         v_words.append(ring.tile([P, BANK], U32, name="v_words3", tag="first", bufs=1, align_bytes=64))
         gather_words(S_CHUNKS - 1)
         w1_codes(0, 2, 2, w1_bf)
@@ -147,15 +139,30 @@ def tile_list_clone_audit_kernel(
                 start=True,
                 stop=True,
             )
-            nc.scalar.activation(h[s][:, c * BANK : (c + 1) * BANK], acc[:], ACT.Copy, scale=-1.0)
+            nc.scalar.copy(h[s][:, c * BANK : (c + 1) * BANK], acc[:])
 
         gap.append(ring.tile([P, PACK, PB], F32, name="own1", tag="big", bufs=1))
         for u in range(2):
             nc.sync.dma_start(gap[1][:, 2 * u : 2 * u + 2, :], own_v[1, :, 2 * u : 2 * u + 2, :])
 
+        wa_w = keep.tile([P, PASSES, 2 * N], U8, name="wa_w", align_bytes=64)
+        nc.sync.dma_start(wa_w[:].bitcast(I32), wa_words.rearrange("a p c -> p a c").bitcast(I32))
+        wa_plane = keep.tile([P, PASSES, N], U8, name="wa_plane", align_bytes=64)
+        nc.gpsimd.memset(wa_plane[:].bitcast(I32), 0)
+        for q in range(4):
+            nc.sync.dma_start(
+                wa_plane[32 * q : 32 * q + 4, :, :].bitcast(I32),
+                wa_scales[:, 4 * q : 4 * q + 4, :].rearrange("a r c -> r a c").bitcast(I32),
+            )
+        ba_sb = keep.tile([P, N_TILES], F32, name="ba_sb")
+        bb_sb = keep.tile([P, N_TILES], F32, name="bb_sb")
+        with nc.allow_non_contiguous_dma(reason="one bias value a partition"):
+            nc.sync.dma_start(ba_sb[:], ba.rearrange("(j p) -> p j", p=P))
+            nc.sync.dma_start(bb_sb[:], bb.rearrange("(j p) -> p j", p=P))
+
         def h_slices(slices):
             for s in slices:
-                h.append(ring.tile([P, S], F32, name="h%d" % s, tag="h", bufs=8))
+                h.append(ring.tile([P, S], F32, name="h%d" % s, tag="h", bufs=7))
             for c in range(S_CHUNKS):
                 for s in slices:
                     h_chunk(s, c)
@@ -220,12 +227,12 @@ def tile_list_clone_audit_kernel(
 
         accs = {}
 
-        def products(b, i):
+        def products(b, i, tiles=range(N_TILES)):
             m0, width = TAIL[i]
             first = m0 if b == 1 else m0 // BLOCK * BLOCK
             codes, plane = z_q[(b, first)]
             per_bank = BLOCK // width
-            for j in range(N_TILES):
+            for j in tiles:
                 if b == 0 and j % per_bank == 0:
                     bank = psum.tile([P, per_bank, 2, width], F32, name="acc_ab", tag=ACC_TAG[i], bufs=MAIN)
                     for jj in range(per_bank):
@@ -276,7 +283,7 @@ def tile_list_clone_audit_kernel(
         xs = {}
 
         def new_h(s):
-            h.append(ring.tile([P, S], F32, name="h%d" % s, tag="h", bufs=8))
+            h.append(ring.tile([P, S], F32, name="h%d" % s, tag="h", bufs=7))
 
         def turn(b, u, i, starts=None):
             m, w = M_CHUNKS[i]
@@ -308,10 +315,10 @@ def tile_list_clone_audit_kernel(
         def rg(b, i):
             z_bf[(b, M_CHUNKS[i][0])] = round_gap(b, *M_CHUNKS[i])
 
-        ACC_TAG = ["acc","main","acc","main","acc"]
-        TAIL = [(0, 256), (256, 256), (512, 256), (768, 256)]
+        ACC_TAG = ["acc", "main", "acc", "main"]
+        TAIL = M_CHUNKS
         h_slices([0])
-        w1_codes(1, 0, 4, round_w1(1, 0, 4, V, "w_bf", 2))
+        w1_codes(1, 0, 4, round_w1(1, 0, 4, negate_on_vector, "w_bf", 1))
         h_slices([1])
         h_slices([2])
         h_slices([3])
@@ -331,56 +338,62 @@ def tile_list_clone_audit_kernel(
             nc.vector.tensor_tensor(d, x, d, ALU.add)
 
         pick_pair(0, 0, PB, "xa", 3)
+        wb_q = [quantise(round_wb(0, V)[:], BANK, "wbq0")]
         pick_pair(2, 0, PB, "xa", 3)
-        banks = [(u, i) for u in range(2) for i in range(4)]
+        wb_q.append(quantise(round_wb(1, V)[:], BANK, "wbq1"))
+
+        def first_words():
+            back(0, 0, False)
+            codes(0, 0)
+            products(0, 0)
+
+        woven = [lambda u=u, i=i: turn(0, u, i) for u in range(2) for i in range(4)] + [first_words]
         n = 0
-        k = 0
         for s in (5, 6, 7):
             new_h(s)
             for c in range(4):
                 h_chunk(s, c)
-                if k in [1,2,3,5,6,7,9,10]:
-                    turn(0, *banks[n])
+                if c > 0 and n < 8:
+                    woven[n]()
                     n = n + 1
-                k = k + 1
-        wb_bf = [round_wb(b, V) for b in range(PASSES)]
         x45 = pick_pair(4, 0, PB, "xa", 3)
-        wb_q = [quantise(wb_bf[b][:], BANK, "wbq%d" % b) for b in range(PASSES)]
-        by_pe = []
         for m, w in [(0, 512), (512, 512)]:
             add_pair(4, m, w, x45[:, :, m : m + w])
-        early = banks[n:]
-        for u, i in early:
-            if i == 0:
-                turn(0, u, i)
-        back(0, 0, False)
-        codes(0, 0)
-        products(0, 0)
-        for u, i in early:
-            if i > 0:
-                turn(0, u, i)
-        for i in by_pe:
-            turn(1, 0, i)
+        for job in woven[n:]:
+            job()
 
         def tail(i):
             m, w = TAIL[i]
             x = pick_pair(6, m, w, "xb", 1)
-            if i in by_pe:
-                turn(1, 1, i)
-                back(1, i, False)
-            else:
-                add_pair(6, m, w, x[:])
-                z_bf[(1, m)] = round_gap(1, m, w)
+            add_pair(6, m, w, x[:])
+            z_bf[(1, m)] = round_gap(1, m, w)
 
-        for i in range(len(TAIL)):
-            tail(i)
-            if i < 3:
-                back(0, i + 1, False)
-            if 1 <= i <= 3:
-                codes(0, i)
-            gap_codes(1, *TAIL[i])
-            if i >= 1:
-                finish(i - 1)
-                products(0, i)
-            products(1, i)
-        finish(len(TAIL) - 1)
+        def both_products(i):
+            for j in range(N_TILES):
+                products(0, i, [j])
+                products(1, i, [j])
+
+        for i in range(1, 4):
+            back(0, i, False)
+        tail(0)
+        codes(0, 1)
+        codes(1, 0)
+        products(1, 0)
+        products(0, 1)
+        tail(1)
+        finish(0)
+        codes(0, 2)
+        codes(1, 1)
+        products(1, 1)
+        products(0, 2)
+        tail(2)
+        tail(3)
+        finish(1)
+        codes(0, 3)
+        codes(1, 2)
+        products(1, 2)
+        products(0, 3)
+        codes(1, 3)
+        products(1, 3)
+        finish(2)
+        finish(3)

@@ -24,9 +24,11 @@ PASSES = H // (P * PACK)
 N_TILES = N // P
 S_CHUNKS = S // BANK
 CLEAR_SPLIT = 2816
-MAIN = 4
-BLOCK = 256
-M_CHUNKS = [(0, 256), (256, 256), (512, 256), (768, 256)]
+CHUNK = 256
+HALF = 512
+CHUNKS = [(m, CHUNK) for m in range(0, PB, CHUNK)]
+HBUFS = 7
+PARTS = CHUNKS
 
 
 def tile_list_clone_audit_kernel(
@@ -36,18 +38,20 @@ def tile_list_clone_audit_kernel(
     with ExitStack() as ctx:
         keep = ctx.enter_context(tc.tile_pool(name="keep", bufs=1))
         ring = ctx.enter_context(tc.tile_pool(name="ring", bufs=2))
-        psum = ctx.enter_context(tc.psum_pool(name="psum", bufs=4))
+        psum = ctx.enter_context(tc.psum_pool(name="psum", bufs=1))
+
+        def bank(n, shape, name):
+            return psum.tile([P] + shape, F32, name=name, tag="bank%d" % n, bufs=1)
 
         idx = keep.tile([P, S // 16], U16, name="idx")
         nc.sync.dma_start(idx[:], offs)
+        idx2 = keep.tile([P, PB // 16], U16, name="idx2")
+        nc.sync.dma_start(idx2[:], offs2)
 
         def load_weight(src, name):
             raw = ring.tile([P, PACK, BANK], F32, name=name, tag="raw", bufs=4)
             nc.sync.dma_start(raw[:], src.rearrange("(p j) c -> p j c", j=PACK))
             return raw
-
-        idx2 = keep.tile([P, PB // 16], U16, name="idx2")
-        nc.sync.dma_start(idx2[:], offs2)
 
         tab_plane = keep.tile([P, T], U8, name="tab_plane")
         nc.vector.memset(tab_plane[:, 0:CLEAR_SPLIT].bitcast(I32), 0)
@@ -62,8 +66,7 @@ def tile_list_clone_audit_kernel(
 
         tab_w = ring.tile([P, T], I32, name="tab_w", tag="big", bufs=1)
         nc.sync.dma_start(tab_w[:], tab_words[0].rearrange("p t i -> p (t i)").bitcast(I32))
-        w1_raw = [load_weight(w1[:, 0:BANK], "w1_raw0")]
-        w1_raw.append(load_weight(w1[:, BANK : 2 * BANK], "w1_raw1"))
+        w1_raw = [load_weight(w1[:, b * BANK : (b + 1) * BANK], "w1_raw%d" % b) for b in range(PASSES)]
         wgt_sb = keep.tile([P, PB], F32, name="wgt_sb")
         nc.sync.dma_start(wgt_sb[:], wgt)
 
@@ -74,12 +77,9 @@ def tile_list_clone_audit_kernel(
             nc.sync.dma_start(gap[0][:, 2 * u : 2 * u + 2, :], own_v[0, :, 2 * u : 2 * u + 2, :])
             wb_raw.append(load_weight(wb[u * BANK : (u + 1) * BANK, :], "wb_raw%d" % u))
 
-        v_plane = keep.tile([P, S], U8, name="v_plane", align_bytes=64)
-        nc.vector.tensor_copy(v_plane[:], tab_plane[:].indirect(idx[:]))
-
         def quantise(grouped, width, name):
-            codes = keep.tile([P, width], U32, name=name + "_codes", align_bytes=64)
-            plane = keep.tile([P, width], U8, name=name + "_plane", align_bytes=64)
+            codes = ring.tile([P, width], U32, name=name + "_codes", tag=name + "_codes", bufs=1, align_bytes=64)
+            plane = ring.tile([P, width], U8, name=name + "_plane", tag=name + "_plane", bufs=1, align_bytes=64)
             nc.vector.quantize_mx(out=codes[:].bitcast(FP8X4), scales=plane[:], in_=grouped)
             return codes, plane
 
@@ -89,47 +89,45 @@ def tile_list_clone_audit_kernel(
         def negate_on_vector(dst, src):
             nc.vector.tensor_scalar(dst, src, -1.0, None, ALU.mult)
 
-        def round_w1(b, t0, nt, copy, tag, bufs):
-            grouped = ring.tile([P, nt * BANK], BF16, name="w1_bf%d_%d" % (b, t0), tag=tag, bufs=bufs, align_bytes=64)
-            copy(
+        def round_w1(s0, nt, negate, tag):
+            b, t0 = divmod(s0, PACK)
+            grouped = ring.tile([P, nt * BANK], BF16, name="w1_bf%d" % s0, tag=tag, bufs=1, align_bytes=64)
+            negate(
                 grouped[:].rearrange("p (t m j) -> p m j t", t=nt, j=PACK),
                 w1_raw[b][:].rearrange("p j (m t) -> p m j t", t=PACK)[:, :, :, t0 : t0 + nt],
             )
             return grouped
 
-        def round_wb(b, copy):
-            grouped = ring.tile([P, PACK * BANK], BF16, name="wb_bf%d" % b, tag="w_bf", bufs=1, align_bytes=64)
+        w1_q = {}
+
+        def w1_codes(s0, nt, grouped):
+            codes, plane = quantise(grouped[:], nt * P, "w1q%d" % s0)
+            for t in range(nt):
+                w1_q[s0 + t] = (codes[:, t * P : (t + 1) * P], plane[:, t * P : (t + 1) * P])
+
+        def round_wb(b, copy, tag, bufs):
+            grouped = ring.tile([P, PACK * BANK], BF16, name="wb_bf%d" % b, tag=tag, bufs=bufs, align_bytes=64)
             copy(
                 grouped[:].rearrange("p (c i j) -> p c j i", i=4, j=PACK),
                 wb_raw[b][:].rearrange("p j (c i) -> p c j i", i=4),
             )
             return grouped
 
-        w1_q = {}
+        v_plane = keep.tile([P, S], U8, name="v_plane", align_bytes=64)
+        v_words = {}
 
-        def w1_codes(b, t0, nt, grouped):
-            codes, plane = quantise(grouped[:], nt * P, "w1q%d_%d" % (b, t0))
-            for t in range(nt):
-                w1_q[PACK * b + t0 + t] = (codes[:, t * P : (t + 1) * P], plane[:, t * P : (t + 1) * P])
-
-        v_words = [keep.tile([P, BANK], U32, name="v_words%d" % c, align_bytes=64) for c in range(S_CHUNKS - 1)]
-
-        def gather_words(c):
+        def gather_words(c, tag):
+            v_words[c] = ring.tile([P, BANK], U32, name="v_words%d" % c, tag=tag, bufs=1, align_bytes=64)
             nc.vector.tensor_copy(
                 v_words[c][:], tab_w[:].bitcast(U32).indirect(idx[:, c * BANK // 16 : (c + 1) * BANK // 16])
             )
 
-        for c in range(S_CHUNKS - 1):
-            gather_words(c)
-        w1_codes(0, 0, 2, round_w1(0, 0, 2, negate_on_scalar, "first", 1))
-        w1_bf = round_w1(0, 2, 2, negate_on_scalar, "w_bf", 1)
-        v_words.append(ring.tile([P, BANK], U32, name="v_words3", tag="first", bufs=1, align_bytes=64))
-        gather_words(S_CHUNKS - 1)
-        w1_codes(0, 2, 2, w1_bf)
-        h = []
+        h = {}
 
-        def h_chunk(s, c):
-            acc = psum.tile([P, BANK], F32, name="h_acc", tag="main", bufs=MAIN)
+        def h_chunk(s, c, n):
+            if s not in h:
+                h[s] = ring.tile([P, S], F32, name="h%d" % s, tag="h", bufs=HBUFS)
+            acc = bank(n, [BANK], "h_acc")
             nc.tensor.matmul_mx(
                 out=acc[:],
                 lhsT=w1_q[s][0].bitcast(FP8X4),
@@ -141,114 +139,121 @@ def tile_list_clone_audit_kernel(
             )
             nc.scalar.copy(h[s][:, c * BANK : (c + 1) * BANK], acc[:])
 
-        gap.append(ring.tile([P, PACK, PB], F32, name="own1", tag="big", bufs=1))
-        for u in range(2):
-            nc.sync.dma_start(gap[1][:, 2 * u : 2 * u + 2, :], own_v[1, :, 2 * u : 2 * u + 2, :])
+        xs = {}
 
-        wa_w = keep.tile([P, PASSES, 2 * N], U8, name="wa_w", align_bytes=64)
-        nc.sync.dma_start(wa_w[:].bitcast(I32), wa_words.rearrange("a p c -> p a c").bitcast(I32))
-        wa_plane = keep.tile([P, PASSES, N], U8, name="wa_plane", align_bytes=64)
-        nc.gpsimd.memset(wa_plane[:].bitcast(I32), 0)
-        for q in range(4):
-            nc.sync.dma_start(
-                wa_plane[32 * q : 32 * q + 4, :, :].bitcast(I32),
-                wa_scales[:, 4 * q : 4 * q + 4, :].rearrange("a r c -> r a c").bitcast(I32),
-            )
-        ba_sb = keep.tile([P, N_TILES], F32, name="ba_sb")
-        bb_sb = keep.tile([P, N_TILES], F32, name="bb_sb")
-        with nc.allow_non_contiguous_dma(reason="one bias value a partition"):
-            nc.sync.dma_start(ba_sb[:], ba.rearrange("(j p) -> p j", p=P))
-            nc.sync.dma_start(bb_sb[:], bb.rearrange("(j p) -> p j", p=P))
+        def pick_pair(s, m0, width, tag, bufs):
+            x = ring.tile([P, 2, width], F32, name="x%d_%d" % (s, m0), tag=tag, bufs=bufs, align_bytes=64)
+            for e in range(2):
+                nc.vector.tensor_tensor(
+                    x[:, e, :],
+                    h[s + e][:].indirect(idx2[:, m0 // 16 : (m0 + width) // 16]),
+                    wgt_sb[:, m0 : m0 + width],
+                    ALU.mult,
+                )
+            for i, (m, w) in enumerate(PARTS if s == 6 else CHUNKS):
+                if m0 <= m < m0 + width:
+                    xs[(s, i)] = x[:, :, m - m0 : m - m0 + w]
 
-        def h_slices(slices):
-            for s in slices:
-                h.append(ring.tile([P, S], F32, name="h%d" % s, tag="h", bufs=7))
-            for c in range(S_CHUNKS):
-                for s in slices:
-                    h_chunk(s, c)
-
-        def pick(s, m0, width, x):
+        def pick(s, m0, width, dst):
             nc.vector.tensor_tensor(
-                x, h[s][:].indirect(idx2[:, m0 // 16 : (m0 + width) // 16]), wgt_sb[:, m0 : m0 + width], ALU.mult
+                dst, h[s][:].indirect(idx2[:, m0 // 16 : (m0 + width) // 16]), wgt_sb[:, m0 : m0 + width], ALU.mult
             )
-            return x
 
-        def round_gap(b, m0, width):
-            z = ring.tile([P, PACK * width], BF16, name="z_bf", tag="z_bf", bufs=6, align_bytes=64)
-            nc.scalar.activation(
-                z[:].rearrange("p (c i t) -> p c t i", i=4, t=PACK),
-                gap[b][:, :, m0 : m0 + width].rearrange("p t (c i) -> p c t i", i=4),
-                ACT.Abs,
-            )
-            return z
+        def add_own(x, t0, nt, m0, width):
+            d = gap[1][:, t0 : t0 + nt, m0 : m0 + width]
+            nc.vector.tensor_tensor(d, x, d, ALU.add)
 
-        def turn_pair(b, u, m0, starts, xs, x0, zt):
-            for j0 in starts:
-                bank = psum.tile([P, 2, 2, P], F32, name="gap_t", tag="main", bufs=MAIN)
-                places = [(jj, e) for jj in range(2) for e in range(2)]
-                for n, (jj, e) in enumerate(places):
-                    c0 = m0 + (j0 + jj) * P
-                    nc.tensor.matmul(
-                        bank[:, jj, e, :], gap[b][:, 2 * u + e, c0 : c0 + P], ident[:],
-                        start=(n == 0), stop=False, is_transpose=True,
-                    )
-                for n, (jj, e) in enumerate(places):
-                    c0 = m0 - x0 + (j0 + jj) * P
-                    nc.tensor.matmul(
-                        bank[:, jj, e, :], xs[e][:, c0 : c0 + P], ident[:],
-                        start=False, stop=(n == 3), is_transpose=True,
-                    )
-                nc.scalar.activation(
-                    zt[:, j0 : j0 + 2, u, :].rearrange("m j (p e) -> m j p e", e=2),
-                    bank[:].rearrange("m j e p -> m j p e"),
-                    ACT.Abs,
-                )
-
-        def turn_back(width, zt, copy, tag):
-            z = ring.tile([P, PACK * width], BF16, name="z_bf", tag="z_bf", bufs=6, align_bytes=64)
-            for j0 in range(0, width // P, 2):
-                bank = psum.tile([P, 2, 2, P], F32, name="z_t", tag=tag, bufs=MAIN if tag == "main" else 8 - MAIN)
-                for jj in range(2):
-                    for u in range(2):
-                        nc.tensor.transpose(bank[:, jj, u, :], zt[:, j0 + jj, u, :].bitcast(F32), ident[:])
-                copy(
-                    z[:, PACK * j0 * P : PACK * (j0 + 2) * P].bitcast(F32).rearrange("p (j m u) -> p j m u", j=2, u=2),
-                    bank[:].rearrange("p j u m -> p j m u"),
-                )
-            return z
-
-        def new_zt(b, m0, width):
-            return keep.tile([P, width // P, 2, 2 * P], BF16, name="zt%d_%d" % (b, m0))
-
+        zt = {}
         z_bf = {}
         z_q = {}
 
-        out_v = out.rearrange("(j p) m -> p j m", p=P)
+        sums = {}
+
+        def add_turned(s, i, n):
+            b, u = s // PACK, s % PACK // 2
+            acc = bank(n, [2, 2, P], "gap_t%d_%d" % (s, i))
+            sums[(s, i)] = acc
+            places = [(j, e) for j in range(2) for e in range(2)]
+            for k, (j, e) in enumerate(places):
+                c0 = i * CHUNK + j * P
+                nc.tensor.matmul(
+                    acc[:, j, e, :], gap[b][:, 2 * u + e, c0 : c0 + P], ident[:],
+                    start=(k == 0), stop=False, is_transpose=True,
+                )
+            for k, (j, e) in enumerate(places):
+                nc.tensor.matmul(
+                    acc[:, j, e, :], xs[(s, i)][:, e, j * P : (j + 1) * P], ident[:],
+                    start=False, stop=(k == 3), is_transpose=True,
+                )
+
+        def round_turned(s, i, tag=None):
+            b, u = s // PACK, s % PACK // 2
+            if (b, i) not in zt:
+                zt[(b, i)] = ring.tile([P, 2, 2, 2 * P], BF16, name="zt%d_%d" % (b, i), tag=tag or "zt%d_%d" % (b, i), bufs=1, align_bytes=64)
+            nc.scalar.activation(
+                zt[(b, i)][:, :, u, :].rearrange("m j (p e) -> m j p e", e=2),
+                sums[(s, i)][:].rearrange("m j e p -> m j p e"),
+                ACT.Abs,
+            )
+
+        def new_z(b, i, tag):
+            z_bf[(b, i)] = ring.tile([P, PACK * (PARTS if b else CHUNKS)[i][1]], BF16, name="z_bf%d_%d" % (b, i), tag=tag, bufs=1, align_bytes=64)
+            return z_bf[(b, i)]
+
+        backs = {}
+
+        def turn_back(b, i, n):
+            acc = bank(n, [2, 2, P], "z_t%d_%d" % (b, i))
+            backs[(b, i)] = acc
+            for j in range(2):
+                for u in range(2):
+                    nc.tensor.transpose(acc[:, j, u, :], zt[(b, i)][:, j, u, :].bitcast(F32), ident[:])
+
+        def copy_back(b, i):
+            nc.scalar.copy(
+                new_z(b, i, "z%d_%d" % (b, i))[:].bitcast(F32).rearrange("p (j m u) -> p j m u", j=2, u=2),
+                backs[(b, i)][:].rearrange("p j u m -> p j m u"),
+            )
+
+        def add_pair(s, i, tag):
+            t0 = s % PACK
+            m, w = (PARTS if s == 6 else CHUNKS)[i]
+            d = gap[1][:, t0 : t0 + 2, m : m + w]
+            nc.vector.tensor_tensor(d, xs[(s, i)], d, ALU.add)
+
+        def round_gap(b, i, tag):
+            nc.scalar.activation(
+                new_z(b, i, tag)[:].rearrange("p (c i t) -> p c t i", i=4, t=PACK),
+                gap[1][:, :, PARTS[i][0] : PARTS[i][0] + PARTS[i][1]].rearrange("p t (c i) -> p c t i", i=4),
+                ACT.Abs,
+            )
+
+        def gap_codes(b, i):
+            z_q[(b, i)] = quantise(z_bf[(b, i)][:], (PARTS if b else CHUNKS)[i][1], "zq%d_%d" % (b, i))
 
         accs = {}
 
-        def products(b, i, tiles=range(N_TILES)):
-            m0, width = TAIL[i]
-            first = m0 if b == 1 else m0 // BLOCK * BLOCK
-            codes, plane = z_q[(b, first)]
-            per_bank = BLOCK // width
+        def products(b, i, banks, tiles=range(N_TILES)):
+            m, w = PARTS[i]
+            codes, plane = z_q[(b, i if b else m // CHUNK)]
+            z0 = 0 if b else m % CHUNK
+            per_bank = CHUNK // w
             for j in tiles:
                 if b == 0 and j % per_bank == 0:
-                    bank = psum.tile([P, per_bank, 2, width], F32, name="acc_ab", tag=ACC_TAG[i], bufs=MAIN)
+                    acc = bank(banks[j // per_bank], [per_bank, 2, w], "acc%d_%d" % (i, j))
                     for jj in range(per_bank):
-                        accs[(i, j + jj)] = bank[:, jj, :, :]
+                        accs[(i, j + jj)] = acc[:, jj, :, :]
                 both = accs[(i, j)]
-                z0 = m0 - first
                 nc.tensor.matmul_mx(
                     out=both[:, 1, :],
                     lhsT=wb_q[b][0][:, j * P : (j + 1) * P].bitcast(FP8X4),
                     lhsT_scale=wb_q[b][1][:, j * P : (j + 1) * P],
-                    rhs=codes[:, z0 : z0 + width].bitcast(FP8X4),
-                    rhs_scale=plane[:, z0 : z0 + width],
+                    rhs=codes[:, z0 : z0 + w].bitcast(FP8X4),
+                    rhs_scale=plane[:, z0 : z0 + w],
                     start=(b == 0 and j % per_bank == 0),
                     stop=False,
                 )
-                for c0 in range(0, width, P):
+                for c0 in range(0, w, P):
                     nc.tensor.matmul_mx(
                         out=both[:, 0, c0 : c0 + P],
                         lhsT=wa_w[:, b, 2 * j * P : 2 * (j + 1) * P].bitcast(FP4X4),
@@ -256,144 +261,165 @@ def tile_list_clone_audit_kernel(
                         rhs=codes[:, z0 + c0 : z0 + c0 + P].bitcast(FP8X4),
                         rhs_scale=plane[:, z0 + c0 : z0 + c0 + P],
                         start=False,
-                        stop=(b == PASSES - 1 and c0 + P == width and j % per_bank == per_bank - 1),
+                        stop=(b == PASSES - 1 and c0 + P == w and j % per_bank == per_bank - 1),
                     )
 
-        def finish(i):
-            m0, width = TAIL[i]
-            group = BANK // width
+        out_v = out.rearrange("(j p) m -> p j m", p=P)
+        staged = {}
+
+        b_sb = {}
+
+        def read_b(i, tiles=range(N_TILES)):
+            for j in tiles:
+                b_sb[(i, j)] = ring.tile([P, PARTS[i][1]], F32, name="b_sb%d_%d" % (i, j), tag="b_sb%d_%d" % (i % 2, j), bufs=1, align_bytes=64)
+                nc.scalar.activation(b_sb[(i, j)][:], accs[(i, j)][:, 1, :], ACT.Identity, bias=bb_sb[:, j : j + 1])
+
+        a_sb = {}
+
+        def read_a(i):
             for j in range(N_TILES):
-                both = accs[(i, j)]
-                b_sb = ring.tile([P, width], F32, name="b_sb", tag="b_sb", bufs=4)
-                nc.scalar.activation(b_sb[:], both[:, 1, :], ACT.Identity, bias=bb_sb[:, j : j + 1])
-                if j % group == 0:
-                    staged = ring.tile([P, group, width], F32, name="staged", tag="staged", bufs=4)
+                a_sb[(i, j)] = ring.tile([P, PARTS[i][1]], F32, name="a_sb%d_%d" % (i, j), tag="a_sb", bufs=4)
+                nc.scalar.copy(a_sb[(i, j)][:], accs[(i, j)][:, 0, :])
+                read_b(i, [j])
+
+        def finish(i, tiles=range(N_TILES)):
+            m, w = PARTS[i]
+            for j in tiles:
+                if j == 0:
+                    staged[i] = ring.tile([P, N_TILES, w], F32, name="staged%d" % i, tag="raw", bufs=4)
                 nc.vector.scalar_tensor_tensor(
-                    staged[:, j % group, :], both[:, 0, :], ba_sb[:, j : j + 1], b_sb[:], ALU.add, ALU.mult
+                    staged[i][:, j, :], a_sb[(i, j)][:] if (i, j) in a_sb else accs[(i, j)][:, 0, :], ba_sb[:, j : j + 1], b_sb[(i, j)][:], ALU.add, ALU.mult
                 )
-                if j % group == group - 1:
-                    nc.sync.dma_start(out_v[:, j + 1 - group : j + 1, m0 : m0 + width], staged[:])
+                if j % 2 == 1:
+                    nc.sync.dma_start(out_v[:, j - 1 : j + 1, m : m + w], staged[i][:, j - 1 : j + 1, :])
 
-        def gap_codes(b, m, width):
-            z_q[(b, m)] = quantise(z_bf[(b, m)][:], width, "zq%d_%d" % (b, m))
+        def late_loads():
+            gap.append(ring.tile([P, PACK, PB], F32, name="own1", tag="big", bufs=1))
+            for u in range(2):
+                nc.sync.dma_start(gap[1][:, 2 * u : 2 * u + 2, :], own_v[1, :, 2 * u : 2 * u + 2, :])
+            nc.sync.dma_start(wa_w[:].bitcast(I32), wa_words.rearrange("a p c -> p a c").bitcast(I32))
+            nc.gpsimd.memset(wa_plane[:].bitcast(I32), 0)
+            for q in range(4):
+                nc.sync.dma_start(
+                    wa_plane[32 * q : 32 * q + 4, :, :].bitcast(I32),
+                    wa_scales[:, 4 * q : 4 * q + 4, :].rearrange("a r c -> r a c").bitcast(I32),
+                )
+            with nc.allow_non_contiguous_dma(reason="one bias value a partition"):
+                nc.sync.dma_start(ba_sb[:], ba.rearrange("(j p) -> p j", p=P))
+                nc.sync.dma_start(bb_sb[:], bb.rearrange("(j p) -> p j", p=P))
 
+        wa_w = keep.tile([P, PASSES, 2 * N], U8, name="wa_w", align_bytes=64)
+        wa_plane = keep.tile([P, PASSES, N], U8, name="wa_plane", align_bytes=64)
+        ba_sb = keep.tile([P, N_TILES], F32, name="ba_sb")
+        bb_sb = keep.tile([P, N_TILES], F32, name="bb_sb")
         V, A = nc.vector.tensor_copy, nc.scalar.copy
-        last = range(PACK, 2 * PACK)
-        zt = {}
-        xs = {}
+        wb_q = []
 
-        def new_h(s):
-            h.append(ring.tile([P, S], F32, name="h%d" % s, tag="h", bufs=7))
+        nc.vector.tensor_copy(v_plane[:], tab_plane[:].indirect(idx[:]))
+        for c in range(3):
+            gather_words(c, "vw%d" % c)
+        bf0 = round_w1(0, 1, negate_on_scalar, "vw3")
+        bf1 = round_w1(1, 1, negate_on_scalar, "w1c")
+        bf23 = round_w1(2, 2, negate_on_scalar, "w1b")
+        w1_codes(0, 1, bf0)
+        gather_words(3, "vw3")
+        w1_codes(1, 1, bf1)
+        late_loads()
+        bf45 = round_w1(4, 2, negate_on_vector, "w1c")
+        w1_codes(2, 2, bf23)
+        bf67 = round_w1(6, 2, negate_on_vector, "w1b")
+        w1_codes(4, 2, bf45)
+        w1_codes(6, 2, bf67)
+        turn_no = [0]
+        lo, hi = [0, 1, 2, 3], [4, 5, 6, 7]
 
-        def turn(b, u, i, starts=None):
-            m, w = M_CHUNKS[i]
-            if (b, m) not in zt:
-                zt[(b, m)] = new_zt(b, m, w)
-            pair = [xs[(4 * b + 2 * u + e, i)] for e in range(2)]
-            turn_pair(b, u, m, starts or range(0, w // P, 2), pair, m, zt[(b, m)])
+        def nb(banks):
+            turn_no[0] = turn_no[0] + 1
+            return banks[turn_no[0] % len(banks)]
 
-        def back(b, i, on_vector):
-            m, w = M_CHUNKS[i]
-            if on_vector:
-                z_bf[(b, m)] = turn_back(w, zt[(b, m)], nc.vector.tensor_copy, "z_t")
-            else:
-                z_bf[(b, m)] = turn_back(w, zt[(b, m)], nc.scalar.copy, "main")
-
-        def pick_full(s, bufs):
-            x = pick(s, 0, PB, ring.tile([P, PB], F32, name="x%d" % s, tag="x", bufs=bufs)[:])
-            for i, (m, w) in enumerate(M_CHUNKS):
-                xs[(s, i)] = x[:, m : m + w]
-            return x
-
-        def add_own(s, m, w, x):
-            d = gap[s // 4][:, s % 4, m : m + w]
-            nc.vector.tensor_tensor(d, x, d, ALU.add)
-
-        def codes(b, i):
-            gap_codes(b, *M_CHUNKS[i])
-
-        def rg(b, i):
-            z_bf[(b, M_CHUNKS[i][0])] = round_gap(b, *M_CHUNKS[i])
-
-        ACC_TAG = ["acc", "main", "acc", "main"]
-        TAIL = M_CHUNKS
-        h_slices([0])
-        w1_codes(1, 0, 4, round_w1(1, 0, 4, negate_on_vector, "w_bf", 1))
-        h_slices([1])
-        h_slices([2])
-        h_slices([3])
-        h_slices([4])
-
-        def pick_pair(s, m, w, tag, bufs):
-            x = ring.tile([P, 2, w], F32, name="x%d_%d" % (s, m), tag=tag, bufs=bufs)
-            for e in range(2):
-                pick(s + e, m, w, x[:, e, :])
-                for i, (mm, ww) in enumerate(M_CHUNKS):
-                    if m <= mm < m + w:
-                        xs[(s + e, i)] = x[:, e, mm - m : mm - m + ww]
-            return x
-
-        def add_pair(s, m, w, x):
-            d = gap[1][:, s - 4 : s - 2, m : m + w]
-            nc.vector.tensor_tensor(d, x, d, ALU.add)
-
-        pick_pair(0, 0, PB, "xa", 3)
-        wb_q = [quantise(round_wb(0, V)[:], BANK, "wbq0")]
-        pick_pair(2, 0, PB, "xa", 3)
-        wb_q.append(quantise(round_wb(1, V)[:], BANK, "wbq1"))
-
-        def first_words():
-            back(0, 0, False)
-            codes(0, 0)
-            products(0, 0)
-
-        woven = [lambda u=u, i=i: turn(0, u, i) for u in range(2) for i in range(4)] + [first_words]
-        n = 0
-        for s in (5, 6, 7):
-            new_h(s)
+        def h_slice(s, banks):
             for c in range(4):
-                h_chunk(s, c)
-                if c > 0 and n < 8:
-                    woven[n]()
-                    n = n + 1
-        x45 = pick_pair(4, 0, PB, "xa", 3)
-        for m, w in [(0, 512), (512, 512)]:
-            add_pair(4, m, w, x45[:, :, m : m + w])
-        for job in woven[n:]:
-            job()
+                h_chunk(s, c, nb(banks))
 
-        def tail(i):
-            m, w = TAIL[i]
-            x = pick_pair(6, m, w, "xb", 1)
-            add_pair(6, m, w, x[:])
-            z_bf[(1, m)] = round_gap(1, m, w)
-
-        def both_products(i):
+        def both_products(i, banks):
             for j in range(N_TILES):
-                products(0, i, [j])
-                products(1, i, [j])
+                products(0, i, banks, [j])
+                products(1, i, banks, [j])
 
-        for i in range(1, 4):
-            back(0, i, False)
-        tail(0)
-        codes(0, 1)
-        codes(1, 0)
-        products(1, 0)
-        products(0, 1)
-        tail(1)
+        def turn(s, i, n):
+            add_turned(s, i, n)
+            round_turned(s, i)
+
+        def back(b, i, n):
+            turn_back(b, i, n)
+            copy_back(b, i)
+
+        h_slice(0, lo + hi)
+        h_slice(1, lo + hi)
+
+        h_slice(2, lo + hi)
+        pick_pair(0, 0, PB, "xa", 2)
+        h_slice(3, lo + hi)
+        h_slice(4, lo + hi)
+        bf = round_wb(0, V, "wb_bf", 1)
+        pick_pair(2, 0, PB, "xa", 2)
+        wb_q.append(quantise(bf[:], BANK, "wbq0"))
+        h_slice(5, lo + hi)
+        for i in range(3):
+            turn(0, i, nb(lo + hi))
+        h_slice(6, lo + hi)
+        turn(0, 3, nb(lo + hi))
+        for i in range(4):
+            turn(2, i, nb(lo + hi))
+        h_slice(7, hi)
+        front = ring.tile([P, PACK, HALF], F32, name="x_front", tag="xa", bufs=2, align_bytes=64)
+        rear = ring.tile([P, 2, HALF], F32, name="x_rear", tag="xc", bufs=1, align_bytes=64)
+        for e in range(2):
+            pick(4 + e, 0, HALF, front[:, e, :])
+            pick(4 + e, HALF, HALF, rear[:, e, :])
+        pick(6, 0, HALF, front[:, 2, :])
+        add_own(rear[:], 0, 2, HALF, HALF)
+        for i in range(2):
+            back(0, i, lo[i])
+        bf = round_wb(1, A, "zt0_1", 1)
+        for i in range(2, 4):
+            turn_back(0, i, lo[i])
+        for i in range(2):
+            pick(7, i * CHUNK, CHUNK, front[:, 3, i * CHUNK : (i + 1) * CHUNK])
+        add_own(front[:, :, 0:CHUNK], 0, PACK, 0, CHUNK)
+        gap_codes(0, 0)
+        gap_codes(0, 1)
+        add_own(front[:, :, CHUNK:HALF], 0, PACK, CHUNK, CHUNK)
+        products(0, 0, hi)
+        round_gap(1, 0, "z1_0")
+        round_gap(1, 1, "z1_1")
+        for i in range(2, 4):
+            copy_back(0, i)
+        products(0, 1, lo)
+        wb_q.append(quantise(bf[:], BANK, "wbq1"))
+        gap_codes(1, 0)
+        products(1, 0, hi)
+        pick_pair(6, 2 * CHUNK, CHUNK, "z1_0", 1)
+        gap_codes(1, 1)
+        products(1, 1, lo)
+        add_pair(6, 2, None)
+        gap_codes(0, 2)
+        read_b(0)
+        round_gap(1, 2, "z1_2")
         finish(0)
-        codes(0, 2)
-        codes(1, 1)
-        products(1, 1)
-        products(0, 2)
-        tail(2)
-        tail(3)
+        products(0, 2, hi)
+        pick_pair(6, 3 * CHUNK, CHUNK, "b_sb0_2", 1)
+        gap_codes(1, 2)
+        products(1, 2, hi)
+        add_pair(6, 3, None)
+        read_b(1)
+        round_gap(1, 3, "z1_3")
+        gap_codes(0, 3)
         finish(1)
-        codes(0, 3)
-        codes(1, 2)
-        products(1, 2)
-        products(0, 3)
-        codes(1, 3)
-        products(1, 3)
+        products(0, 3, lo)
+        read_b(2)
+        gap_codes(1, 3)
+        products(1, 3, lo)
         finish(2)
+        read_b(3)
         finish(3)

@@ -28,7 +28,8 @@ CHUNK = 256
 HALF = 512
 CHUNKS = [(m, CHUNK) for m in range(0, PB, CHUNK)]
 HBUFS = 7
-PARTS = CHUNKS
+PARTS = CHUNKS[:3] + [(768, P), (896, P)]
+STAGE = ["w1_raw0", "w1_raw1", "wb_raw0", "wb_raw1", "wb_bf"]
 
 
 def tile_list_clone_audit_kernel(
@@ -49,7 +50,7 @@ def tile_list_clone_audit_kernel(
         nc.sync.dma_start(idx2[:], offs2)
 
         def load_weight(src, name):
-            raw = ring.tile([P, PACK, BANK], F32, name=name, tag="raw", bufs=4)
+            raw = ring.tile([P, PACK, BANK], F32, name=name, tag=name, bufs=1, align_bytes=64)
             nc.sync.dma_start(raw[:], src.rearrange("(p j) c -> p j c", j=PACK))
             return raw
 
@@ -89,9 +90,9 @@ def tile_list_clone_audit_kernel(
         def negate_on_vector(dst, src):
             nc.vector.tensor_scalar(dst, src, -1.0, None, ALU.mult)
 
-        def round_w1(s0, nt, negate, tag):
+        def round_w1(s0, nt, negate, tag, bufs=1):
             b, t0 = divmod(s0, PACK)
-            grouped = ring.tile([P, nt * BANK], BF16, name="w1_bf%d" % s0, tag=tag, bufs=1, align_bytes=64)
+            grouped = ring.tile([P, nt * BANK], BF16, name="w1_bf%d" % s0, tag=tag, bufs=bufs, align_bytes=64)
             negate(
                 grouped[:].rearrange("p (t m j) -> p m j t", t=nt, j=PACK),
                 w1_raw[b][:].rearrange("p j (m t) -> p m j t", t=PACK)[:, :, :, t0 : t0 + nt],
@@ -116,11 +117,13 @@ def tile_list_clone_audit_kernel(
         v_plane = keep.tile([P, S], U8, name="v_plane", align_bytes=64)
         v_words = {}
 
-        def gather_words(c, tag):
-            v_words[c] = ring.tile([P, BANK], U32, name="v_words%d" % c, tag=tag, bufs=1, align_bytes=64)
+        def gather_words(c0, count, tag):
+            words = ring.tile([P, count * BANK], U32, name="v_words%d" % c0, tag=tag, bufs=1, align_bytes=64)
             nc.vector.tensor_copy(
-                v_words[c][:], tab_w[:].bitcast(U32).indirect(idx[:, c * BANK // 16 : (c + 1) * BANK // 16])
+                words[:], tab_w[:].bitcast(U32).indirect(idx[:, c0 * BANK // 16 : (c0 + count) * BANK // 16])
             )
+            for c in range(count):
+                v_words[c0 + c] = words[:, c * BANK : (c + 1) * BANK]
 
         h = {}
 
@@ -132,7 +135,7 @@ def tile_list_clone_audit_kernel(
                 out=acc[:],
                 lhsT=w1_q[s][0].bitcast(FP8X4),
                 lhsT_scale=w1_q[s][1],
-                rhs=v_words[c][:].bitcast(FP8X4),
+                rhs=v_words[c].bitcast(FP8X4),
                 rhs_scale=v_plane[:, c * BANK : (c + 1) * BANK],
                 start=True,
                 stop=True,
@@ -286,12 +289,13 @@ def tile_list_clone_audit_kernel(
             m, w = PARTS[i]
             for j in tiles:
                 if j == 0:
-                    staged[i] = ring.tile([P, N_TILES, w], F32, name="staged%d" % i, tag="raw", bufs=4)
+                    staged[i] = ring.tile([P, N_TILES, w], F32, name="staged%d" % i, tag=STAGE[i], bufs=1, align_bytes=64)
                 nc.vector.scalar_tensor_tensor(
                     staged[i][:, j, :], a_sb[(i, j)][:] if (i, j) in a_sb else accs[(i, j)][:, 0, :], ba_sb[:, j : j + 1], b_sb[(i, j)][:], ALU.add, ALU.mult
                 )
-                if j % 2 == 1:
-                    nc.sync.dma_start(out_v[:, j - 1 : j + 1, m : m + w], staged[i][:, j - 1 : j + 1, :])
+                group = 1 if i == len(PARTS) - 1 and j >= 2 else 2
+                if j % group == group - 1:
+                    nc.sync.dma_start(out_v[:, j + 1 - group : j + 1, m : m + w], staged[i][:, j + 1 - group : j + 1, :])
 
         def late_loads():
             gap.append(ring.tile([P, PACK, PB], F32, name="own1", tag="big", bufs=1))
@@ -316,20 +320,15 @@ def tile_list_clone_audit_kernel(
         wb_q = []
 
         nc.vector.tensor_copy(v_plane[:], tab_plane[:].indirect(idx[:]))
-        for c in range(3):
-            gather_words(c, "vw%d" % c)
-        bf0 = round_w1(0, 1, negate_on_scalar, "vw3")
-        bf1 = round_w1(1, 1, negate_on_scalar, "w1c")
+        gather_words(0, 3, "vw0")
+        bf01 = round_w1(0, 2, negate_on_scalar, "vw1")
         bf23 = round_w1(2, 2, negate_on_scalar, "w1b")
-        w1_codes(0, 1, bf0)
-        gather_words(3, "vw3")
-        w1_codes(1, 1, bf1)
+        w1_codes(0, 2, bf01)
+        gather_words(3, 1, "vw1")
         late_loads()
-        bf45 = round_w1(4, 2, negate_on_vector, "w1c")
         w1_codes(2, 2, bf23)
-        bf67 = round_w1(6, 2, negate_on_vector, "w1b")
-        w1_codes(4, 2, bf45)
-        w1_codes(6, 2, bf67)
+        bf47 = round_w1(4, 4, negate_on_vector, "w1_raw0")
+        w1_codes(4, 4, bf47)
         turn_no = [0]
         lo, hi = [0, 1, 2, 3], [4, 5, 6, 7]
 
@@ -364,37 +363,37 @@ def tile_list_clone_audit_kernel(
         bf = round_wb(0, V, "wb_bf", 1)
         pick_pair(2, 0, PB, "xa", 2)
         wb_q.append(quantise(bf[:], BANK, "wbq0"))
-        h_slice(5, lo + hi)
-        for i in range(3):
-            turn(0, i, nb(lo + hi))
-        h_slice(6, lo + hi)
-        turn(0, 3, nb(lo + hi))
-        for i in range(4):
-            turn(2, i, nb(lo + hi))
-        h_slice(7, hi)
-        front = ring.tile([P, PACK, HALF], F32, name="x_front", tag="xa", bufs=2, align_bytes=64)
+        sums_left = [(s, i) for s in (0, 2) for i in range(4)][:-1]
+        for s in (5, 6, 7):
+            for c in range(S_CHUNKS):
+                h_chunk(s, c, nb(lo + hi))
+                if c > 0 and sums_left:
+                    turn(*sums_left.pop(0), nb(lo + hi))
+        front = ring.tile([P, PACK, HALF], F32, name="x_front", tag="xf", bufs=1, align_bytes=64)
         rear = ring.tile([P, 2, HALF], F32, name="x_rear", tag="xc", bufs=1, align_bytes=64)
         for e in range(2):
-            pick(4 + e, 0, HALF, front[:, e, :])
             pick(4 + e, HALF, HALF, rear[:, e, :])
+            pick(4 + e, 0, HALF, front[:, e, :])
         pick(6, 0, HALF, front[:, 2, :])
         add_own(rear[:], 0, 2, HALF, HALF)
         for i in range(2):
-            back(0, i, lo[i])
+            back(0, i, nb(lo + hi))
         bf = round_wb(1, A, "zt0_1", 1)
-        for i in range(2, 4):
-            turn_back(0, i, lo[i])
+        add_turned(2, 3, lo[3])
+        turn_back(0, 2, lo[2])
         for i in range(2):
             pick(7, i * CHUNK, CHUNK, front[:, 3, i * CHUNK : (i + 1) * CHUNK])
-        add_own(front[:, :, 0:CHUNK], 0, PACK, 0, CHUNK)
         gap_codes(0, 0)
+        add_own(front[:, :, 0:CHUNK], 0, PACK, 0, CHUNK)
         gap_codes(0, 1)
         add_own(front[:, :, CHUNK:HALF], 0, PACK, CHUNK, CHUNK)
         products(0, 0, hi)
         round_gap(1, 0, "z1_0")
+        round_turned(2, 3)
+        turn_back(0, 3, lo[3])
+        copy_back(0, 2)
         round_gap(1, 1, "z1_1")
-        for i in range(2, 4):
-            copy_back(0, i)
+        copy_back(0, 3)
         products(0, 1, lo)
         wb_q.append(quantise(bf[:], BANK, "wbq1"))
         gap_codes(1, 0)
@@ -406,20 +405,31 @@ def tile_list_clone_audit_kernel(
         gap_codes(0, 2)
         read_b(0)
         round_gap(1, 2, "z1_2")
+
         finish(0)
         products(0, 2, hi)
-        pick_pair(6, 3 * CHUNK, CHUNK, "b_sb0_2", 1)
+        pick_pair(6, *PARTS[3], "b_sb0_2", 1)
         gap_codes(1, 2)
         products(1, 2, hi)
         add_pair(6, 3, None)
         read_b(1)
         round_gap(1, 3, "z1_3")
         gap_codes(0, 3)
-        finish(1)
-        products(0, 3, lo)
-        read_b(2)
+        finish(1, [0, 1])
+        products(0, 3, lo[0:2])
+        pick_pair(6, *PARTS[4], "b_sb1_0", 1)
         gap_codes(1, 3)
-        products(1, 3, lo)
-        finish(2)
+        add_pair(6, 4, None)
+        round_gap(1, 4, "z1_4")
+        finish(1, [2, 3])
+        products(1, 3, lo[0:2])
+        products(0, 4, lo[2:4])
+        read_b(2)
+        finish(2, [0, 1])
+        gap_codes(1, 4)
+        products(1, 4, lo[2:4])
+        finish(2, [2, 3])
         read_b(3)
         finish(3)
+        read_b(4)
+        finish(4)

@@ -48,6 +48,8 @@ def tile_list_clone_audit_kernel(
         nc.sync.dma_start(idx[:], offs)
         idx2 = keep.tile([P, PB // 16], U16, name="idx2")
         nc.sync.dma_start(idx2[:], offs2)
+        ba_sb = keep.tile([P, N_TILES], F32, name="ba_sb")
+        bb_sb = keep.tile([P, N_TILES], F32, name="bb_sb")
 
         def load_weight(src, name):
             raw = ring.tile([P, PACK, BANK], F32, name=name, tag=name, bufs=1, align_bytes=64)
@@ -63,11 +65,12 @@ def tile_list_clone_audit_kernel(
                 tab_scales[0, 4 * q : 4 * q + 4, :].bitcast(I32),
             )
         ident = keep.tile([P, P], F32, name="ident")
-        make_identity(nc, ident[:])
+        nc.vector.memset(ident[:], 0.0)
+        make_identity(nc, ident[:], nomemset=True)
 
         tab_w = ring.tile([P, T], I32, name="tab_w", tag="big", bufs=1)
         nc.sync.dma_start(tab_w[:], tab_words[0].rearrange("p t i -> p (t i)").bitcast(I32))
-        w1_raw = [load_weight(w1[:, b * BANK : (b + 1) * BANK], "w1_raw%d" % b) for b in range(PASSES)]
+        w1_raw = [load_weight(w1[:, b * BANK : (b + 1) * BANK], "w1_raw%d" % b)[:] for b in range(PASSES)]
         wgt_sb = keep.tile([P, PB], F32, name="wgt_sb")
         nc.sync.dma_start(wgt_sb[:], wgt)
 
@@ -90,20 +93,22 @@ def tile_list_clone_audit_kernel(
         def negate_on_vector(dst, src):
             nc.vector.tensor_scalar(dst, src, -1.0, None, ALU.mult)
 
-        def round_w1(s0, nt, negate, tag, bufs=1):
+        def round_w1(s0, negate, grouped):
             b, t0 = divmod(s0, PACK)
-            grouped = ring.tile([P, nt * BANK], BF16, name="w1_bf%d" % s0, tag=tag, bufs=bufs, align_bytes=64)
             negate(
-                grouped[:].rearrange("p (t m j) -> p m j t", t=nt, j=PACK),
-                w1_raw[b][:].rearrange("p j (m t) -> p m j t", t=PACK)[:, :, :, t0 : t0 + nt],
+                grouped.rearrange("p (t m j) -> p m j t", t=2, j=PACK),
+                w1_raw[b].rearrange("p j (m t) -> p m j t", t=PACK)[:, :, :, t0 : t0 + 2],
             )
-            return grouped
+
+        def w1_tile(name, count, tag):
+            tile = ring.tile([P, count, 2 * BANK], BF16, name=name, tag=tag, bufs=1, align_bytes=64)
+            return [tile[:, n, :] for n in range(count)]
 
         w1_q = {}
 
-        def w1_codes(s0, nt, grouped):
-            codes, plane = quantise(grouped[:], nt * P, "w1q%d" % s0)
-            for t in range(nt):
+        def w1_codes(s0, grouped):
+            codes, plane = quantise(grouped, 2 * P, "w1q%d" % s0)
+            for t in range(2):
                 w1_q[s0 + t] = (codes[:, t * P : (t + 1) * P], plane[:, t * P : (t + 1) * P])
 
         def round_wb(b, copy, tag, bufs):
@@ -302,7 +307,7 @@ def tile_list_clone_audit_kernel(
             for u in range(2):
                 nc.sync.dma_start(gap[1][:, 2 * u : 2 * u + 2, :], own_v[1, :, 2 * u : 2 * u + 2, :])
             nc.sync.dma_start(wa_w[:].bitcast(I32), wa_words.rearrange("a p c -> p a c").bitcast(I32))
-            nc.gpsimd.memset(wa_plane[:].bitcast(I32), 0)
+            nc.vector.memset(wa_plane[:].bitcast(I32), 0)
             for q in range(4):
                 nc.sync.dma_start(
                     wa_plane[32 * q : 32 * q + 4, :, :].bitcast(I32),
@@ -314,21 +319,24 @@ def tile_list_clone_audit_kernel(
 
         wa_w = keep.tile([P, PASSES, 2 * N], U8, name="wa_w", align_bytes=64)
         wa_plane = keep.tile([P, PASSES, N], U8, name="wa_plane", align_bytes=64)
-        ba_sb = keep.tile([P, N_TILES], F32, name="ba_sb")
-        bb_sb = keep.tile([P, N_TILES], F32, name="bb_sb")
         V, A = nc.vector.tensor_copy, nc.scalar.copy
         wb_q = []
 
         nc.vector.tensor_copy(v_plane[:], tab_plane[:].indirect(idx[:]))
         gather_words(0, 3, "vw0")
-        bf01 = round_w1(0, 2, negate_on_scalar, "vw1")
-        bf23 = round_w1(2, 2, negate_on_scalar, "w1b")
-        w1_codes(0, 2, bf01)
+        (bf01,) = w1_tile("w1_bf01", 1, "vw1")
+        (bf23,) = w1_tile("w1_bf23", 1, "w1b")
+        round_w1(0, negate_on_scalar, bf01)
+        round_w1(2, negate_on_scalar, bf23)
+        w1_codes(0, bf01)
         gather_words(3, 1, "vw1")
         late_loads()
-        w1_codes(2, 2, bf23)
-        bf47 = round_w1(4, 4, negate_on_vector, "w1_raw0")
-        w1_codes(4, 4, bf47)
+        w1_codes(2, bf23)
+        bf45, bf67 = w1_tile("w1_bf47", 2, "w1_raw0")
+        round_w1(4, negate_on_vector, bf45)
+        round_w1(6, negate_on_vector, bf67)
+        w1_codes(4, bf45)
+        w1_codes(6, bf67)
         turn_no = [0]
         lo, hi = [0, 1, 2, 3], [4, 5, 6, 7]
 
@@ -389,26 +397,29 @@ def tile_list_clone_audit_kernel(
         add_own(front[:, :, CHUNK:HALF], 0, PACK, CHUNK, CHUNK)
         products(0, 0, hi)
         round_gap(1, 0, "z1_0")
-        round_turned(2, 3)
-        turn_back(0, 3, lo[3])
-        copy_back(0, 2)
         round_gap(1, 1, "z1_1")
-        copy_back(0, 3)
-        products(0, 1, lo)
+        round_turned(2, 3)
+        copy_back(0, 2)
+        products(0, 1, lo, [0, 1])
         wb_q.append(quantise(bf[:], BANK, "wbq1"))
         gap_codes(1, 0)
         products(1, 0, hi)
+        back(0, 3, lo[3])
         pick_pair(6, 2 * CHUNK, CHUNK, "z1_0", 1)
         gap_codes(1, 1)
-        products(1, 1, lo)
+        products(1, 1, lo, [0, 1])
+        for j in (2, 3):
+            products(0, 1, lo, [j])
+            products(1, 1, lo, [j])
         add_pair(6, 2, None)
         gap_codes(0, 2)
         read_b(0)
         round_gap(1, 2, "z1_2")
 
-        finish(0)
+        finish(0, [0, 1, 2])
+        pick_pair(6, *PARTS[3], "b_sb0_1", 1)
+        finish(0, [3])
         products(0, 2, hi)
-        pick_pair(6, *PARTS[3], "b_sb0_2", 1)
         gap_codes(1, 2)
         products(1, 2, hi)
         add_pair(6, 3, None)

@@ -29,7 +29,7 @@ HALF = 512
 CHUNKS = [(m, CHUNK) for m in range(0, PB, CHUNK)]
 HBUFS = 7
 PARTS = CHUNKS[:3] + [(768, P), (896, P)]
-STAGE = ["w1_raw0", "w1_raw1", "wb_raw0", "wb_raw1", "wb_bf"]
+STAGE = ["w1_raw0", "big", "xc", "vw0", "wb_bf"]
 
 
 def tile_list_clone_audit_kernel(
@@ -46,40 +46,50 @@ def tile_list_clone_audit_kernel(
 
         idx = keep.tile([P, S // 16], U16, name="idx")
         nc.sync.dma_start(idx[:], offs)
-        idx2 = keep.tile([P, PB // 16], U16, name="idx2")
-        nc.sync.dma_start(idx2[:], offs2)
-        ba_sb = keep.tile([P, N_TILES], F32, name="ba_sb")
-        bb_sb = keep.tile([P, N_TILES], F32, name="bb_sb")
 
         def load_weight(src, name):
             raw = ring.tile([P, PACK, BANK], F32, name=name, tag=name, bufs=1, align_bytes=64)
             nc.sync.dma_start(raw[:], src.rearrange("(p j) c -> p j c", j=PACK))
             return raw
 
-        tab_plane = keep.tile([P, T], U8, name="tab_plane")
+        tab_plane = ring.tile([P, T], U8, name="tab_plane", tag="late", bufs=1)
         nc.vector.memset(tab_plane[:, 0:CLEAR_SPLIT].bitcast(I32), 0)
         nc.gpsimd.memset(tab_plane[:, CLEAR_SPLIT:T].bitcast(I32), 0)
-        for q in range(4):
-            nc.sync.dma_start(
-                tab_plane[32 * q : 32 * q + 4, :].bitcast(I32),
-                tab_scales[0, 4 * q : 4 * q + 4, :].bitcast(I32),
-            )
+        idx2 = keep.tile([P, PB // 16], U16, name="idx2")
+        nc.sync.dma_start(idx2[:], offs2)
+        nc.sync.dma_start(tab_plane[0:P:8, :].bitcast(I32), tab_scales[0].bitcast(I32))
+        v_plane = keep.tile([P, S], U8, name="v_plane", align_bytes=64)
+        nc.vector.memset(v_plane[:].bitcast(I32), 0)
         ident = keep.tile([P, P], F32, name="ident")
         nc.vector.memset(ident[:], 0.0)
         make_identity(nc, ident[:], nomemset=True)
 
-        tab_w = ring.tile([P, T], I32, name="tab_w", tag="big", bufs=1)
+        tab_w = ring.tile([P, T], I32, name="tab_w", tag="big", bufs=1, align_bytes=64)
         nc.sync.dma_start(tab_w[:], tab_words[0].rearrange("p t i -> p (t i)").bitcast(I32))
-        w1_raw = [load_weight(w1[:, b * BANK : (b + 1) * BANK], "w1_raw%d" % b)[:] for b in range(PASSES)]
-        wgt_sb = keep.tile([P, PB], F32, name="wgt_sb")
-        nc.sync.dma_start(wgt_sb[:], wgt)
+        w1_raw = [load_weight(w1[:, 0:BANK], "w1_raw0")[:]]
+        picked = ring.tile([P, S], U8, name="picked", tag="wb_bf", bufs=1, align_bytes=64)
+        nc.vector.tensor_copy(picked[:], tab_plane[:].indirect(idx[:]))
+        for r in range(4):
+            nc.sync.dma_start(v_plane[r:P:32, :].bitcast(I32), picked[8 * r : P : 32, :].bitcast(I32))
 
         own_v = own.rearrange("(b p t) m -> b p t m", p=P, t=PACK)
-        gap = [keep.tile([P, PACK, PB], F32, name="own0")]
-        wb_raw = []
+        late = ring.tile([P, 3 * PACK * PB + PACK * BANK + PB], F32, name="late", tag="late", bufs=1)
+        w1_at = 3 * PACK * PB
+        w1_raw.append(late[:, w1_at : w1_at + PACK * BANK].rearrange("p (j c) -> p j c", j=PACK))
+        nc.sync.dma_start(w1_raw[1], w1[:, BANK : 2 * BANK].rearrange("(p j) c -> p j c", j=PACK))
+        wgt_sb = late[:, w1_at + PACK * BANK : w1_at + PACK * BANK + PB]
+        nc.sync.dma_start(wgt_sb, wgt)
+        gap = [late[:, b * PACK * PB : (b + 1) * PACK * PB].rearrange("p (t m) -> p t m", t=PACK) for b in range(PASSES)]
+        wb_at = 2 * PACK * PB
+        wb_raw = [
+            late[:, wb_at + b * PACK * N : wb_at + (b + 1) * PACK * N].rearrange("p (j c) -> p j c", j=PACK)
+            for b in range(PASSES)
+        ]
         for u in range(2):
             nc.sync.dma_start(gap[0][:, 2 * u : 2 * u + 2, :], own_v[0, :, 2 * u : 2 * u + 2, :])
-            wb_raw.append(load_weight(wb[u * BANK : (u + 1) * BANK, :], "wb_raw%d" % u))
+            nc.sync.dma_start(wb_raw[u], wb[u * BANK : (u + 1) * BANK, :].rearrange("(p j) c -> p j c", j=PACK))
+        for u in range(2):
+            nc.sync.dma_start(gap[1][:, 2 * u : 2 * u + 2, :], own_v[1, :, 2 * u : 2 * u + 2, :])
 
         def quantise(grouped, width, name):
             codes = ring.tile([P, width], U32, name=name + "_codes", tag=name + "_codes", bufs=1, align_bytes=64)
@@ -115,11 +125,10 @@ def tile_list_clone_audit_kernel(
             grouped = ring.tile([P, PACK * BANK], BF16, name="wb_bf%d" % b, tag=tag, bufs=bufs, align_bytes=64)
             copy(
                 grouped[:].rearrange("p (c i j) -> p c j i", i=4, j=PACK),
-                wb_raw[b][:].rearrange("p j (c i) -> p c j i", i=4),
+                wb_raw[b].rearrange("p j (c i) -> p c j i", i=4),
             )
             return grouped
 
-        v_plane = keep.tile([P, S], U8, name="v_plane", align_bytes=64)
         v_words = {}
 
         def gather_words(c0, count, tag):
@@ -264,8 +273,8 @@ def tile_list_clone_audit_kernel(
                 for c0 in range(0, w, P):
                     nc.tensor.matmul_mx(
                         out=both[:, 0, c0 : c0 + P],
-                        lhsT=wa_w[:, b, 2 * j * P : 2 * (j + 1) * P].bitcast(FP4X4),
-                        lhsT_scale=wa_plane[:, b, j * P : (j + 1) * P],
+                        lhsT=wa[0][:, b, 2 * j * P : 2 * (j + 1) * P].bitcast(FP4X4),
+                        lhsT_scale=wa[1][:, b, j * P : (j + 1) * P],
                         rhs=codes[:, z0 + c0 : z0 + c0 + P].bitcast(FP8X4),
                         rhs_scale=plane[:, z0 + c0 : z0 + c0 + P],
                         start=False,
@@ -280,7 +289,7 @@ def tile_list_clone_audit_kernel(
         def read_b(i, tiles=range(N_TILES)):
             for j in tiles:
                 b_sb[(i, j)] = ring.tile([P, PARTS[i][1]], F32, name="b_sb%d_%d" % (i, j), tag="b_sb%d_%d" % (i % 2, j), bufs=1, align_bytes=64)
-                nc.scalar.activation(b_sb[(i, j)][:], accs[(i, j)][:, 1, :], ACT.Identity, bias=bb_sb[:, j : j + 1])
+                nc.scalar.activation(b_sb[(i, j)][:], accs[(i, j)][:, 1, :], ACT.Identity, bias=wa[2][:, 1, j : j + 1])
 
         a_sb = {}
 
@@ -296,16 +305,17 @@ def tile_list_clone_audit_kernel(
                 if j == 0:
                     staged[i] = ring.tile([P, N_TILES, w], F32, name="staged%d" % i, tag=STAGE[i], bufs=1, align_bytes=64)
                 nc.vector.scalar_tensor_tensor(
-                    staged[i][:, j, :], a_sb[(i, j)][:] if (i, j) in a_sb else accs[(i, j)][:, 0, :], ba_sb[:, j : j + 1], b_sb[(i, j)][:], ALU.add, ALU.mult
+                    staged[i][:, j, :], a_sb[(i, j)][:] if (i, j) in a_sb else accs[(i, j)][:, 0, :], wa[2][:, 0, j : j + 1], b_sb[(i, j)][:], ALU.add, ALU.mult
                 )
                 group = 1 if i == len(PARTS) - 1 and j >= 2 else 2
                 if j % group == group - 1:
                     nc.sync.dma_start(out_v[:, j + 1 - group : j + 1, m : m + w], staged[i][:, j + 1 - group : j + 1, :])
 
         def late_loads():
-            gap.append(ring.tile([P, PACK, PB], F32, name="own1", tag="big", bufs=1))
-            for u in range(2):
-                nc.sync.dma_start(gap[1][:, 2 * u : 2 * u + 2, :], own_v[1, :, 2 * u : 2 * u + 2, :])
+            wa.append(ring.tile([P, PASSES, 2 * N], U8, name="wa_w", tag="w1q0_codes", bufs=1, align_bytes=64))
+            wa.append(ring.tile([P, PASSES, N], U8, name="wa_plane", tag="w1q2_plane", bufs=1, align_bytes=64))
+            wa.append(ring.tile([P, 2, 2 * N_TILES], F32, name="bias", tag="w1q0_plane", bufs=1, align_bytes=64))
+            wa_w, wa_plane, bias = wa
             nc.sync.dma_start(wa_w[:].bitcast(I32), wa_words.rearrange("a p c -> p a c").bitcast(I32))
             nc.vector.memset(wa_plane[:].bitcast(I32), 0)
             for q in range(4):
@@ -314,15 +324,13 @@ def tile_list_clone_audit_kernel(
                     wa_scales[:, 4 * q : 4 * q + 4, :].rearrange("a r c -> r a c").bitcast(I32),
                 )
             with nc.allow_non_contiguous_dma(reason="one bias value a partition"):
-                nc.sync.dma_start(ba_sb[:], ba.rearrange("(j p) -> p j", p=P))
-                nc.sync.dma_start(bb_sb[:], bb.rearrange("(j p) -> p j", p=P))
+                nc.sync.dma_start(bias[:, 0, 0:N_TILES], ba.rearrange("(j p) -> p j", p=P))
+                nc.sync.dma_start(bias[:, 1, 0:N_TILES], bb.rearrange("(j p) -> p j", p=P))
 
-        wa_w = keep.tile([P, PASSES, 2 * N], U8, name="wa_w", align_bytes=64)
-        wa_plane = keep.tile([P, PASSES, N], U8, name="wa_plane", align_bytes=64)
+        wa = []
         V, A = nc.vector.tensor_copy, nc.scalar.copy
         wb_q = []
 
-        nc.vector.tensor_copy(v_plane[:], tab_plane[:].indirect(idx[:]))
         gather_words(0, 3, "vw0")
         (bf01,) = w1_tile("w1_bf01", 1, "vw1")
         (bf23,) = w1_tile("w1_bf23", 1, "w1b")
@@ -330,7 +338,6 @@ def tile_list_clone_audit_kernel(
         round_w1(2, negate_on_scalar, bf23)
         w1_codes(0, bf01)
         gather_words(3, 1, "vw1")
-        late_loads()
         w1_codes(2, bf23)
         bf45, bf67 = w1_tile("w1_bf47", 2, "w1_raw0")
         round_w1(4, negate_on_vector, bf45)
@@ -367,6 +374,7 @@ def tile_list_clone_audit_kernel(
         h_slice(2, lo + hi)
         pick_pair(0, 0, PB, "xa", 2)
         h_slice(3, lo + hi)
+        late_loads()
         h_slice(4, lo + hi)
         bf = round_wb(0, V, "wb_bf", 1)
         pick_pair(2, 0, PB, "xa", 2)
@@ -377,7 +385,7 @@ def tile_list_clone_audit_kernel(
                 h_chunk(s, c, nb(lo + hi))
                 if c > 0 and sums_left:
                     turn(*sums_left.pop(0), nb(lo + hi))
-        front = ring.tile([P, PACK, HALF], F32, name="x_front", tag="xf", bufs=1, align_bytes=64)
+        front = ring.tile([P, PACK, HALF], F32, name="x_front", tag="big", bufs=1, align_bytes=64)
         rear = ring.tile([P, 2, HALF], F32, name="x_rear", tag="xc", bufs=1, align_bytes=64)
         for e in range(2):
             pick(4 + e, HALF, HALF, rear[:, e, :])

@@ -23,7 +23,6 @@ BANK = 512
 PASSES = H // (P * PACK)
 N_TILES = N // P
 S_CHUNKS = S // BANK
-CLEAR_SPLIT = 2816
 CHUNK = 256
 HALF = 512
 CHUNKS = [(m, CHUNK) for m in range(0, PB, CHUNK)]
@@ -53,10 +52,12 @@ def tile_list_clone_audit_kernel(
             return raw
 
         tab_plane = ring.tile([P, T], U8, name="tab_plane", tag="late", bufs=1)
-        nc.vector.memset(tab_plane[:, 0:CLEAR_SPLIT].bitcast(I32), 0)
-        nc.gpsimd.memset(tab_plane[:, CLEAR_SPLIT:T].bitcast(I32), 0)
+        nc.vector.memset(tab_plane[:].bitcast(I32), 0)
         idx2 = keep.tile([P, PB // 16], U16, name="idx2")
         nc.sync.dma_start(idx2[:], offs2)
+        ba_sb = keep.tile([P, N_TILES], F32, name="ba_sb")
+        with nc.allow_non_contiguous_dma(reason="one bias value a partition"):
+            nc.sync.dma_start(ba_sb[:], ba.rearrange("(j p) -> p j", p=P))
         nc.sync.dma_start(tab_plane[0:P:8, :].bitcast(I32), tab_scales[0].bitcast(I32))
         v_plane = keep.tile([P, S], U8, name="v_plane", align_bytes=64)
         nc.vector.memset(v_plane[:].bitcast(I32), 0)
@@ -289,7 +290,7 @@ def tile_list_clone_audit_kernel(
         def read_b(i, tiles=range(N_TILES)):
             for j in tiles:
                 b_sb[(i, j)] = ring.tile([P, PARTS[i][1]], F32, name="b_sb%d_%d" % (i, j), tag="b_sb%d_%d" % (i % 2, j), bufs=1, align_bytes=64)
-                nc.scalar.activation(b_sb[(i, j)][:], accs[(i, j)][:, 1, :], ACT.Identity, bias=wa[2][:, 1, j : j + 1])
+                nc.scalar.activation(b_sb[(i, j)][:], accs[(i, j)][:, 1, :], ACT.Identity, bias=wa[2][:, j : j + 1])
 
         a_sb = {}
 
@@ -305,7 +306,7 @@ def tile_list_clone_audit_kernel(
                 if j == 0:
                     staged[i] = ring.tile([P, N_TILES, w], F32, name="staged%d" % i, tag=STAGE[i], bufs=1, align_bytes=64)
                 nc.vector.scalar_tensor_tensor(
-                    staged[i][:, j, :], a_sb[(i, j)][:] if (i, j) in a_sb else accs[(i, j)][:, 0, :], wa[2][:, 0, j : j + 1], b_sb[(i, j)][:], ALU.add, ALU.mult
+                    staged[i][:, j, :], a_sb[(i, j)][:] if (i, j) in a_sb else accs[(i, j)][:, 0, :], ba_sb[:, j : j + 1], b_sb[(i, j)][:], ALU.add, ALU.mult
                 )
                 group = 1 if i == len(PARTS) - 1 and j >= 2 else 2
                 if j % group == group - 1:
@@ -314,7 +315,7 @@ def tile_list_clone_audit_kernel(
         def late_loads():
             wa.append(ring.tile([P, PASSES, 2 * N], U8, name="wa_w", tag="w1q0_codes", bufs=1, align_bytes=64))
             wa.append(ring.tile([P, PASSES, N], U8, name="wa_plane", tag="w1q2_plane", bufs=1, align_bytes=64))
-            wa.append(ring.tile([P, 2, 2 * N_TILES], F32, name="bias", tag="w1q0_plane", bufs=1, align_bytes=64))
+            wa.append(ring.tile([P, N_TILES], F32, name="bb_sb", tag="w1q0_plane", bufs=1, align_bytes=64))
             wa_w, wa_plane, bias = wa
             nc.sync.dma_start(wa_w[:].bitcast(I32), wa_words.rearrange("a p c -> p a c").bitcast(I32))
             nc.vector.memset(wa_plane[:].bitcast(I32), 0)
@@ -324,8 +325,7 @@ def tile_list_clone_audit_kernel(
                     wa_scales[:, 4 * q : 4 * q + 4, :].rearrange("a r c -> r a c").bitcast(I32),
                 )
             with nc.allow_non_contiguous_dma(reason="one bias value a partition"):
-                nc.sync.dma_start(bias[:, 0, 0:N_TILES], ba.rearrange("(j p) -> p j", p=P))
-                nc.sync.dma_start(bias[:, 1, 0:N_TILES], bb.rearrange("(j p) -> p j", p=P))
+                nc.sync.dma_start(bias[:], bb.rearrange("(j p) -> p j", p=P))
 
         wa = []
         V, A = nc.vector.tensor_copy, nc.scalar.copy

@@ -92,8 +92,8 @@ def tile_list_clone_audit_kernel(
         for u in range(2):
             nc.sync.dma_start(gap[1][:, 2 * u : 2 * u + 2, :], own_v[1, :, 2 * u : 2 * u + 2, :])
 
-        def quantise(grouped, width, name):
-            codes = ring.tile([P, width], U32, name=name + "_codes", tag=name + "_codes", bufs=1, align_bytes=64)
+        def quantise(grouped, width, name, tag=None):
+            codes = ring.tile([P, width], U32, name=name + "_codes", tag=tag or name + "_codes", bufs=1, align_bytes=64)
             plane = ring.tile([P, width], U8, name=name + "_plane", tag=name + "_plane", bufs=1, align_bytes=64)
             nc.vector.quantize_mx(out=codes[:].bitcast(FP8X4), scales=plane[:], in_=grouped)
             return codes, plane
@@ -239,15 +239,17 @@ def tile_list_clone_audit_kernel(
             d = gap[1][:, t0 : t0 + 2, m : m + w]
             nc.vector.tensor_tensor(d, xs[(s, i)], d, ALU.add)
 
-        def round_gap(b, i, tag):
+        def round_gap(b, i, tag, summed=None):
+            if summed is None:
+                summed = gap[1][:, :, PARTS[i][0] : PARTS[i][0] + PARTS[i][1]]
             nc.scalar.activation(
                 new_z(b, i, tag)[:].rearrange("p (c i t) -> p c t i", i=4, t=PACK),
-                gap[1][:, :, PARTS[i][0] : PARTS[i][0] + PARTS[i][1]].rearrange("p t (c i) -> p c t i", i=4),
+                summed.rearrange("p t (c i) -> p c t i", i=4),
                 ACT.Abs,
             )
 
-        def gap_codes(b, i):
-            z_q[(b, i)] = quantise(z_bf[(b, i)][:], (PARTS if b else CHUNKS)[i][1], "zq%d_%d" % (b, i))
+        def gap_codes(b, i, tag=None):
+            z_q[(b, i)] = quantise(z_bf[(b, i)][:], (PARTS if b else CHUNKS)[i][1], "zq%d_%d" % (b, i), tag)
 
         accs = {}
 
@@ -255,7 +257,7 @@ def tile_list_clone_audit_kernel(
             m, w = PARTS[i]
             codes, plane = z_q[(b, i if b else m // CHUNK)]
             z0 = 0 if b else m % CHUNK
-            per_bank = CHUNK // w
+            per_bank = N_TILES // len(banks)
             for j in tiles:
                 if b == 0 and j % per_bank == 0:
                     acc = bank(banks[j // per_bank], [per_bank, 2, w], "acc%d_%d" % (i, j))
@@ -289,7 +291,7 @@ def tile_list_clone_audit_kernel(
 
         def read_b(i, tiles=range(N_TILES)):
             for j in tiles:
-                b_sb[(i, j)] = ring.tile([P, PARTS[i][1]], F32, name="b_sb%d_%d" % (i, j), tag="b_sb%d_%d" % (i % 2, j), bufs=1, align_bytes=64)
+                b_sb[(i, j)] = ring.tile([P, PARTS[i][1]], F32, name="b_sb%d_%d" % (i, j), tag="z0_%d" % (i // 4) if i in (2, 4) and j == 2 else "b_sb%d_%d" % (i % 2, j), bufs=1, align_bytes=64)
                 nc.scalar.activation(b_sb[(i, j)][:], accs[(i, j)][:, 1, :], ACT.Identity, bias=wa[2][:, j : j + 1])
 
         a_sb = {}
@@ -372,81 +374,102 @@ def tile_list_clone_audit_kernel(
         h_slice(1, lo + hi)
 
         h_slice(2, lo + hi)
-        pick_pair(0, 0, PB, "xa", 2)
+        pick_pair(0, 0, PB, "xa0", 1)
         h_slice(3, lo + hi)
         late_loads()
         h_slice(4, lo + hi)
         bf = round_wb(0, V, "wb_bf", 1)
-        pick_pair(2, 0, PB, "xa", 2)
+        pick_pair(2, 0, PB, "xa2", 1)
         wb_q.append(quantise(bf[:], BANK, "wbq0"))
         sums_left = [(s, i) for s in (0, 2) for i in range(4)][:-1]
-        for s in (5, 6, 7):
+        for s in (5, 6):
             for c in range(S_CHUNKS):
                 h_chunk(s, c, nb(lo + hi))
-                if c > 0 and sums_left:
+                if c > 0:
                     turn(*sums_left.pop(0), nb(lo + hi))
+        for c in range(S_CHUNKS):
+            h_chunk(7, c, hi[c])
+            if c == 1:
+                turn(*sums_left.pop(0), lo[0])
+        turn_back(0, 0, lo[1])
+        turn_back(0, 1, lo[2])
+        add_turned(2, 3, lo[3])
         front = ring.tile([P, PACK, HALF], F32, name="x_front", tag="big", bufs=1, align_bytes=64)
-        rear = ring.tile([P, 2, HALF], F32, name="x_rear", tag="xc", bufs=1, align_bytes=64)
+        rear = ring.tile([P, 3, HALF], F32, name="x_rear", tag="xc", bufs=1, align_bytes=64)
+
+        def pick_last(i, tag):
+            m, w = PARTS[i]
+            x = ring.tile([P, 1, w], F32, name="x_last%d" % i, tag=tag, bufs=1, align_bytes=64)
+            pick(7, m, w, x[:, 0, :])
+            return x
+
         for e in range(2):
             pick(4 + e, HALF, HALF, rear[:, e, :])
             pick(4 + e, 0, HALF, front[:, e, :])
+        pick(6, HALF, CHUNK + P, rear[:, 2, 0 : CHUNK + P])
         pick(6, 0, HALF, front[:, 2, :])
-        add_own(rear[:], 0, 2, HALF, HALF)
-        for i in range(2):
-            back(0, i, nb(lo + hi))
-        bf = round_wb(1, A, "zt0_1", 1)
-        add_turned(2, 3, lo[3])
-        turn_back(0, 2, lo[2])
+        add_own(rear[:, :, CHUNK : CHUNK + P], 0, 3, *PARTS[3])
+        add_own(rear[:, 0:2, CHUNK + P : HALF], 0, 2, *PARTS[4])
+        copy_back(0, 0)
+        round_turned(2, 3)
+        copy_back(0, 1)
+        bf = round_wb(1, A, "xa2", 1)
+        turn_back(0, 2, lo[0])
+        turn_back(0, 3, lo[3])
         for i in range(2):
             pick(7, i * CHUNK, CHUNK, front[:, 3, i * CHUNK : (i + 1) * CHUNK])
         gap_codes(0, 0)
-        add_own(front[:, :, 0:CHUNK], 0, PACK, 0, CHUNK)
+        first = ring.tile([P, PACK, CHUNK], F32, name="gap_first", tag="xa0", bufs=1, align_bytes=64)
+        nc.vector.tensor_tensor(first[:], front[:, :, 0:CHUNK], gap[1][:, :, 0:CHUNK], ALU.add)
         gap_codes(0, 1)
         add_own(front[:, :, CHUNK:HALF], 0, PACK, CHUNK, CHUNK)
+        second = [lo[1], lo[2], lo[0], lo[3]]
         products(0, 0, hi)
-        round_gap(1, 0, "z1_0")
-        round_gap(1, 1, "z1_1")
-        round_turned(2, 3)
+        products(0, 1, second, [0, 1])
+        round_gap(1, 0, "z1_0", first[:])
         copy_back(0, 2)
-        products(0, 1, lo, [0, 1])
+        copy_back(0, 3)
+        round_gap(1, 1, "z1_1")
         wb_q.append(quantise(bf[:], BANK, "wbq1"))
         gap_codes(1, 0)
         products(1, 0, hi)
-        back(0, 3, lo[3])
-        pick_pair(6, 2 * CHUNK, CHUNK, "z1_0", 1)
+        products(0, 1, second, [2, 3])
+        third = ring.tile([P, PACK, CHUNK], F32, name="gap_third", tag="xa0", bufs=1, align_bytes=64)
+        pick(7, HALF, CHUNK, third[:, 3, :])
+        nc.vector.tensor_tensor(third[:, 0:3, :], rear[:, :, 0:CHUNK], gap[1][:, 0:3, HALF : HALF + CHUNK], ALU.add)
+        nc.vector.tensor_tensor(third[:, 3, :], third[:, 3, :], gap[1][:, 3, HALF : HALF + CHUNK], ALU.add)
         gap_codes(1, 1)
-        products(1, 1, lo, [0, 1])
-        for j in (2, 3):
-            products(0, 1, lo, [j])
-            products(1, 1, lo, [j])
-        add_pair(6, 2, None)
         gap_codes(0, 2)
+        products(1, 1, second)
         read_b(0)
-        round_gap(1, 2, "z1_2")
-
-        finish(0, [0, 1, 2])
-        pick_pair(6, *PARTS[3], "b_sb0_1", 1)
-        finish(0, [3])
+        round_gap(1, 2, "z1_2", third[:])
+        finish(0)
         products(0, 2, hi)
+        x = pick_last(3, "b_sb0_1")
+        gap_codes(0, 3, "b_sb0_2")
+        add_own(x[:], 3, 1, *PARTS[3])
         gap_codes(1, 2)
         products(1, 2, hi)
-        add_pair(6, 3, None)
         read_b(1)
-        round_gap(1, 3, "z1_3")
-        gap_codes(0, 3)
         finish(1, [0, 1])
-        products(0, 3, lo[0:2])
         pick_pair(6, *PARTS[4], "b_sb1_0", 1)
+        round_gap(1, 3, "z1_3")
         gap_codes(1, 3)
         add_pair(6, 4, None)
-        round_gap(1, 4, "z1_4")
         finish(1, [2, 3])
-        products(1, 3, lo[0:2])
-        products(0, 4, lo[2:4])
-        read_b(2)
+        products(0, 3, [lo[1], lo[2]])
+        products(1, 3, [lo[1], lo[2]])
+        last = [lo[0], lo[3], hi[0], hi[1]]
+        products(0, 4, last, [0, 1])
+        read_b(2, [0, 1])
+        round_gap(1, 4, "z1_4")
+        read_b(2, [2, 3])
         finish(2, [0, 1])
         gap_codes(1, 4)
-        products(1, 4, lo[2:4])
+        products(1, 4, last, [0, 1])
+        for j in (2, 3):
+            products(0, 4, last, [j])
+            products(1, 4, last, [j])
         finish(2, [2, 3])
         read_b(3)
         finish(3)

@@ -52,26 +52,25 @@ def tile_list_clone_audit_kernel(
             return raw
 
         tab_plane = ring.tile([P, T], U8, name="tab_plane", tag="late", bufs=1)
-        nc.vector.memset(tab_plane[:].bitcast(I32), 0)
-        idx2 = keep.tile([P, PB // 16], U16, name="idx2")
-        nc.sync.dma_start(idx2[:], offs2)
-        ba_sb = keep.tile([P, N_TILES], F32, name="ba_sb")
-        with nc.allow_non_contiguous_dma(reason="one bias value a partition"):
-            nc.sync.dma_start(ba_sb[:], ba.rearrange("(j p) -> p j", p=P))
-        nc.sync.dma_start(tab_plane[0:P:8, :].bitcast(I32), tab_scales[0].bitcast(I32))
-        v_plane = keep.tile([P, S], U8, name="v_plane", align_bytes=64)
-        nc.vector.memset(v_plane[:].bitcast(I32), 0)
         ident = keep.tile([P, P], F32, name="ident")
         nc.vector.memset(ident[:], 0.0)
         make_identity(nc, ident[:], nomemset=True)
+        for first in range(2):
+            nc.sync.dma_start(tab_plane[first:32:2, :].bitcast(I32), tab_scales[0].bitcast(I32))
+        nc.vector.memset(tab_plane[64:P, :].bitcast(I32), 0)
+        nc.vector.memset(tab_plane[32:64, :].bitcast(I32), 0)
+        v_plane = keep.tile([P, S], U8, name="v_plane", align_bytes=64)
+        nc.vector.memset(v_plane[:].bitcast(I32), 0)
 
         tab_w = ring.tile([P, T], I32, name="tab_w", tag="big", bufs=1, align_bytes=64)
         nc.sync.dma_start(tab_w[:], tab_words[0].rearrange("p t i -> p (t i)").bitcast(I32))
         w1_raw = [load_weight(w1[:, 0:BANK], "w1_raw0")[:]]
+        idx2 = keep.tile([P, PB // 16], U16, name="idx2")
+        nc.sync.dma_start(idx2[:], offs2)
         picked = ring.tile([P, S], U8, name="picked", tag="wb_bf", bufs=1, align_bytes=64)
         nc.vector.tensor_copy(picked[:], tab_plane[:].indirect(idx[:]))
         for r in range(4):
-            nc.sync.dma_start(v_plane[r:P:32, :].bitcast(I32), picked[8 * r : P : 32, :].bitcast(I32))
+            nc.sync.dma_start(v_plane[r:P:32, :].bitcast(I32), picked[2 * r : 32 : 8, :].bitcast(I32))
 
         own_v = own.rearrange("(b p t) m -> b p t m", p=P, t=PACK)
         late = ring.tile([P, 3 * PACK * PB + PACK * BANK + PB], F32, name="late", tag="late", bufs=1)
@@ -308,7 +307,7 @@ def tile_list_clone_audit_kernel(
                 if j == 0:
                     staged[i] = ring.tile([P, N_TILES, w], F32, name="staged%d" % i, tag=STAGE[i], bufs=1, align_bytes=64)
                 nc.vector.scalar_tensor_tensor(
-                    staged[i][:, j, :], a_sb[(i, j)][:] if (i, j) in a_sb else accs[(i, j)][:, 0, :], ba_sb[:, j : j + 1], b_sb[(i, j)][:], ALU.add, ALU.mult
+                    staged[i][:, j, :], a_sb[(i, j)][:] if (i, j) in a_sb else accs[(i, j)][:, 0, :], wa[3][:, j : j + 1], b_sb[(i, j)][:], ALU.add, ALU.mult
                 )
                 group = 1 if i == len(PARTS) - 1 and j >= 2 else 2
                 if j % group == group - 1:
@@ -318,9 +317,10 @@ def tile_list_clone_audit_kernel(
             wa.append(ring.tile([P, PASSES, 2 * N], U8, name="wa_w", tag="w1q0_codes", bufs=1, align_bytes=64))
             wa.append(ring.tile([P, PASSES, N], U8, name="wa_plane", tag="w1q2_plane", bufs=1, align_bytes=64))
             wa.append(ring.tile([P, N_TILES], F32, name="bb_sb", tag="w1q0_plane", bufs=1, align_bytes=64))
-            wa_w, wa_plane, bias = wa
+            wa.append(ring.tile([P, N_TILES], F32, name="ba_sb", tag="w1q2_codes", bufs=1, align_bytes=64))
+            wa_w, wa_plane, bias, bias_a = wa
             nc.sync.dma_start(wa_w[:].bitcast(I32), wa_words.rearrange("a p c -> p a c").bitcast(I32))
-            nc.vector.memset(wa_plane[:].bitcast(I32), 0)
+            nc.gpsimd.memset(wa_plane[:].bitcast(I32), 0)
             for q in range(4):
                 nc.sync.dma_start(
                     wa_plane[32 * q : 32 * q + 4, :, :].bitcast(I32),
@@ -328,6 +328,7 @@ def tile_list_clone_audit_kernel(
                 )
             with nc.allow_non_contiguous_dma(reason="one bias value a partition"):
                 nc.sync.dma_start(bias[:], bb.rearrange("(j p) -> p j", p=P))
+                nc.sync.dma_start(bias_a[:], ba.rearrange("(j p) -> p j", p=P))
 
         wa = []
         V, A = nc.vector.tensor_copy, nc.scalar.copy
@@ -427,9 +428,9 @@ def tile_list_clone_audit_kernel(
         products(0, 0, hi)
         products(0, 1, second, [0, 1])
         round_gap(1, 0, "z1_0", first[:])
+        round_gap(1, 1, "z1_1")
         copy_back(0, 2)
         copy_back(0, 3)
-        round_gap(1, 1, "z1_1")
         wb_q.append(quantise(bf[:], BANK, "wbq1"))
         gap_codes(1, 0)
         products(1, 0, hi)

@@ -121,12 +121,13 @@ def tile_list_clone_audit_kernel(
             for t in range(2):
                 w1_q[s0 + t] = (codes[:, t * P : (t + 1) * P], plane[:, t * P : (t + 1) * P])
 
-        def round_wb(b, copy, tag, bufs):
-            grouped = ring.tile([P, PACK * BANK], BF16, name="wb_bf%d" % b, tag=tag, bufs=bufs, align_bytes=64)
-            copy(
-                grouped[:].rearrange("p (c i j) -> p c j i", i=4, j=PACK),
-                wb_raw[b].rearrange("p j (c i) -> p c j i", i=4),
-            )
+        def round_wb(b, shares, tag):
+            grouped = ring.tile([P, PACK * BANK], BF16, name="wb_bf%d" % b, tag=tag, bufs=1, align_bytes=64)
+            for copy, first, last in shares:
+                copy(
+                    grouped[:, PACK * first : PACK * last].rearrange("p (c i j) -> p c j i", i=4, j=PACK),
+                    wb_raw[b][:, :, first:last].rearrange("p j (c i) -> p c j i", i=4),
+                )
             return grouped
 
         v_words = {}
@@ -378,21 +379,26 @@ def tile_list_clone_audit_kernel(
         pick_pair(0, 0, PB, "xa0", 1)
         h_slice(3, lo + hi)
         late_loads()
-        h_slice(4, lo + hi)
-        bf = round_wb(0, V, "wb_bf", 1)
-        pick_pair(2, 0, PB, "xa2", 1)
-        wb_q.append(quantise(bf[:], BANK, "wbq0"))
-        sums_left = [(s, i) for s in (0, 2) for i in range(4)][:-1]
-        for s in (5, 6):
+        sums_left = [(s, i) for s in (0, 2) for i in range(len(CHUNKS))][:-1]
+
+        def woven_slice(s):
             for c in range(S_CHUNKS):
                 h_chunk(s, c, nb(lo + hi))
-                if c > 0:
+                if c % 2 == 1:
                     turn(*sums_left.pop(0), nb(lo + hi))
+
+        woven_slice(4)
+        bf = round_wb(0, [(V, 0, N)], "wb_bf")
+        pick_pair(2, 0, PB, "xa2", 1)
+        wb_q.append(quantise(bf[:], BANK, "wbq0"))
+        woven_slice(5)
+        woven_slice(6)
         for c in range(S_CHUNKS):
             h_chunk(7, c, hi[c])
             if c == 1:
                 turn(*sums_left.pop(0), lo[0])
-        turn_back(0, 0, lo[1])
+            if c == 2:
+                back(0, 0, lo[1])
         turn_back(0, 1, lo[2])
         add_turned(2, 3, lo[3])
         front = ring.tile([P, PACK, HALF], F32, name="x_front", tag="big", bufs=1, align_bytes=64)
@@ -404,22 +410,18 @@ def tile_list_clone_audit_kernel(
             pick(7, m, w, x[:, 0, :])
             return x
 
-        for e in range(2):
+        for e in range(3):
             pick(4 + e, HALF, HALF, rear[:, e, :])
             pick(4 + e, 0, HALF, front[:, e, :])
-        pick(6, HALF, CHUNK + P, rear[:, 2, 0 : CHUNK + P])
-        pick(6, 0, HALF, front[:, 2, :])
-        add_own(rear[:, :, CHUNK : CHUNK + P], 0, 3, *PARTS[3])
-        add_own(rear[:, 0:2, CHUNK + P : HALF], 0, 2, *PARTS[4])
-        copy_back(0, 0)
+        add_own(rear[:, :, CHUNK:HALF], 0, 3, HALF + CHUNK, CHUNK)
         round_turned(2, 3)
         copy_back(0, 1)
-        bf = round_wb(1, A, "xa2", 1)
+        bf = round_wb(1, [(A, 0, N)], "xa2")
         turn_back(0, 2, lo[0])
         turn_back(0, 3, lo[3])
+        gap_codes(0, 0)
         for i in range(2):
             pick(7, i * CHUNK, CHUNK, front[:, 3, i * CHUNK : (i + 1) * CHUNK])
-        gap_codes(0, 0)
         first = ring.tile([P, PACK, CHUNK], F32, name="gap_first", tag="xa0", bufs=1, align_bytes=64)
         nc.vector.tensor_tensor(first[:], front[:, :, 0:CHUNK], gap[1][:, :, 0:CHUNK], ALU.add)
         gap_codes(0, 1)
@@ -453,11 +455,12 @@ def tile_list_clone_audit_kernel(
         products(1, 2, hi)
         read_b(1)
         finish(1, [0, 1])
-        pick_pair(6, *PARTS[4], "b_sb1_0", 1)
+        x = pick_last(4, "b_sb1_0")
         round_gap(1, 3, "z1_3")
+        finish(1, [2])
+        add_own(x[:], 3, 1, *PARTS[4])
         gap_codes(1, 3)
-        add_pair(6, 4, None)
-        finish(1, [2, 3])
+        finish(1, [3])
         products(0, 3, [lo[1], lo[2]])
         products(1, 3, [lo[1], lo[2]])
         last = [lo[0], lo[3], hi[0], hi[1]]

@@ -291,7 +291,7 @@ def tile_list_clone_audit_kernel(
 
         def read_b(i, tiles=range(N_TILES)):
             for j in tiles:
-                b_sb[(i, j)] = ring.tile([P, PARTS[i][1]], F32, name="b_sb%d_%d" % (i, j), tag="z0_%d" % (i // 4) if i in (2, 4) and j == 2 else "b_sb%d_%d" % (i % 2, j), bufs=1, align_bytes=64)
+                b_sb[(i, j)] = ring.tile([P, PARTS[i][1]], F32, name="b_sb%d_%d" % (i, j), tag="z0_%d" % (i // 4) if i in (2, 4) and j == 3 else "b_sb%d_%d" % (i % 2, j), bufs=1, align_bytes=64)
                 nc.scalar.activation(b_sb[(i, j)][:], accs[(i, j)][:, 1, :], ACT.Identity, bias=wa[2][:, j : j + 1])
 
         a_sb = {}
@@ -406,14 +406,23 @@ def tile_list_clone_audit_kernel(
 
         def pick_last(i, tag):
             m, w = PARTS[i]
-            x = ring.tile([P, 1, w], F32, name="x_last%d" % i, tag=tag, bufs=1, align_bytes=64)
-            pick(7, m, w, x[:, 0, :])
+            x = ring.tile([P, w], F32, name="x_last%d" % i, tag=tag, bufs=1, align_bytes=64)
+            pick(7, m, w, x[:])
             return x
+
+        def add_rear(i, tag):
+            m, w = PARTS[i]
+            d = ring.tile([P, PACK, w], F32, name="gap_late%d" % i, tag=tag, bufs=1, align_bytes=64)
+            nc.gpsimd.tensor_tensor(d[:, 0:3, :], rear[:, :, m - HALF : m - HALF + w], gap[1][:, 0:3, m : m + w], ALU.add)
+            return d
+
+        def add_last(i, x, d):
+            m, w = PARTS[i]
+            nc.vector.tensor_tensor(d[:, 3, :], x[:], gap[1][:, 3, m : m + w], ALU.add)
 
         for e in range(3):
             pick(4 + e, HALF, HALF, rear[:, e, :])
             pick(4 + e, 0, HALF, front[:, e, :])
-        add_own(rear[:, :, CHUNK:HALF], 0, 3, HALF + CHUNK, CHUNK)
         round_turned(2, 3)
         copy_back(0, 1)
         bf = round_wb(1, [(A, 0, N)], "xa2")
@@ -443,30 +452,30 @@ def tile_list_clone_audit_kernel(
         nc.vector.tensor_tensor(third[:, 3, :], third[:, 3, :], gap[1][:, 3, HALF : HALF + CHUNK], ALU.add)
         gap_codes(1, 1)
         gap_codes(0, 2)
+        fourth = add_rear(3, "z0_2")
         products(1, 1, second)
         read_b(0)
         round_gap(1, 2, "z1_2", third[:])
         finish(0)
         products(0, 2, hi)
-        x = pick_last(3, "b_sb0_1")
-        gap_codes(0, 3, "b_sb0_2")
-        add_own(x[:], 3, 1, *PARTS[3])
+        x = pick_last(3, "b_sb0_2")
+        gap_codes(0, 3, "b_sb0_3")
+        add_last(3, x, fourth)
         gap_codes(1, 2)
+        fifth = add_rear(4, "z1_2")
         products(1, 2, hi)
         read_b(1)
-        finish(1, [0, 1])
-        x = pick_last(4, "b_sb1_0")
-        round_gap(1, 3, "z1_3")
-        finish(1, [2])
-        add_own(x[:], 3, 1, *PARTS[4])
+        finish(1)
+        x = pick_last(4, "b_sb1_2")
+        round_gap(1, 3, "z1_3", fourth[:])
         gap_codes(1, 3)
-        finish(1, [3])
+        add_last(4, x, fifth)
         products(0, 3, [lo[1], lo[2]])
         products(1, 3, [lo[1], lo[2]])
         last = [lo[0], lo[3], hi[0], hi[1]]
         products(0, 4, last, [0, 1])
         read_b(2, [0, 1])
-        round_gap(1, 4, "z1_4")
+        round_gap(1, 4, "z1_4", fifth[:])
         read_b(2, [2, 3])
         finish(2, [0, 1])
         gap_codes(1, 4)

@@ -3,8 +3,8 @@ from contextlib import ExitStack
 import concourse.mybir as mybir
 from concourse.masks import make_identity
 
-K, T, S, PB, H, N = 512, 4096, 2048, 1024, 1024, 512
-FLOPS = 2 * K * H * S + 2 * 2 * H * N * PB
+K, T, S, M, H, N = 512, 4096, 2048, 1024, 1024, 512
+FLOPS = 2 * K * H * S + 2 * 2 * H * N * M
 
 F32 = mybir.dt.float32
 BF16 = mybir.dt.bfloat16
@@ -19,16 +19,21 @@ ACT = mybir.ActivationFunctionType
 
 P = 128
 PACK = 4
+RUN = 4
+GROUP = 16
 BANK = 512
-PASSES = H // (P * PACK)
+K_PASS = P * PACK
+PASSES = H // K_PASS
 N_TILES = N // P
-S_CHUNKS = S // BANK
-CHUNK = 256
-HALF = 512
-CHUNKS = [(m, CHUNK) for m in range(0, PB, CHUNK)]
-HBUFS = 7
-PARTS = CHUNKS[:3] + [(768, P), (896, P)]
-STAGE = ["w1_raw0", "big", "xc", "vw0", "wb_bf"]
+H_PIECES = S // BANK
+H_BUFS = 7
+LAST = 2 * PACK - 1
+WORDS_AHEAD = 3
+CHUNK = BANK // 2
+CHUNKS = [(m, CHUNK) for m in range(0, M, CHUNK)]
+PARTS = CHUNKS[:-1] + [(M - 2 * P, P), (M - P, P)]
+LOW, HIGH = [0, 1, 2, 3], [4, 5, 6, 7]
+STAGE_TAGS = ["w1_raw0", "x_pair2", "stage2", "words0", "wb_bf"]
 
 
 def tile_list_clone_audit_kernel(
@@ -43,58 +48,79 @@ def tile_list_clone_audit_kernel(
         def bank(n, shape, name):
             return psum.tile([P] + shape, F32, name=name, tag="bank%d" % n, bufs=1)
 
-        idx = keep.tile([P, S // 16], U16, name="idx")
+        def buffer(shape, dtype, name, tag):
+            return ring.tile([P] + shape, dtype, name=name, tag=tag, bufs=1, align_bytes=64)
+
+        def by_word(rows):
+            return rows.rearrange("(p t) c -> p t c", t=PACK)
+
+        idx = keep.tile([P, S // GROUP], U16, name="idx")
         nc.sync.dma_start(idx[:], offs)
 
-        def load_weight(src, name):
-            raw = ring.tile([P, PACK, BANK], F32, name=name, tag=name, bufs=1, align_bytes=64)
-            nc.sync.dma_start(raw[:], src.rearrange("(p j) c -> p j c", j=PACK))
-            return raw
-
-        tab_plane = ring.tile([P, T], U8, name="tab_plane", tag="late", bufs=1)
+        tab_rows = ring.tile([P, T], U8, name="tab_rows", tag="inputs", bufs=1)
+        nc.vector.memset(tab_rows[:].bitcast(I32), 0)
+        idx2 = keep.tile([P, M // GROUP], U16, name="idx2")
+        nc.sync.dma_start(idx2[:], offs2)
+        ba_sb = keep.tile([P, N_TILES], F32, name="ba_sb")
+        with nc.allow_non_contiguous_dma(reason="one bias value a partition"):
+            nc.sync.dma_start(ba_sb[:], ba.rearrange("(j p) -> p j", p=P))
+        nc.sync.dma_start(tab_rows[0:P:8, :].bitcast(I32), tab_scales[0].bitcast(I32))
+        v_plane = keep.tile([P, S], U8, name="v_plane", align_bytes=64)
+        nc.vector.memset(v_plane[:].bitcast(I32), 0)
         ident = keep.tile([P, P], F32, name="ident")
         nc.vector.memset(ident[:], 0.0)
         make_identity(nc, ident[:], nomemset=True)
-        for first in range(2):
-            nc.sync.dma_start(tab_plane[first:32:2, :].bitcast(I32), tab_scales[0].bitcast(I32))
-        nc.vector.memset(tab_plane[64:P, :].bitcast(I32), 0)
-        nc.vector.memset(tab_plane[32:64, :].bitcast(I32), 0)
-        v_plane = keep.tile([P, S], U8, name="v_plane", align_bytes=64)
-        nc.vector.memset(v_plane[:].bitcast(I32), 0)
 
-        tab_w = ring.tile([P, T], I32, name="tab_w", tag="big", bufs=1, align_bytes=64)
+        tab_w = buffer([T], I32, "tab_w", "table")
         nc.sync.dma_start(tab_w[:], tab_words[0].rearrange("p t i -> p (t i)").bitcast(I32))
-        w1_raw = [load_weight(w1[:, 0:BANK], "w1_raw0")[:]]
-        idx2 = keep.tile([P, PB // 16], U16, name="idx2")
-        nc.sync.dma_start(idx2[:], offs2)
-        picked = ring.tile([P, S], U8, name="picked", tag="wb_bf", bufs=1, align_bytes=64)
-        nc.vector.tensor_copy(picked[:], tab_plane[:].indirect(idx[:]))
+        w1_first = buffer([PACK, K_PASS], F32, "w1_first", "w1_raw0")
+        nc.sync.dma_start(w1_first[:], by_word(w1[:, 0:K_PASS]))
+
+        picked = buffer([S], U8, "picked", "wb_bf")
+        nc.vector.tensor_copy(picked[:], tab_rows[:].indirect(idx[:]))
         for r in range(4):
-            nc.sync.dma_start(v_plane[r:P:32, :].bitcast(I32), picked[2 * r : 32 : 8, :].bitcast(I32))
+            nc.sync.dma_start(v_plane[r:P:32, :].bitcast(I32), picked[8 * r : P : 32, :].bitcast(I32))
 
-        own_v = own.rearrange("(b p t) m -> b p t m", p=P, t=PACK)
-        late = ring.tile([P, 3 * PACK * PB + PACK * BANK + PB], F32, name="late", tag="late", bufs=1)
-        w1_at = 3 * PACK * PB
-        w1_raw.append(late[:, w1_at : w1_at + PACK * BANK].rearrange("p (j c) -> p j c", j=PACK))
-        nc.sync.dma_start(w1_raw[1], w1[:, BANK : 2 * BANK].rearrange("(p j) c -> p j c", j=PACK))
-        wgt_sb = late[:, w1_at + PACK * BANK : w1_at + PACK * BANK + PB]
+        wb_at = PASSES * PACK * M
+        w1_at = wb_at + PASSES * PACK * N
+        wgt_at = w1_at + PACK * K_PASS
+        inputs = ring.tile([P, wgt_at + M], F32, name="inputs", tag="inputs", bufs=1)
+
+        def region(first, width):
+            return inputs[:, first : first + PACK * width].rearrange("p (t c) -> p t c", t=PACK)
+
+        w1_raw = [w1_first[:], region(w1_at, K_PASS)]
+        nc.sync.dma_start(w1_raw[1], by_word(w1[:, K_PASS : 2 * K_PASS]))
+        wgt_sb = inputs[:, wgt_at : wgt_at + M]
         nc.sync.dma_start(wgt_sb, wgt)
-        gap = [late[:, b * PACK * PB : (b + 1) * PACK * PB].rearrange("p (t m) -> p t m", t=PACK) for b in range(PASSES)]
-        wb_at = 2 * PACK * PB
-        wb_raw = [
-            late[:, wb_at + b * PACK * N : wb_at + (b + 1) * PACK * N].rearrange("p (j c) -> p j c", j=PACK)
-            for b in range(PASSES)
-        ]
+        own_sb = [region(g * PACK * M, M) for g in range(PASSES)]
+        wb_raw = [region(wb_at + g * PACK * N, N) for g in range(PASSES)]
+        own_v = own.rearrange("(g p t) m -> g p t m", p=P, t=PACK)
         for u in range(2):
-            nc.sync.dma_start(gap[0][:, 2 * u : 2 * u + 2, :], own_v[0, :, 2 * u : 2 * u + 2, :])
-            nc.sync.dma_start(wb_raw[u], wb[u * BANK : (u + 1) * BANK, :].rearrange("(p j) c -> p j c", j=PACK))
+            nc.sync.dma_start(own_sb[0][:, 2 * u : 2 * u + 2, :], own_v[0, :, 2 * u : 2 * u + 2, :])
+            nc.sync.dma_start(wb_raw[u], by_word(wb[u * K_PASS : (u + 1) * K_PASS, :]))
         for u in range(2):
-            nc.sync.dma_start(gap[1][:, 2 * u : 2 * u + 2, :], own_v[1, :, 2 * u : 2 * u + 2, :])
+            nc.sync.dma_start(own_sb[1][:, 2 * u : 2 * u + 2, :], own_v[1, :, 2 * u : 2 * u + 2, :])
 
-        def quantise(grouped, width, name, tag=None):
-            codes = ring.tile([P, width], U32, name=name + "_codes", tag=tag or name + "_codes", bufs=1, align_bytes=64)
-            plane = ring.tile([P, width], U8, name=name + "_plane", tag=name + "_plane", bufs=1, align_bytes=64)
-            nc.vector.quantize_mx(out=codes[:].bitcast(FP8X4), scales=plane[:], in_=grouped)
+        def load_wa_and_bb():
+            words = buffer([PASSES, 2 * N], U8, "wa_w", "w1q0_codes")
+            plane = buffer([PASSES, N], U8, "wa_plane", "w1q2_plane")
+            bias = buffer([N_TILES], F32, "bb_sb", "w1q0_plane")
+            nc.sync.dma_start(words[:].bitcast(I32), wa_words.rearrange("g p c -> p g c").bitcast(I32))
+            nc.gpsimd.memset(plane[:].bitcast(I32), 0)
+            for q in range(4):
+                nc.sync.dma_start(
+                    plane[32 * q : 32 * q + 4, :, :].bitcast(I32),
+                    wa_scales[:, 4 * q : 4 * q + 4, :].rearrange("g r c -> r g c").bitcast(I32),
+                )
+            with nc.allow_non_contiguous_dma(reason="one bias value a partition"):
+                nc.sync.dma_start(bias[:], bb.rearrange("(j p) -> p j", p=P))
+            return words, plane, bias
+
+        def quantise(rounded, width, name, codes_tag=None):
+            codes = buffer([width], U32, name + "_codes", codes_tag or name + "_codes")
+            plane = buffer([width], U8, name + "_plane", name + "_plane")
+            nc.vector.quantize_mx(out=codes[:].bitcast(FP8X4), scales=plane[:], in_=rounded)
             return codes, plane
 
         def negate_on_scalar(dst, src):
@@ -103,48 +129,42 @@ def tile_list_clone_audit_kernel(
         def negate_on_vector(dst, src):
             nc.vector.tensor_scalar(dst, src, -1.0, None, ALU.mult)
 
-        def round_w1(s0, negate, grouped):
-            b, t0 = divmod(s0, PACK)
+        def round_w1(s, negate, rounded):
+            g, t = divmod(s, PACK)
             negate(
-                grouped.rearrange("p (t m j) -> p m j t", t=2, j=PACK),
-                w1_raw[b].rearrange("p j (m t) -> p m j t", t=PACK)[:, :, :, t0 : t0 + 2],
+                rounded.rearrange("p (e c a) -> p c a e", e=2, a=PACK),
+                w1_raw[g].rearrange("p a (c t) -> p c a t", t=PACK)[:, :, :, t : t + 2],
             )
-
-        def w1_tile(name, count, tag):
-            tile = ring.tile([P, count, 2 * BANK], BF16, name=name, tag=tag, bufs=1, align_bytes=64)
-            return [tile[:, n, :] for n in range(count)]
 
         w1_q = {}
 
-        def w1_codes(s0, grouped):
-            codes, plane = quantise(grouped, 2 * P, "w1q%d" % s0)
-            for t in range(2):
-                w1_q[s0 + t] = (codes[:, t * P : (t + 1) * P], plane[:, t * P : (t + 1) * P])
+        def quantise_w1(s, rounded):
+            codes, plane = quantise(rounded, 2 * P, "w1q%d" % s)
+            for e in range(2):
+                w1_q[s + e] = (codes[:, e * P : (e + 1) * P], plane[:, e * P : (e + 1) * P])
 
-        def round_wb(b, shares, tag):
-            grouped = ring.tile([P, PACK * BANK], BF16, name="wb_bf%d" % b, tag=tag, bufs=1, align_bytes=64)
-            for copy, first, last in shares:
-                copy(
-                    grouped[:, PACK * first : PACK * last].rearrange("p (c i j) -> p c j i", i=4, j=PACK),
-                    wb_raw[b][:, :, first:last].rearrange("p j (c i) -> p c j i", i=4),
-                )
-            return grouped
+        def round_wb(g, copy, tag):
+            rounded = buffer([PACK * N], BF16, "wb_bf%d" % g, tag)
+            copy(
+                rounded[:].rearrange("p (c d t) -> p c t d", d=RUN, t=PACK),
+                wb_raw[g].rearrange("p t (c d) -> p c t d", d=RUN),
+            )
+            return rounded
 
         v_words = {}
 
-        def gather_words(c0, count, tag):
-            words = ring.tile([P, count * BANK], U32, name="v_words%d" % c0, tag=tag, bufs=1, align_bytes=64)
-            nc.vector.tensor_copy(
-                words[:], tab_w[:].bitcast(U32).indirect(idx[:, c0 * BANK // 16 : (c0 + count) * BANK // 16])
-            )
+        def gather_words(first, count, tag):
+            words = buffer([count * BANK], U32, "v_words%d" % first, tag)
+            entries = idx[:, first * BANK // GROUP : (first + count) * BANK // GROUP]
+            nc.vector.tensor_copy(words[:], tab_w[:].bitcast(U32).indirect(entries))
             for c in range(count):
-                v_words[c0 + c] = words[:, c * BANK : (c + 1) * BANK]
+                v_words[first + c] = words[:, c * BANK : (c + 1) * BANK]
 
         h = {}
 
-        def h_chunk(s, c, n):
+        def h_piece(s, c, n):
             if s not in h:
-                h[s] = ring.tile([P, S], F32, name="h%d" % s, tag="h", bufs=HBUFS)
+                h[s] = ring.tile([P, S], F32, name="h%d" % s, tag="h", bufs=H_BUFS)
             acc = bank(n, [BANK], "h_acc")
             nc.tensor.matmul_mx(
                 out=acc[:],
@@ -157,334 +177,266 @@ def tile_list_clone_audit_kernel(
             )
             nc.scalar.copy(h[s][:, c * BANK : (c + 1) * BANK], acc[:])
 
-        xs = {}
+        def pick(s, m, width, dst):
+            entries = idx2[:, m // GROUP : (m + width) // GROUP]
+            nc.vector.tensor_tensor(dst, h[s][:].indirect(entries), wgt_sb[:, m : m + width], ALU.mult)
 
-        def pick_pair(s, m0, width, tag, bufs):
-            x = ring.tile([P, 2, width], F32, name="x%d_%d" % (s, m0), tag=tag, bufs=bufs, align_bytes=64)
+        x_pair, turned_sum, turned_z, returned = {}, {}, {}, {}
+        z_bf, z_q = {}, {}
+
+        def pick_pair(u):
+            x_pair[u] = buffer([2, M], F32, "x_pair%d" % u, "x_pair%d" % (2 * u))
             for e in range(2):
-                nc.vector.tensor_tensor(
-                    x[:, e, :],
-                    h[s + e][:].indirect(idx2[:, m0 // 16 : (m0 + width) // 16]),
-                    wgt_sb[:, m0 : m0 + width],
-                    ALU.mult,
-                )
-            for i, (m, w) in enumerate(PARTS if s == 6 else CHUNKS):
-                if m0 <= m < m0 + width:
-                    xs[(s, i)] = x[:, :, m - m0 : m - m0 + w]
+                pick(2 * u + e, 0, M, x_pair[u][:, e, :])
 
-        def pick(s, m0, width, dst):
-            nc.vector.tensor_tensor(
-                dst, h[s][:].indirect(idx2[:, m0 // 16 : (m0 + width) // 16]), wgt_sb[:, m0 : m0 + width], ALU.mult
-            )
-
-        def add_own(x, t0, nt, m0, width):
-            d = gap[1][:, t0 : t0 + nt, m0 : m0 + width]
-            nc.vector.tensor_tensor(d, x, d, ALU.add)
-
-        zt = {}
-        z_bf = {}
-        z_q = {}
-
-        sums = {}
-
-        def add_turned(s, i, n):
-            b, u = s // PACK, s % PACK // 2
-            acc = bank(n, [2, 2, P], "gap_t%d_%d" % (s, i))
-            sums[(s, i)] = acc
-            places = [(j, e) for j in range(2) for e in range(2)]
-            for k, (j, e) in enumerate(places):
-                c0 = i * CHUNK + j * P
+        def add_turned(u, i, n):
+            acc = bank(n, [2, 2, P], "sum%d_%d" % (u, i))
+            turned_sum[(u, i)] = acc
+            places = [(f, e, i * CHUNK + f * P) for f in range(2) for e in range(2)]
+            for no, (f, e, m) in enumerate(places):
                 nc.tensor.matmul(
-                    acc[:, j, e, :], gap[b][:, 2 * u + e, c0 : c0 + P], ident[:],
-                    start=(k == 0), stop=False, is_transpose=True,
+                    acc[:, f, e, :], own_sb[0][:, 2 * u + e, m : m + P], ident[:],
+                    start=(no == 0), stop=False, is_transpose=True,
                 )
-            for k, (j, e) in enumerate(places):
+            for no, (f, e, m) in enumerate(places):
                 nc.tensor.matmul(
-                    acc[:, j, e, :], xs[(s, i)][:, e, j * P : (j + 1) * P], ident[:],
-                    start=False, stop=(k == 3), is_transpose=True,
+                    acc[:, f, e, :], x_pair[u][:, e, m : m + P], ident[:],
+                    start=False, stop=(no == len(places) - 1), is_transpose=True,
                 )
 
-        def round_turned(s, i, tag=None):
-            b, u = s // PACK, s % PACK // 2
-            if (b, i) not in zt:
-                zt[(b, i)] = ring.tile([P, 2, 2, 2 * P], BF16, name="zt%d_%d" % (b, i), tag=tag or "zt%d_%d" % (b, i), bufs=1, align_bytes=64)
+        def round_turned(u, i):
+            if i not in turned_z:
+                turned_z[i] = buffer([2, 2, 2 * P], BF16, "zt%d" % i, "zt%d" % i)
             nc.scalar.activation(
-                zt[(b, i)][:, :, u, :].rearrange("m j (p e) -> m j p e", e=2),
-                sums[(s, i)][:].rearrange("m j e p -> m j p e"),
+                turned_z[i][:, :, u, :].rearrange("m f (p e) -> m f p e", e=2),
+                turned_sum[(u, i)][:].rearrange("m f e p -> m f p e"),
                 ACT.Abs,
             )
 
-        def new_z(b, i, tag):
-            z_bf[(b, i)] = ring.tile([P, PACK * (PARTS if b else CHUNKS)[i][1]], BF16, name="z_bf%d_%d" % (b, i), tag=tag, bufs=1, align_bytes=64)
-            return z_bf[(b, i)]
-
-        backs = {}
-
-        def turn_back(b, i, n):
-            acc = bank(n, [2, 2, P], "z_t%d_%d" % (b, i))
-            backs[(b, i)] = acc
-            for j in range(2):
+        def turn_back(i, n):
+            returned[i] = bank(n, [2, 2, P], "back%d" % i)
+            for f in range(2):
                 for u in range(2):
-                    nc.tensor.transpose(acc[:, j, u, :], zt[(b, i)][:, j, u, :].bitcast(F32), ident[:])
+                    nc.tensor.transpose(returned[i][:, f, u, :], turned_z[i][:, f, u, :].bitcast(F32), ident[:])
 
-        def copy_back(b, i):
+        def copy_back(i):
+            z_bf[(0, i)] = buffer([PACK * CHUNK], BF16, "z_bf0_%d" % i, "z0_%d" % i)
             nc.scalar.copy(
-                new_z(b, i, "z%d_%d" % (b, i))[:].bitcast(F32).rearrange("p (j m u) -> p j m u", j=2, u=2),
-                backs[(b, i)][:].rearrange("p j u m -> p j m u"),
+                z_bf[(0, i)][:].bitcast(F32).rearrange("p (f m u) -> p f m u", f=2, u=2),
+                returned[i][:].rearrange("p f u m -> p f m u"),
             )
 
-        def add_pair(s, i, tag):
-            t0 = s % PACK
-            m, w = (PARTS if s == 6 else CHUNKS)[i]
-            d = gap[1][:, t0 : t0 + 2, m : m + w]
-            nc.vector.tensor_tensor(d, xs[(s, i)], d, ALU.add)
+        def add_own(engine, dst, x, t0, t1, i):
+            m, w = PARTS[i]
+            engine.tensor_tensor(dst, x, own_sb[1][:, t0:t1, m : m + w], ALU.add)
 
-        def round_gap(b, i, tag, summed=None):
-            if summed is None:
-                summed = gap[1][:, :, PARTS[i][0] : PARTS[i][0] + PARTS[i][1]]
+        def round_gap(i, gap):
+            z_bf[(1, i)] = buffer([PACK * PARTS[i][1]], BF16, "z_bf1_%d" % i, "z1_%d" % i)
             nc.scalar.activation(
-                new_z(b, i, tag)[:].rearrange("p (c i t) -> p c t i", i=4, t=PACK),
-                summed.rearrange("p t (c i) -> p c t i", i=4),
+                z_bf[(1, i)][:].rearrange("p (c d t) -> p c t d", d=RUN, t=PACK),
+                gap.rearrange("p t (c d) -> p c t d", d=RUN),
                 ACT.Abs,
             )
 
-        def gap_codes(b, i, tag=None):
-            z_q[(b, i)] = quantise(z_bf[(b, i)][:], (PARTS if b else CHUNKS)[i][1], "zq%d_%d" % (b, i), tag)
+        def quantise_z(g, i, codes_tag=None):
+            z_q[(g, i)] = quantise(z_bf[(g, i)][:], (PARTS if g else CHUNKS)[i][1], "zq%d_%d" % (g, i), codes_tag)
 
-        accs = {}
+        wb_q, sums_ab, b_sb, staged = {}, {}, {}, {}
+        out_v = out.rearrange("(j p) m -> p j m", p=P)
 
-        def products(b, i, banks, tiles=range(N_TILES)):
+        def products(g, i, banks, tiles=range(N_TILES)):
             m, w = PARTS[i]
-            codes, plane = z_q[(b, i if b else m // CHUNK)]
-            z0 = 0 if b else m % CHUNK
+            codes, plane = z_q[(g, i if g else m // CHUNK)]
+            z0 = 0 if g else m % CHUNK
             per_bank = N_TILES // len(banks)
             for j in tiles:
-                if b == 0 and j % per_bank == 0:
+                opens = g == 0 and j % per_bank == 0
+                if opens:
                     acc = bank(banks[j // per_bank], [per_bank, 2, w], "acc%d_%d" % (i, j))
                     for jj in range(per_bank):
-                        accs[(i, j + jj)] = acc[:, jj, :, :]
-                both = accs[(i, j)]
+                        sums_ab[(i, j + jj)] = acc[:, jj, :, :]
                 nc.tensor.matmul_mx(
-                    out=both[:, 1, :],
-                    lhsT=wb_q[b][0][:, j * P : (j + 1) * P].bitcast(FP8X4),
-                    lhsT_scale=wb_q[b][1][:, j * P : (j + 1) * P],
+                    out=sums_ab[(i, j)][:, 1, :],
+                    lhsT=wb_q[g][0][:, j * P : (j + 1) * P].bitcast(FP8X4),
+                    lhsT_scale=wb_q[g][1][:, j * P : (j + 1) * P],
                     rhs=codes[:, z0 : z0 + w].bitcast(FP8X4),
                     rhs_scale=plane[:, z0 : z0 + w],
-                    start=(b == 0 and j % per_bank == 0),
+                    start=opens,
                     stop=False,
                 )
-                for c0 in range(0, w, P):
+                for c in range(0, w, P):
                     nc.tensor.matmul_mx(
-                        out=both[:, 0, c0 : c0 + P],
-                        lhsT=wa[0][:, b, 2 * j * P : 2 * (j + 1) * P].bitcast(FP4X4),
-                        lhsT_scale=wa[1][:, b, j * P : (j + 1) * P],
-                        rhs=codes[:, z0 + c0 : z0 + c0 + P].bitcast(FP8X4),
-                        rhs_scale=plane[:, z0 + c0 : z0 + c0 + P],
+                        out=sums_ab[(i, j)][:, 0, c : c + P],
+                        lhsT=wa_w[:, g, 2 * j * P : 2 * (j + 1) * P].bitcast(FP4X4),
+                        lhsT_scale=wa_plane[:, g, j * P : (j + 1) * P],
+                        rhs=codes[:, z0 + c : z0 + c + P].bitcast(FP8X4),
+                        rhs_scale=plane[:, z0 + c : z0 + c + P],
                         start=False,
-                        stop=(b == PASSES - 1 and c0 + P == w and j % per_bank == per_bank - 1),
+                        stop=(g == PASSES - 1 and c + P == w and j % per_bank == per_bank - 1),
                     )
 
-        out_v = out.rearrange("(j p) m -> p j m", p=P)
-        staged = {}
-
-        b_sb = {}
+        def b_tag(i, j):
+            if i > 0 and i % 2 == 0 and j == N_TILES - 1:
+                return "z0_%d" % (i // 2 - 1)
+            return "b%d_%d" % (i % 2, j)
 
         def read_b(i, tiles=range(N_TILES)):
             for j in tiles:
-                b_sb[(i, j)] = ring.tile([P, PARTS[i][1]], F32, name="b_sb%d_%d" % (i, j), tag="z0_%d" % (i // 4) if i in (2, 4) and j == 3 else "b_sb%d_%d" % (i % 2, j), bufs=1, align_bytes=64)
-                nc.scalar.activation(b_sb[(i, j)][:], accs[(i, j)][:, 1, :], ACT.Identity, bias=wa[2][:, j : j + 1])
-
-        a_sb = {}
-
-        def read_a(i):
-            for j in range(N_TILES):
-                a_sb[(i, j)] = ring.tile([P, PARTS[i][1]], F32, name="a_sb%d_%d" % (i, j), tag="a_sb", bufs=4)
-                nc.scalar.copy(a_sb[(i, j)][:], accs[(i, j)][:, 0, :])
-                read_b(i, [j])
+                b_sb[(i, j)] = buffer([PARTS[i][1]], F32, "b_sb%d_%d" % (i, j), b_tag(i, j))
+                nc.scalar.activation(b_sb[(i, j)][:], sums_ab[(i, j)][:, 1, :], ACT.Identity, bias=bb_sb[:, j : j + 1])
 
         def finish(i, tiles=range(N_TILES)):
             m, w = PARTS[i]
             for j in tiles:
                 if j == 0:
-                    staged[i] = ring.tile([P, N_TILES, w], F32, name="staged%d" % i, tag=STAGE[i], bufs=1, align_bytes=64)
+                    staged[i] = buffer([N_TILES, w], F32, "staged%d" % i, STAGE_TAGS[i])
                 nc.vector.scalar_tensor_tensor(
-                    staged[i][:, j, :], a_sb[(i, j)][:] if (i, j) in a_sb else accs[(i, j)][:, 0, :], wa[3][:, j : j + 1], b_sb[(i, j)][:], ALU.add, ALU.mult
+                    staged[i][:, j, :], sums_ab[(i, j)][:, 0, :], ba_sb[:, j : j + 1], b_sb[(i, j)][:], ALU.add, ALU.mult
                 )
-                group = 1 if i == len(PARTS) - 1 and j >= 2 else 2
-                if j % group == group - 1:
-                    nc.sync.dma_start(out_v[:, j + 1 - group : j + 1, m : m + w], staged[i][:, j + 1 - group : j + 1, :])
+                stored = 1 if i == len(PARTS) - 1 and j >= 2 else 2
+                if j % stored == stored - 1:
+                    nc.sync.dma_start(out_v[:, j + 1 - stored : j + 1, m : m + w], staged[i][:, j + 1 - stored : j + 1, :])
 
-        def late_loads():
-            wa.append(ring.tile([P, PASSES, 2 * N], U8, name="wa_w", tag="w1q0_codes", bufs=1, align_bytes=64))
-            wa.append(ring.tile([P, PASSES, N], U8, name="wa_plane", tag="w1q2_plane", bufs=1, align_bytes=64))
-            wa.append(ring.tile([P, N_TILES], F32, name="bb_sb", tag="w1q0_plane", bufs=1, align_bytes=64))
-            wa.append(ring.tile([P, N_TILES], F32, name="ba_sb", tag="w1q2_codes", bufs=1, align_bytes=64))
-            wa_w, wa_plane, bias, bias_a = wa
-            nc.sync.dma_start(wa_w[:].bitcast(I32), wa_words.rearrange("a p c -> p a c").bitcast(I32))
-            nc.gpsimd.memset(wa_plane[:].bitcast(I32), 0)
-            for q in range(4):
-                nc.sync.dma_start(
-                    wa_plane[32 * q : 32 * q + 4, :, :].bitcast(I32),
-                    wa_scales[:, 4 * q : 4 * q + 4, :].rearrange("a r c -> r a c").bitcast(I32),
-                )
-            with nc.allow_non_contiguous_dma(reason="one bias value a partition"):
-                nc.sync.dma_start(bias[:], bb.rearrange("(j p) -> p j", p=P))
-                nc.sync.dma_start(bias_a[:], ba.rearrange("(j p) -> p j", p=P))
+        gather_words(0, WORDS_AHEAD, "words0")
+        w1_bf0 = buffer([1, 2 * K_PASS], BF16, "w1_bf0", "words1")
+        w1_bf2 = buffer([1, 2 * K_PASS], BF16, "w1_bf2", "w1_bf2")
+        round_w1(0, negate_on_scalar, w1_bf0[:, 0, :])
+        round_w1(2, negate_on_scalar, w1_bf2[:, 0, :])
+        quantise_w1(0, w1_bf0[:, 0, :])
+        gather_words(WORDS_AHEAD, H_PIECES - WORDS_AHEAD, "words1")
+        quantise_w1(2, w1_bf2[:, 0, :])
+        w1_bf4 = buffer([2, 2 * K_PASS], BF16, "w1_bf4", "w1_raw0")
+        for e in range(2):
+            round_w1(PACK + 2 * e, negate_on_vector, w1_bf4[:, e, :])
+        for e in range(2):
+            quantise_w1(PACK + 2 * e, w1_bf4[:, e, :])
 
-        wa = []
-        V, A = nc.vector.tensor_copy, nc.scalar.copy
-        wb_q = []
+        banks_taken = []
 
-        gather_words(0, 3, "vw0")
-        (bf01,) = w1_tile("w1_bf01", 1, "vw1")
-        (bf23,) = w1_tile("w1_bf23", 1, "w1b")
-        round_w1(0, negate_on_scalar, bf01)
-        round_w1(2, negate_on_scalar, bf23)
-        w1_codes(0, bf01)
-        gather_words(3, 1, "vw1")
-        w1_codes(2, bf23)
-        bf45, bf67 = w1_tile("w1_bf47", 2, "w1_raw0")
-        round_w1(4, negate_on_vector, bf45)
-        round_w1(6, negate_on_vector, bf67)
-        w1_codes(4, bf45)
-        w1_codes(6, bf67)
-        turn_no = [0]
-        lo, hi = [0, 1, 2, 3], [4, 5, 6, 7]
+        def next_bank():
+            banks_taken.append(None)
+            return len(banks_taken) % len(LOW + HIGH)
 
-        def nb(banks):
-            turn_no[0] = turn_no[0] + 1
-            return banks[turn_no[0] % len(banks)]
+        sums_left = [(u, i) for u in range(2) for i in range(len(CHUNKS))]
 
-        def h_slice(s, banks):
-            for c in range(4):
-                h_chunk(s, c, nb(banks))
+        def next_sum(n):
+            u, i = sums_left.pop(0)
+            add_turned(u, i, n)
+            round_turned(u, i)
 
-        def both_products(i, banks):
-            for j in range(N_TILES):
-                products(0, i, banks, [j])
-                products(1, i, banks, [j])
+        def h_slice(s):
+            for c in range(H_PIECES):
+                h_piece(s, c, next_bank())
+                if s >= PACK and c % 2 == 1:
+                    next_sum(next_bank())
 
-        def turn(s, i, n):
-            add_turned(s, i, n)
-            round_turned(s, i)
-
-        def back(b, i, n):
-            turn_back(b, i, n)
-            copy_back(b, i)
-
-        h_slice(0, lo + hi)
-        h_slice(1, lo + hi)
-
-        h_slice(2, lo + hi)
-        pick_pair(0, 0, PB, "xa0", 1)
-        h_slice(3, lo + hi)
-        late_loads()
-        sums_left = [(s, i) for s in (0, 2) for i in range(len(CHUNKS))][:-1]
-
-        def woven_slice(s):
-            for c in range(S_CHUNKS):
-                h_chunk(s, c, nb(lo + hi))
-                if c % 2 == 1:
-                    turn(*sums_left.pop(0), nb(lo + hi))
-
-        woven_slice(4)
-        bf = round_wb(0, [(V, 0, N)], "wb_bf")
-        pick_pair(2, 0, PB, "xa2", 1)
-        wb_q.append(quantise(bf[:], BANK, "wbq0"))
-        woven_slice(5)
-        woven_slice(6)
-        for c in range(S_CHUNKS):
-            h_chunk(7, c, hi[c])
+        for s in range(3):
+            h_slice(s)
+        pick_pair(0)
+        h_slice(3)
+        wa_w, wa_plane, bb_sb = load_wa_and_bb()
+        h_slice(4)
+        wb_bf = round_wb(0, nc.vector.tensor_copy, "wb_bf")
+        pick_pair(1)
+        wb_q[0] = quantise(wb_bf[:], N, "wbq0")
+        h_slice(5)
+        h_slice(6)
+        for c in range(H_PIECES):
+            h_piece(LAST, c, HIGH[c])
             if c == 1:
-                turn(*sums_left.pop(0), lo[0])
-            if c == 2:
-                back(0, 0, lo[1])
-        turn_back(0, 1, lo[2])
-        add_turned(2, 3, lo[3])
-        front = ring.tile([P, PACK, HALF], F32, name="x_front", tag="big", bufs=1, align_bytes=64)
-        rear = ring.tile([P, 3, HALF], F32, name="x_rear", tag="xc", bufs=1, align_bytes=64)
+                next_sum(LOW[0])
+            if c == H_PIECES - 2:
+                turn_back(0, LOW[1])
+                copy_back(0)
+        turn_back(1, LOW[2])
+        last_sum = sums_left.pop(0)
+        add_turned(*last_sum, LOW[3])
+
+        x1 = buffer([PACK, M], F32, "x1", "table")
+        early = PACK - 1
+
+        def x1_part(i, t1):
+            m, w = PARTS[i]
+            return x1[:, 0:t1, m : m + w]
 
         def pick_last(i, tag):
-            m, w = PARTS[i]
-            x = ring.tile([P, w], F32, name="x_last%d" % i, tag=tag, bufs=1, align_bytes=64)
-            pick(7, m, w, x[:])
+            x = buffer([1, PARTS[i][1]], F32, "x_last%d" % i, tag)
+            pick(LAST, *PARTS[i], x[:, 0, :])
             return x
 
-        def add_rear(i, tag):
-            m, w = PARTS[i]
-            d = ring.tile([P, PACK, w], F32, name="gap_late%d" % i, tag=tag, bufs=1, align_bytes=64)
-            nc.gpsimd.tensor_tensor(d[:, 0:3, :], rear[:, :, m - HALF : m - HALF + w], gap[1][:, 0:3, m : m + w], ALU.add)
-            return d
+        def add_early_on_gpsimd(i, tag):
+            gap = buffer([PACK, PARTS[i][1]], F32, "gap%d" % i, tag)
+            add_own(nc.gpsimd, gap[:, 0:early, :], x1_part(i, early), 0, early, i)
+            return gap
 
-        def add_last(i, x, d):
-            m, w = PARTS[i]
-            nc.vector.tensor_tensor(d[:, 3, :], x[:], gap[1][:, 3, m : m + w], ALU.add)
+        for t in range(early):
+            pick(PACK + t, 0, M, x1[:, t, :])
+        round_turned(*last_sum)
+        copy_back(1)
+        wb_bf = round_wb(1, nc.scalar.copy, "x_pair2")
+        turn_back(2, LOW[0])
+        turn_back(3, LOW[3])
 
-        for e in range(3):
-            pick(4 + e, HALF, HALF, rear[:, e, :])
-            pick(4 + e, 0, HALF, front[:, e, :])
-        round_turned(2, 3)
-        copy_back(0, 1)
-        bf = round_wb(1, [(A, 0, N)], "xa2")
-        turn_back(0, 2, lo[0])
-        turn_back(0, 3, lo[3])
-        gap_codes(0, 0)
+        quantise_z(0, 0)
         for i in range(2):
-            pick(7, i * CHUNK, CHUNK, front[:, 3, i * CHUNK : (i + 1) * CHUNK])
-        first = ring.tile([P, PACK, CHUNK], F32, name="gap_first", tag="xa0", bufs=1, align_bytes=64)
-        nc.vector.tensor_tensor(first[:], front[:, :, 0:CHUNK], gap[1][:, :, 0:CHUNK], ALU.add)
-        gap_codes(0, 1)
-        add_own(front[:, :, CHUNK:HALF], 0, PACK, CHUNK, CHUNK)
-        second = [lo[1], lo[2], lo[0], lo[3]]
-        products(0, 0, hi)
-        products(0, 1, second, [0, 1])
-        round_gap(1, 0, "z1_0", first[:])
-        round_gap(1, 1, "z1_1")
-        copy_back(0, 2)
-        copy_back(0, 3)
-        wb_q.append(quantise(bf[:], BANK, "wbq1"))
-        gap_codes(1, 0)
-        products(1, 0, hi)
-        products(0, 1, second, [2, 3])
-        third = ring.tile([P, PACK, CHUNK], F32, name="gap_third", tag="xa0", bufs=1, align_bytes=64)
-        pick(7, HALF, CHUNK, third[:, 3, :])
-        nc.vector.tensor_tensor(third[:, 0:3, :], rear[:, :, 0:CHUNK], gap[1][:, 0:3, HALF : HALF + CHUNK], ALU.add)
-        nc.vector.tensor_tensor(third[:, 3, :], third[:, 3, :], gap[1][:, 3, HALF : HALF + CHUNK], ALU.add)
-        gap_codes(1, 1)
-        gap_codes(0, 2)
-        fourth = add_rear(3, "z0_2")
-        products(1, 1, second)
+            m, w = PARTS[i]
+            pick(LAST, m, w, x1[:, early, m : m + w])
+        gap0 = buffer([PACK, CHUNK], F32, "gap0", "x_pair0")
+        add_own(nc.vector, gap0[:], x1_part(0, PACK), 0, PACK, 0)
+        quantise_z(0, 1)
+        gap1 = own_sb[1][:, :, CHUNK : 2 * CHUNK]
+        add_own(nc.vector, gap1, x1_part(1, PACK), 0, PACK, 1)
+        low_as_freed = [LOW[1], LOW[2], LOW[0], LOW[3]]
+        products(0, 0, HIGH)
+        products(0, 1, low_as_freed, [0, 1])
+        round_gap(0, gap0[:])
+        round_gap(1, gap1)
+        copy_back(2)
+        copy_back(3)
+        wb_q[1] = quantise(wb_bf[:], N, "wbq1")
+        quantise_z(1, 0)
+        products(1, 0, HIGH)
+        products(0, 1, low_as_freed, [2, 3])
+
+        gap2 = buffer([PACK, CHUNK], F32, "gap2", "x_pair0")
+        pick(LAST, *PARTS[2], gap2[:, early, :])
+        add_own(nc.vector, gap2[:, 0:early, :], x1_part(2, early), 0, early, 2)
+        add_own(nc.vector, gap2[:, early:PACK, :], gap2[:, early:PACK, :], early, PACK, 2)
+        quantise_z(1, 1)
+        quantise_z(0, 2)
+        gap3 = add_early_on_gpsimd(3, "z0_2")
+        products(1, 1, low_as_freed)
         read_b(0)
-        round_gap(1, 2, "z1_2", third[:])
+        round_gap(2, gap2[:])
+
         finish(0)
-        products(0, 2, hi)
-        x = pick_last(3, "b_sb0_2")
-        gap_codes(0, 3, "b_sb0_3")
-        add_last(3, x, fourth)
-        gap_codes(1, 2)
-        fifth = add_rear(4, "z1_2")
-        products(1, 2, hi)
+        products(0, 2, HIGH)
+        x_last = pick_last(3, b_tag(0, 2))
+        quantise_z(0, 3, b_tag(0, 3))
+        add_own(nc.vector, gap3[:, early:PACK, :], x_last[:], early, PACK, 3)
+        quantise_z(1, 2)
+        gap4 = add_early_on_gpsimd(4, "z1_2")
+        products(1, 2, HIGH)
         read_b(1)
         finish(1)
-        x = pick_last(4, "b_sb1_2")
-        round_gap(1, 3, "z1_3", fourth[:])
-        gap_codes(1, 3)
-        add_last(4, x, fifth)
-        products(0, 3, [lo[1], lo[2]])
-        products(1, 3, [lo[1], lo[2]])
-        last = [lo[0], lo[3], hi[0], hi[1]]
-        products(0, 4, last, [0, 1])
+        x_last = pick_last(4, b_tag(1, 2))
+        round_gap(3, gap3[:])
+        quantise_z(1, 3)
+        add_own(nc.vector, gap4[:, early:PACK, :], x_last[:], early, PACK, 4)
+        for g in range(PASSES):
+            products(g, 3, low_as_freed[0:2])
+        last_banks = low_as_freed[2:4] + HIGH[0:2]
+        products(0, 4, last_banks, [0, 1])
         read_b(2, [0, 1])
-        round_gap(1, 4, "z1_4", fifth[:])
+        round_gap(4, gap4[:])
         read_b(2, [2, 3])
         finish(2, [0, 1])
-        gap_codes(1, 4)
-        products(1, 4, last, [0, 1])
+        quantise_z(1, 4)
+        products(1, 4, last_banks, [0, 1])
         for j in (2, 3):
-            products(0, 4, last, [j])
-            products(1, 4, last, [j])
+            for g in range(PASSES):
+                products(g, 4, last_banks, [j])
         finish(2, [2, 3])
-        read_b(3)
-        finish(3)
-        read_b(4)
-        finish(4)
+        for i in (3, 4):
+            read_b(i)
+            finish(i)

@@ -27,6 +27,7 @@ PASSES = H // K_PASS
 N_TILES = N // P
 H_PIECES = S // BANK
 H_BUFS = 7
+ROWS_AT = P - K // 32
 LAST = 2 * PACK - 1
 WORDS_AHEAD = 3
 CHUNK = BANK // 2
@@ -58,13 +59,8 @@ def tile_list_clone_audit_kernel(
         nc.sync.dma_start(idx[:], offs)
 
         tab_rows = ring.tile([P, T], U8, name="tab_rows", tag="inputs", bufs=1)
-        nc.vector.memset(tab_rows[:].bitcast(I32), 0)
-        idx2 = keep.tile([P, M // GROUP], U16, name="idx2")
-        nc.sync.dma_start(idx2[:], offs2)
-        ba_sb = keep.tile([P, N_TILES], F32, name="ba_sb")
-        with nc.allow_non_contiguous_dma(reason="one bias value a partition"):
-            nc.sync.dma_start(ba_sb[:], ba.rearrange("(j p) -> p j", p=P))
-        nc.sync.dma_start(tab_rows[0:P:8, :].bitcast(I32), tab_scales[0].bitcast(I32))
+        nc.sync.dma_start(tab_rows[ROWS_AT:P, :].bitcast(I32), tab_scales[0].bitcast(I32))
+        nc.vector.memset(tab_rows[0:ROWS_AT, :].bitcast(I32), 0)
         v_plane = keep.tile([P, S], U8, name="v_plane", align_bytes=64)
         nc.vector.memset(v_plane[:].bitcast(I32), 0)
         ident = keep.tile([P, P], F32, name="ident")
@@ -75,11 +71,13 @@ def tile_list_clone_audit_kernel(
         nc.sync.dma_start(tab_w[:], tab_words[0].rearrange("p t i -> p (t i)").bitcast(I32))
         w1_first = buffer([PACK, K_PASS], F32, "w1_first", "w1_raw0")
         nc.sync.dma_start(w1_first[:], by_word(w1[:, 0:K_PASS]))
+        idx2 = keep.tile([P, M // GROUP], U16, name="idx2")
+        nc.sync.dma_start(idx2[:], offs2)
 
         picked = buffer([S], U8, "picked", "wb_bf")
         nc.vector.tensor_copy(picked[:], tab_rows[:].indirect(idx[:]))
         for r in range(4):
-            nc.sync.dma_start(v_plane[r:P:32, :].bitcast(I32), picked[8 * r : P : 32, :].bitcast(I32))
+            nc.sync.dma_start(v_plane[r:P:32, :].bitcast(I32), picked[ROWS_AT + r : P : 4, :].bitcast(I32))
 
         wb_at = PASSES * PACK * M
         w1_at = wb_at + PASSES * PACK * N
@@ -105,7 +103,7 @@ def tile_list_clone_audit_kernel(
         def load_wa_and_bb():
             words = buffer([PASSES, 2 * N], U8, "wa_w", "w1q0_codes")
             plane = buffer([PASSES, N], U8, "wa_plane", "w1q2_plane")
-            bias = buffer([N_TILES], F32, "bb_sb", "w1q0_plane")
+            biases = buffer([2, 2 * N_TILES], F32, "biases", "w1q0_plane")
             nc.sync.dma_start(words[:].bitcast(I32), wa_words.rearrange("g p c -> p g c").bitcast(I32))
             nc.gpsimd.memset(plane[:].bitcast(I32), 0)
             for q in range(4):
@@ -114,8 +112,9 @@ def tile_list_clone_audit_kernel(
                     wa_scales[:, 4 * q : 4 * q + 4, :].rearrange("g r c -> r g c").bitcast(I32),
                 )
             with nc.allow_non_contiguous_dma(reason="one bias value a partition"):
-                nc.sync.dma_start(bias[:], bb.rearrange("(j p) -> p j", p=P))
-            return words, plane, bias
+                nc.sync.dma_start(biases[:, 0, 0:N_TILES], ba.rearrange("(j p) -> p j", p=P))
+                nc.sync.dma_start(biases[:, 1, 0:N_TILES], bb.rearrange("(j p) -> p j", p=P))
+            return words, plane, biases[:, 0, :], biases[:, 1, :]
 
         def quantise(rounded, width, name, codes_tag=None):
             codes = buffer([width], U32, name + "_codes", codes_tag or name + "_codes")
@@ -264,16 +263,15 @@ def tile_list_clone_audit_kernel(
                     start=opens,
                     stop=False,
                 )
-                for c in range(0, w, P):
-                    nc.tensor.matmul_mx(
-                        out=sums_ab[(i, j)][:, 0, c : c + P],
-                        lhsT=wa_w[:, g, 2 * j * P : 2 * (j + 1) * P].bitcast(FP4X4),
-                        lhsT_scale=wa_plane[:, g, j * P : (j + 1) * P],
-                        rhs=codes[:, z0 + c : z0 + c + P].bitcast(FP8X4),
-                        rhs_scale=plane[:, z0 + c : z0 + c + P],
-                        start=False,
-                        stop=(g == PASSES - 1 and c + P == w and j % per_bank == per_bank - 1),
-                    )
+                nc.tensor.matmul_mx(
+                    out=sums_ab[(i, j)][:, 0, :],
+                    lhsT=wa_w[:, g, 2 * j * P : 2 * (j + 1) * P].bitcast(FP4X4),
+                    lhsT_scale=wa_plane[:, g, j * P : (j + 1) * P],
+                    rhs=codes[:, z0 : z0 + w].bitcast(FP8X4),
+                    rhs_scale=plane[:, z0 : z0 + w],
+                    start=False,
+                    stop=(g == PASSES - 1 and j % per_bank == per_bank - 1),
+                )
 
         def b_tag(i, j):
             if i > 0 and i % 2 == 0 and j == N_TILES - 1:
@@ -334,7 +332,7 @@ def tile_list_clone_audit_kernel(
             h_slice(s)
         pick_pair(0)
         h_slice(3)
-        wa_w, wa_plane, bb_sb = load_wa_and_bb()
+        wa_w, wa_plane, ba_sb, bb_sb = load_wa_and_bb()
         h_slice(4)
         wb_bf = round_wb(0, nc.vector.tensor_copy, "wb_bf")
         pick_pair(1)

@@ -33,6 +33,7 @@ WORDS_AHEAD = 3
 CHUNK = BANK // 2
 CHUNKS = [(m, CHUNK) for m in range(0, M, CHUNK)]
 PARTS = CHUNKS[:-1] + [(M - 2 * P, P), (M - P, P)]
+WB_ON_VECTOR = N // 4
 LOW, HIGH = [0, 1, 2, 3], [4, 5, 6, 7]
 STAGE_TAGS = ["w1_raw0", "x_pair2", "stage2", "words0", "wb_bf"]
 
@@ -96,9 +97,9 @@ def tile_list_clone_audit_kernel(
         own_v = own.rearrange("(g p t) m -> g p t m", p=P, t=PACK)
         for u in range(2):
             nc.sync.dma_start(own_sb[0][:, 2 * u : 2 * u + 2, :], own_v[0, :, 2 * u : 2 * u + 2, :])
-            nc.sync.dma_start(wb_raw[u], by_word(wb[u * K_PASS : (u + 1) * K_PASS, :]))
         for u in range(2):
             nc.sync.dma_start(own_sb[1][:, 2 * u : 2 * u + 2, :], own_v[1, :, 2 * u : 2 * u + 2, :])
+            nc.sync.dma_start(wb_raw[u], by_word(wb[u * K_PASS : (u + 1) * K_PASS, :]))
 
         def load_wa_and_bb():
             words = buffer([PASSES, 2 * N], U8, "wa_w", "w1q0_codes")
@@ -142,13 +143,11 @@ def tile_list_clone_audit_kernel(
             for e in range(2):
                 w1_q[s + e] = (codes[:, e * P : (e + 1) * P], plane[:, e * P : (e + 1) * P])
 
-        def round_wb(g, copy, tag):
-            rounded = buffer([PACK * N], BF16, "wb_bf%d" % g, tag)
+        def round_wb(g, copy, rounded, n0, n1):
             copy(
-                rounded[:].rearrange("p (c d t) -> p c t d", d=RUN, t=PACK),
-                wb_raw[g].rearrange("p t (c d) -> p c t d", d=RUN),
+                rounded[:, PACK * n0 : PACK * n1].rearrange("p (c d t) -> p c t d", d=RUN, t=PACK),
+                wb_raw[g][:, :, n0:n1].rearrange("p t (c d) -> p c t d", d=RUN),
             )
-            return rounded
 
         v_words = {}
 
@@ -334,8 +333,9 @@ def tile_list_clone_audit_kernel(
         h_slice(3)
         wa_w, wa_plane, ba_sb, bb_sb = load_wa_and_bb()
         h_slice(4)
-        wb_bf = round_wb(0, nc.vector.tensor_copy, "wb_bf")
         pick_pair(1)
+        wb_bf = buffer([PACK * N], BF16, "wb_bf0", "wb_bf")
+        round_wb(0, nc.vector.tensor_copy, wb_bf, 0, N)
         wb_q[0] = quantise(wb_bf[:], N, "wbq0")
         h_slice(5)
         h_slice(6)
@@ -367,11 +367,15 @@ def tile_list_clone_audit_kernel(
             add_own(nc.gpsimd, gap[:, 0:early, :], x1_part(i, early), 0, early, i)
             return gap
 
+        wb_bf = buffer([PACK * N], BF16, "wb_bf1", "wb_bf1")
+        round_wb(1, nc.vector.tensor_copy, wb_bf, 0, WB_ON_VECTOR)
         for t in range(early):
             pick(PACK + t, 0, M, x1[:, t, :])
+        gap0 = buffer([PACK, CHUNK], F32, "gap0", "x_pair0")
+        add_own(nc.vector, gap0[:, 0:early, :], x1_part(0, early), 0, early, 0)
         round_turned(*last_sum)
         copy_back(1)
-        wb_bf = round_wb(1, nc.scalar.copy, "x_pair2")
+        round_wb(1, nc.scalar.copy, wb_bf, WB_ON_VECTOR, N)
         turn_back(2, LOW[0])
         turn_back(3, LOW[3])
 
@@ -379,8 +383,7 @@ def tile_list_clone_audit_kernel(
         for i in range(2):
             m, w = PARTS[i]
             pick(LAST, m, w, x1[:, early, m : m + w])
-        gap0 = buffer([PACK, CHUNK], F32, "gap0", "x_pair0")
-        add_own(nc.vector, gap0[:], x1_part(0, PACK), 0, PACK, 0)
+        add_own(nc.vector, gap0[:, early:PACK, :], x1[:, early:PACK, 0:CHUNK], early, PACK, 0)
         quantise_z(0, 1)
         gap1 = own_sb[1][:, :, CHUNK : 2 * CHUNK]
         add_own(nc.vector, gap1, x1_part(1, PACK), 0, PACK, 1)

from contextlib import ExitStack

import concourse.mybir as mybir
from concourse.masks import make_identity

K, T, S, M, H, N = 512, 4096, 2048, 1024, 1024, 512
FLOPS = 2 * K * H * S + 2 * 2 * H * N * M

F32 = mybir.dt.float32
BF16 = mybir.dt.bfloat16
I32 = mybir.dt.int32
U32 = mybir.dt.uint32
U16 = mybir.dt.uint16
U8 = mybir.dt.uint8
FP8X4 = mybir.dt.float8_e4m3fn_x4
FP4X4 = mybir.dt.float4_e2m1fn_x4
ALU = mybir.AluOpType
ACT = mybir.ActivationFunctionType

P = 128
PACK = 4
RUN = 4
GROUP = 16
BANK = 512
K_PASS = P * PACK
PASSES = H // K_PASS
N_TILES = N // P
H_PIECES = S // BANK
H_BUFS = 7
ROWS_AT = P - K // 32
LAST = 2 * PACK - 1
WORDS_AHEAD = 3
CHUNK = BANK // 2
CHUNKS = [(m, CHUNK) for m in range(0, M, CHUNK)]
PARTS = CHUNKS[:-1] + [(M - 2 * P, P), (M - P, P)]
WB_ON_VECTOR = N // 4
LOW, HIGH = [0, 1, 2, 3], [4, 5, 6, 7]
STAGE_TAGS = ["w1_raw0", "x_pair2", "stage2", "words0", "wb_bf"]


def tile_list_clone_audit_kernel(
    tc, tab_words, tab_scales, offs, w1, offs2, wgt, own, wa_words, wa_scales, ba, wb, bb, out
):
    nc = tc.nc
    with ExitStack() as ctx:
        keep = ctx.enter_context(tc.tile_pool(name="keep", bufs=1))
        ring = ctx.enter_context(tc.tile_pool(name="ring", bufs=2))
        psum = ctx.enter_context(tc.psum_pool(name="psum", bufs=1))

        def bank(n, shape, name):
            return psum.tile([P] + shape, F32, name=name, tag="bank%d" % n, bufs=1)

        def buffer(shape, dtype, name, tag):
            return ring.tile([P] + shape, dtype, name=name, tag=tag, bufs=1, align_bytes=64)

        def by_word(rows):
            return rows.rearrange("(p t) c -> p t c", t=PACK)

        idx = keep.tile([P, S // GROUP], U16, name="idx")
        nc.sync.dma_start(idx[:], offs)

        tab_rows = ring.tile([P, T], U8, name="tab_rows", tag="inputs", bufs=1)
        nc.sync.dma_start(tab_rows[ROWS_AT:P, :].bitcast(I32), tab_scales[0].bitcast(I32))
        nc.vector.memset(tab_rows[0:ROWS_AT, :].bitcast(I32), 0)
        v_plane = keep.tile([P, S], U8, name="v_plane", align_bytes=64)
        nc.vector.memset(v_plane[:].bitcast(I32), 0)
        ident = keep.tile([P, P], F32, name="ident")
        nc.vector.memset(ident[:], 0.0)
        make_identity(nc, ident[:], nomemset=True)

        tab_w = buffer([T], I32, "tab_w", "table")
        nc.sync.dma_start(tab_w[:], tab_words[0].rearrange("p t i -> p (t i)").bitcast(I32))
        w1_first = buffer([PACK, K_PASS], F32, "w1_first", "w1_raw0")
        nc.sync.dma_start(w1_first[:], by_word(w1[:, 0:K_PASS]))
        idx2 = keep.tile([P, M // GROUP], U16, name="idx2")
        nc.sync.dma_start(idx2[:], offs2)

        picked = buffer([S], U8, "picked", "wb_bf")
        nc.vector.tensor_copy(picked[:], tab_rows[:].indirect(idx[:]))
        for r in range(4):
            nc.sync.dma_start(v_plane[r:P:32, :].bitcast(I32), picked[ROWS_AT + r : P : 4, :].bitcast(I32))

        wb_at = PASSES * PACK * M
        w1_at = wb_at + PASSES * PACK * N
        wgt_at = w1_at + PACK * K_PASS
        inputs = ring.tile([P, wgt_at + M], F32, name="inputs", tag="inputs", bufs=1)

        def region(first, width):
            return inputs[:, first : first + PACK * width].rearrange("p (t c) -> p t c", t=PACK)

        w1_raw = [w1_first[:], region(w1_at, K_PASS)]
        nc.sync.dma_start(w1_raw[1], by_word(w1[:, K_PASS : 2 * K_PASS]))
        wgt_sb = inputs[:, wgt_at : wgt_at + M]
        nc.sync.dma_start(wgt_sb, wgt)
        own_sb = [region(g * PACK * M, M) for g in range(PASSES)]
        wb_raw = [region(wb_at + g * PACK * N, N) for g in range(PASSES)]
        own_v = own.rearrange("(g p t) m -> g p t m", p=P, t=PACK)
        for u in range(2):
            nc.sync.dma_start(own_sb[0][:, 2 * u : 2 * u + 2, :], own_v[0, :, 2 * u : 2 * u + 2, :])
        for u in range(2):
            nc.sync.dma_start(own_sb[1][:, 2 * u : 2 * u + 2, :], own_v[1, :, 2 * u : 2 * u + 2, :])
            nc.sync.dma_start(wb_raw[u], by_word(wb[u * K_PASS : (u + 1) * K_PASS, :]))

        def load_wa_and_bb():
            words = buffer([PASSES, 2 * N], U8, "wa_w", "w1q0_codes")
            plane = buffer([PASSES, N], U8, "wa_plane", "w1q2_plane")
            biases = buffer([2, 2 * N_TILES], F32, "biases", "w1q0_plane")
            nc.sync.dma_start(words[:].bitcast(I32), wa_words.rearrange("g p c -> p g c").bitcast(I32))
            nc.gpsimd.memset(plane[:].bitcast(I32), 0)
            for q in range(4):
                nc.sync.dma_start(
                    plane[32 * q : 32 * q + 4, :, :].bitcast(I32),
                    wa_scales[:, 4 * q : 4 * q + 4, :].rearrange("g r c -> r g c").bitcast(I32),
                )
            with nc.allow_non_contiguous_dma(reason="one bias value a partition"):
                nc.sync.dma_start(biases[:, 0, 0:N_TILES], ba.rearrange("(j p) -> p j", p=P))
                nc.sync.dma_start(biases[:, 1, 0:N_TILES], bb.rearrange("(j p) -> p j", p=P))
            return words, plane, biases[:, 0, :], biases[:, 1, :]

        def quantise(rounded, width, name, codes_tag=None):
            codes = buffer([width], U32, name + "_codes", codes_tag or name + "_codes")
            plane = buffer([width], U8, name + "_plane", name + "_plane")
            nc.vector.quantize_mx(out=codes[:].bitcast(FP8X4), scales=plane[:], in_=rounded)
            return codes, plane

        def negate_on_scalar(dst, src):
            nc.scalar.activation(dst, src, ACT.Copy, scale=-1.0)

        def negate_on_vector(dst, src):
            nc.vector.tensor_scalar(dst, src, -1.0, None, ALU.mult)

        def round_w1(s, negate, rounded):
            g, t = divmod(s, PACK)
            negate(
                rounded.rearrange("p (e c a) -> p c a e", e=2, a=PACK),
                w1_raw[g].rearrange("p a (c t) -> p c a t", t=PACK)[:, :, :, t : t + 2],
            )

        w1_q = {}

        def quantise_w1(s, rounded):
            codes, plane = quantise(rounded, 2 * P, "w1q%d" % s)
            for e in range(2):
                w1_q[s + e] = (codes[:, e * P : (e + 1) * P], plane[:, e * P : (e + 1) * P])

        def round_wb(g, copy, rounded, n0, n1):
            copy(
                rounded[:, PACK * n0 : PACK * n1].rearrange("p (c d t) -> p c t d", d=RUN, t=PACK),
                wb_raw[g][:, :, n0:n1].rearrange("p t (c d) -> p c t d", d=RUN),
            )

        v_words = {}

        def gather_words(first, count, tag):
            words = buffer([count * BANK], U32, "v_words%d" % first, tag)
            entries = idx[:, first * BANK // GROUP : (first + count) * BANK // GROUP]
            nc.vector.tensor_copy(words[:], tab_w[:].bitcast(U32).indirect(entries))
            for c in range(count):
                v_words[first + c] = words[:, c * BANK : (c + 1) * BANK]

        h = {}

        def h_piece(s, c, n):
            if s not in h:
                h[s] = ring.tile([P, S], F32, name="h%d" % s, tag="h", bufs=H_BUFS)
            acc = bank(n, [BANK], "h_acc")
            nc.tensor.matmul_mx(
                out=acc[:],
                lhsT=w1_q[s][0].bitcast(FP8X4),
                lhsT_scale=w1_q[s][1],
                rhs=v_words[c].bitcast(FP8X4),
                rhs_scale=v_plane[:, c * BANK : (c + 1) * BANK],
                start=True,
                stop=True,
            )
            nc.scalar.copy(h[s][:, c * BANK : (c + 1) * BANK], acc[:])

        def pick(s, m, width, dst):
            entries = idx2[:, m // GROUP : (m + width) // GROUP]
            nc.vector.tensor_tensor(dst, h[s][:].indirect(entries), wgt_sb[:, m : m + width], ALU.mult)

        x_pair, turned_sum, turned_z, returned = {}, {}, {}, {}
        z_bf, z_q = {}, {}

        def pick_pair(u):
            x_pair[u] = buffer([2, M], F32, "x_pair%d" % u, "x_pair%d" % (2 * u))
            for e in range(2):
                pick(2 * u + e, 0, M, x_pair[u][:, e, :])

        def add_turned(u, i, n):
            acc = bank(n, [2, 2, P], "sum%d_%d" % (u, i))
            turned_sum[(u, i)] = acc
            places = [(f, e, i * CHUNK + f * P) for f in range(2) for e in range(2)]
            for no, (f, e, m) in enumerate(places):
                nc.tensor.matmul(
                    acc[:, f, e, :], own_sb[0][:, 2 * u + e, m : m + P], ident[:],
                    start=(no == 0), stop=False, is_transpose=True,
                )
            for no, (f, e, m) in enumerate(places):
                nc.tensor.matmul(
                    acc[:, f, e, :], x_pair[u][:, e, m : m + P], ident[:],
                    start=False, stop=(no == len(places) - 1), is_transpose=True,
                )

        def round_turned(u, i):
            if i not in turned_z:
                turned_z[i] = buffer([2, 2, 2 * P], BF16, "zt%d" % i, "zt%d" % i)
            nc.scalar.activation(
                turned_z[i][:, :, u, :].rearrange("m f (p e) -> m f p e", e=2),
                turned_sum[(u, i)][:].rearrange("m f e p -> m f p e"),
                ACT.Abs,
            )

        def turn_back(i, n):
            returned[i] = bank(n, [2, 2, P], "back%d" % i)
            for f in range(2):
                for u in range(2):
                    nc.tensor.transpose(returned[i][:, f, u, :], turned_z[i][:, f, u, :].bitcast(F32), ident[:])

        def copy_back(i):
            z_bf[(0, i)] = buffer([PACK * CHUNK], BF16, "z_bf0_%d" % i, "z0_%d" % i)
            nc.scalar.copy(
                z_bf[(0, i)][:].bitcast(F32).rearrange("p (f m u) -> p f m u", f=2, u=2),
                returned[i][:].rearrange("p f u m -> p f m u"),
            )

        def add_own(engine, dst, x, t0, t1, i):
            m, w = PARTS[i]
            engine.tensor_tensor(dst, x, own_sb[1][:, t0:t1, m : m + w], ALU.add)

        def round_gap(i, gap):
            z_bf[(1, i)] = buffer([PACK * PARTS[i][1]], BF16, "z_bf1_%d" % i, "z1_%d" % i)
            nc.scalar.activation(
                z_bf[(1, i)][:].rearrange("p (c d t) -> p c t d", d=RUN, t=PACK),
                gap.rearrange("p t (c d) -> p c t d", d=RUN),
                ACT.Abs,
            )

        def quantise_z(g, i, codes_tag=None):
            z_q[(g, i)] = quantise(z_bf[(g, i)][:], (PARTS if g else CHUNKS)[i][1], "zq%d_%d" % (g, i), codes_tag)

        wb_q, sums_ab, b_sb, staged = {}, {}, {}, {}
        out_v = out.rearrange("(j p) m -> p j m", p=P)

        def products(g, i, banks, tiles=range(N_TILES)):
            m, w = PARTS[i]
            codes, plane = z_q[(g, i if g else m // CHUNK)]
            z0 = 0 if g else m % CHUNK
            per_bank = N_TILES // len(banks)
            for j in tiles:
                opens = g == 0 and j % per_bank == 0
                if opens:
                    acc = bank(banks[j // per_bank], [per_bank, 2, w], "acc%d_%d" % (i, j))
                    for jj in range(per_bank):
                        sums_ab[(i, j + jj)] = acc[:, jj, :, :]
                nc.tensor.matmul_mx(
                    out=sums_ab[(i, j)][:, 1, :],
                    lhsT=wb_q[g][0][:, j * P : (j + 1) * P].bitcast(FP8X4),
                    lhsT_scale=wb_q[g][1][:, j * P : (j + 1) * P],
                    rhs=codes[:, z0 : z0 + w].bitcast(FP8X4),
                    rhs_scale=plane[:, z0 : z0 + w],
                    start=opens,
                    stop=False,
                )
                nc.tensor.matmul_mx(
                    out=sums_ab[(i, j)][:, 0, :],
                    lhsT=wa_w[:, g, 2 * j * P : 2 * (j + 1) * P].bitcast(FP4X4),
                    lhsT_scale=wa_plane[:, g, j * P : (j + 1) * P],
                    rhs=codes[:, z0 : z0 + w].bitcast(FP8X4),
                    rhs_scale=plane[:, z0 : z0 + w],
                    start=False,
                    stop=(g == PASSES - 1 and j % per_bank == per_bank - 1),
                )

        def b_tag(i, j):
            if i > 0 and i % 2 == 0 and j == N_TILES - 1:
                return "z0_%d" % (i // 2 - 1)
            return "b%d_%d" % (i % 2, j)

        def read_b(i, tiles=range(N_TILES)):
            for j in tiles:
                b_sb[(i, j)] = buffer([PARTS[i][1]], F32, "b_sb%d_%d" % (i, j), b_tag(i, j))
                nc.scalar.activation(b_sb[(i, j)][:], sums_ab[(i, j)][:, 1, :], ACT.Identity, bias=bb_sb[:, j : j + 1])

        def finish(i, tiles=range(N_TILES)):
            m, w = PARTS[i]
            for j in tiles:
                if j == 0:
                    staged[i] = buffer([N_TILES, w], F32, "staged%d" % i, STAGE_TAGS[i])
                nc.vector.scalar_tensor_tensor(
                    staged[i][:, j, :], sums_ab[(i, j)][:, 0, :], ba_sb[:, j : j + 1], b_sb[(i, j)][:], ALU.add, ALU.mult
                )
                stored = 1 if i == len(PARTS) - 1 and j >= 2 else 2
                if j % stored == stored - 1:
                    nc.sync.dma_start(out_v[:, j + 1 - stored : j + 1, m : m + w], staged[i][:, j + 1 - stored : j + 1, :])

        gather_words(0, WORDS_AHEAD, "words0")
        w1_bf0 = buffer([1, 2 * K_PASS], BF16, "w1_bf0", "words1")
        w1_bf2 = buffer([1, 2 * K_PASS], BF16, "w1_bf2", "w1_bf2")
        round_w1(0, negate_on_scalar, w1_bf0[:, 0, :])
        round_w1(2, negate_on_scalar, w1_bf2[:, 0, :])
        quantise_w1(0, w1_bf0[:, 0, :])
        gather_words(WORDS_AHEAD, H_PIECES - WORDS_AHEAD, "words1")
        quantise_w1(2, w1_bf2[:, 0, :])
        w1_bf4 = buffer([2, 2 * K_PASS], BF16, "w1_bf4", "w1_raw0")
        for e in range(2):
            round_w1(PACK + 2 * e, negate_on_vector, w1_bf4[:, e, :])
        for e in range(2):
            quantise_w1(PACK + 2 * e, w1_bf4[:, e, :])

        banks_taken = []

        def next_bank():
            banks_taken.append(None)
            return len(banks_taken) % len(LOW + HIGH)

        sums_left = [(u, i) for u in range(2) for i in range(len(CHUNKS))]

        def next_sum(n):
            u, i = sums_left.pop(0)
            add_turned(u, i, n)
            round_turned(u, i)

        def h_slice(s):
            for c in range(H_PIECES):
                h_piece(s, c, next_bank())
                if s >= PACK and c % 2 == 1:
                    next_sum(next_bank())

        for s in range(3):
            h_slice(s)
        pick_pair(0)
        h_slice(3)
        wa_w, wa_plane, ba_sb, bb_sb = load_wa_and_bb()
        h_slice(4)
        pick_pair(1)
        wb_bf = buffer([PACK * N], BF16, "wb_bf0", "wb_bf")
        round_wb(0, nc.vector.tensor_copy, wb_bf, 0, N)
        wb_q[0] = quantise(wb_bf[:], N, "wbq0")
        h_slice(5)
        h_slice(6)
        for c in range(H_PIECES):
            h_piece(LAST, c, HIGH[c])
            if c == 1:
                next_sum(LOW[0])
            if c == H_PIECES - 2:
                turn_back(0, LOW[1])
                copy_back(0)
        turn_back(1, LOW[2])
        last_sum = sums_left.pop(0)
        add_turned(*last_sum, LOW[3])

        x1 = buffer([PACK, M], F32, "x1", "table")
        early = PACK - 1

        def x1_part(i, t1):
            m, w = PARTS[i]
            return x1[:, 0:t1, m : m + w]

        def pick_last(i, tag):
            x = buffer([1, PARTS[i][1]], F32, "x_last%d" % i, tag)
            pick(LAST, *PARTS[i], x[:, 0, :])
            return x

        def add_early_on_gpsimd(i, tag):
            gap = buffer([PACK, PARTS[i][1]], F32, "gap%d" % i, tag)
            add_own(nc.gpsimd, gap[:, 0:early, :], x1_part(i, early), 0, early, i)
            return gap

        wb_bf = buffer([PACK * N], BF16, "wb_bf1", "wb_bf1")
        round_wb(1, nc.vector.tensor_copy, wb_bf, 0, WB_ON_VECTOR)
        for t in range(early):
            pick(PACK + t, 0, M, x1[:, t, :])
        gap0 = buffer([PACK, CHUNK], F32, "gap0", "x_pair0")
        add_own(nc.vector, gap0[:, 0:early, :], x1_part(0, early), 0, early, 0)
        round_turned(*last_sum)
        copy_back(1)
        round_wb(1, nc.scalar.copy, wb_bf, WB_ON_VECTOR, N)
        turn_back(2, LOW[0])
        turn_back(3, LOW[3])

        quantise_z(0, 0)
        for i in range(2):
            m, w = PARTS[i]
            pick(LAST, m, w, x1[:, early, m : m + w])
        add_own(nc.vector, gap0[:, early:PACK, :], x1[:, early:PACK, 0:CHUNK], early, PACK, 0)
        quantise_z(0, 1)
        gap1 = own_sb[1][:, :, CHUNK : 2 * CHUNK]
        add_own(nc.vector, gap1, x1_part(1, PACK), 0, PACK, 1)
        low_as_freed = [LOW[1], LOW[2], LOW[0], LOW[3]]
        products(0, 0, HIGH)
        products(0, 1, low_as_freed, [0, 1])
        round_gap(0, gap0[:])
        round_gap(1, gap1)
        copy_back(2)
        copy_back(3)
        wb_q[1] = quantise(wb_bf[:], N, "wbq1")
        quantise_z(1, 0)
        products(1, 0, HIGH)
        products(0, 1, low_as_freed, [2, 3])

        gap2 = buffer([PACK, CHUNK], F32, "gap2", "x_pair0")
        pick(LAST, *PARTS[2], gap2[:, early, :])
        add_own(nc.vector, gap2[:, 0:early, :], x1_part(2, early), 0, early, 2)
        add_own(nc.vector, gap2[:, early:PACK, :], gap2[:, early:PACK, :], early, PACK, 2)
        quantise_z(1, 1)
        quantise_z(0, 2)
        gap3 = add_early_on_gpsimd(3, "z0_2")
        products(1, 1, low_as_freed)
        read_b(0)
        round_gap(2, gap2[:])

        finish(0)
        products(0, 2, HIGH)
        x_last = pick_last(3, b_tag(0, 2))
        quantise_z(0, 3, b_tag(0, 3))
        add_own(nc.vector, gap3[:, early:PACK, :], x_last[:], early, PACK, 3)
        quantise_z(1, 2)
        gap4 = add_early_on_gpsimd(4, "z1_2")
        products(1, 2, HIGH)
        read_b(1)
        finish(1)
        x_last = pick_last(4, b_tag(1, 2))
        round_gap(3, gap3[:])
        quantise_z(1, 3)
        add_own(nc.vector, gap4[:, early:PACK, :], x_last[:], early, PACK, 4)
        for g in range(PASSES):
            products(g, 3, low_as_freed[0:2])
        last_banks = low_as_freed[2:4] + HIGH[0:2]
        products(0, 4, last_banks, [0, 1])
        read_b(2, [0, 1])
        round_gap(4, gap4[:])
        read_b(2, [2, 3])
        finish(2, [0, 1])
        quantise_z(1, 4)
        products(1, 4, last_banks, [0, 1])
        for j in (2, 3):
            for g in range(PASSES):
                products(g, 4, last_banks, [j])
        finish(2, [2, 3])
        for i in (3, 4):
            read_b(i)
            finish(i)
